import numpy as np, ml_dtypes
CORES = [16,18,20,22]
N = 4
BF = ml_dtypes.bfloat16
Q, B, H, L, CAP, TR, ST, LN = 4096, 4096, 1024, 256, 64, 4, 3, 2
def code(rng, r):
    m = rng.integers(0, 2, (r, 16)); m[0] = 1
    return (((np.arange(2 ** r)[:, None] >> np.arange(r)) & 1) @ m) & 1
def lay(rng, cb, n, noise, wild):
    v = 63 * cb[rng.integers(0, len(cb), n)].T
    v = np.abs(v - rng.integers(1, 4, (16, n)) * (rng.random((16, n)) < noise))
    return np.where(rng.random((1, n)) < wild, rng.integers(0, 64, (16, n)), v)
def coefs(rng):
    co = rng.integers(1, 256, (N, 8, 16, 3)); co[..., 2] = co[0, ..., 2].copy()
    return co
def home(v, c):
    s = np.add.reduce(c[:, None] * (v >> 2), axis=0)
    return s & (N - 1), (s >> LN) & (H - 1)
def store(p, g, v, words, at=None):
    d, h = home(v if at is None else at, p["co"][0, g, :, 2])
    for j in range(v.shape[1]):
        p["xst"][d[j], g, :, h[j]] = v[:, j]; p["vst"][d[j], g, h[j]] = words[j]
def fill(u):
    c = np.zeros(16, np.int64)
    for i in range(6):
        c[i] = min(255, u); u = u - int(c[i])
    return c
def parts(rng, co, noise, wild):
    p = dict(co=co, gen=np.zeros((N, 8, 16, Q), np.int64), hlp=rng.integers(0, Q, (N, 8, 16, B)), xl=np.zeros((N, 8, 16, L), np.int64), wl=rng.integers(0, Q, (N, 8, L)), vst=rng.integers(0, Q, (N, 8, H)), cb=[])
    p["xst"] = np.where(rng.random((N, 8, 1, H)) < 0.1, rng.integers(0, 256, (N, 8, 16, H)), 255)
    for g in range(8):
        cb = code(rng, int(rng.integers(5, 9))); p["cb"].append(cb)
        for a in range(N):
            p["gen"][a, g] = lay(rng, cb, Q, noise, wild); p["xl"][a, g] = lay(rng, cb, L, noise, 4 * wild)
        v = lay(rng, cb, len(cb), noise, 0.0); store(p, g, v, rng.integers(0, Q, len(cb)))
    return p
def pack(p):
    def b(a, n): return np.ascontiguousarray(a.reshape(N, 128, n)).astype(np.float32).astype(BF)
    return {"gen": b(p["gen"], Q), "hlp": np.ascontiguousarray(p["hlp"].reshape(N, 128, B)).astype(np.int32), "xl": b(p["xl"], L), "wl": p["wl"].astype(np.int32),
            "xst": b(p["xst"], H), "vst": p["vst"].astype(np.int32), "co": b(p["co"], 3)}
def setup_inputs(rng):
    return pack(parts(rng, coefs(rng), 0.008, 0.02))
def setup_inputs_spread(rng):
    co = coefs(rng); co[..., 0] = np.minimum(np.exp2(8 * rng.random((N, 8, 16))).astype(np.int64), 255)
    p = parts(rng, co, 0.02, 0.02)
    for g in range(1, 8, 2):
        p["gen"][:, g] = np.minimum((np.exp2(1 + 5 * rng.random((N, 1, Q))) * 2 * rng.random((N, 16, Q))).astype(np.int64), 63)
        p["xl"][:, g] = np.minimum((np.exp2(1 + 5 * rng.random((N, 1, L))) * 2 * rng.random((N, 16, L))).astype(np.int64), 63)
        p["xst"][:, g] = np.where(rng.random((N, 1, H)) < 0.5, (256 * rng.random((N, 16, H)) ** 3).astype(np.int64), p["xst"][:, g])
    p["hlp"][:, ::2] = (Q * rng.random((N, 4, 16, B)) ** 3).astype(np.int64)
    p["wl"] = (Q * rng.random((N, 8, L)) ** 2).astype(np.int64)
    return pack(p)
def setup_inputs_ends(rng):
    co = 255 * rng.integers(0, 2, (N, 8, 16, 3)); mid = rng.integers(1, 256, co.shape); half = rng.random(co.shape) < 0.5
    co[:, 0::4] = np.where(half, mid, co)[:, 0::4]; co[:, 3::4] = 255
    co[:, 2, :, 0] = 0; co[:, 2, 15, 0] = 255; co[:, 5, :, 0] = 0; co[:, 5, :, 2] = 255; co[..., 2] = co[0, ..., 2].copy()
    p = parts(rng, co, 0.0, 0.0)
    def e(hi, sh): return np.where(rng.random(sh) < 0.7, hi * rng.integers(0, 2, sh), rng.integers(0, hi + 1, sh))
    p["hlp"] = e(Q - 1, (N, 8, 16, B)); p["wl"] = e(Q - 1, (N, 8, L)); p["vst"] = e(Q - 1, (N, 8, H))
    xs = p["xst"]; p["xst"] = np.where((xs == 0) | (xs == 63) | (xs == 255), xs, 255 * rng.integers(0, 2, xs.shape))
    bb = (255 * 15 * 16) & (B - 1)
    for a in range(N):
        for g in range(8):
            G = p["gen"][a, g]
            if g % 4 == 3:
                G[:, 0] = 0; G[:, Q - 1] = 63; G[:, Q - 2] = 63; G[:, 1] = 0; G[15, 1] = 1; G[:, Q - 3] = G[:, 1]
                h = np.zeros(16, np.int64)
                if a % 2 == 1: h[9] = Q - 3; h[15] = 1
                else: h[6] = Q - 2; h[15] = Q - 1
                p["hlp"][a, g, :, bb] = h
                pick = rng.random(L) < 0.15; pick[0] = True; pick[3] = True; pick[L - 1] = True
                p["xl"][a, g][:, pick] = 63
            elif g % 4 == 0: G[:, 0] = 63; G[:, Q - 1] = 0
            else: G[:, 0] = 63 * p["cb"][g][int(rng.integers(1, len(p["cb"][g])))]; G[:, Q - 1] = G[:, 0]
    p["hlp"][:, 7, :, B - 1] = Q - 1; p["hlp"][:, 7, :, B - 2] = 0
    v = np.full(16, 63); v[15] = 0
    p["xl"][:, 5] = v[:, None]; store(p, 5, v[:, None], [Q - 1])
    p["wl"][:, 5, 0] = Q - 1; p["wl"][:, 5, 1] = 0
    return pack(p)
def setup_inputs_corners(rng):
    co = coefs(rng)
    for g in range(0, 8, 2):
        co[:, g, :, 0] = 0; co[:, g, :, 2] = N * rng.integers(1, 31, 16); co[:, g, 0, 2] = 1
        co[:, g + 1, :, 0] = 255 * rng.integers(0, 2, (N, 16))
    p = parts(rng, co, 0.008, 0.02)
    p["wl"] = np.where(rng.random((N, 8, L)) < 0.3, (Q - 1) * rng.integers(0, 2, (N, 8, L)), p["wl"])
    p["xst"][:, 3] = 255
    for a in range(N): p["xst"][a, 1] = lay(rng, p["cb"][1], H, 0.008, 0.02)
    for g in range(0, 8, 2):
        for a in range(N):
            if g == 2: to = [(a + 1) % N] * L
            elif g == 6: to = [N - 1] * L
            else: to = [(a + 1) % N] * CAP + [(a + 2) % N] * (CAP + 1) + [(a + 3) % N] * (CAP - 1) + [(a + 4) % N] + [a] * (L - 3 * CAP - 1)
            p["xl"][a, g, 0] = 4 * rng.permutation(np.array(to)) + rng.integers(0, 4, L)
            ls = rng.permutation(L)[:60]; its = p["xl"][a, g][:, ls]
            far = (its == 63) & (rng.random((1, 60)) < 0.3); far[0] = False
            store(p, g, np.where(far, 255, its), np.where(rng.random(60) < 0.5, p["wl"][a, g, ls], rng.integers(0, Q, 60)), its)
    return pack(p)
def setup_inputs_crowd(rng):
    co = coefs(rng); co[:, 3:, :, 0] = 0; co[:, 1, :, 0] = 0
    v = np.full(16, 21); v[:6] = 63; v[11] = 5; v[12] = 0; v[13] = 1
    u, rem = divmod(N * H - 1, 15); c = fill(u); c[13] = (-u) & (N - 1); c[15] = 1; v[15] = 4 * rem + 1; co[:, 3:, :, 2] = c
    u, rem = divmod(B - 1, 15); c = fill(u); c[11] = rem
    co[:, 4, :, 1] = c; co[:, 7, :, 1] = c
    gw = v.copy(); gw[12] = 63; aft = (63 - np.abs(v - gw))[:, None]
    p = parts(rng, co, 0.008, 0.02)
    for g, far in ((3, 0), (4, 1), (5, 7), (6, 7), (7, 5)):
        w0 = int(rng.integers(0, Q)); word = w0 ^ 1
        if g == 4: w0, word = Q - 9, Q - 7
        if g == 7: w0, word = Q - 7, Q - 9
        p["gen"][:, g, :, w0] = gw; p["xl"][:, g] = v[:, None]; p["wl"][:, g] = w0
        store(p, g, v[:, None], [word]); s = aft.copy(); s[3, 0] = 63 - far
        if g == 3: s[12, 0] = 255
        store(p, g, s, [int(rng.integers(0, Q))], aft)
        if g in (3, 5, 6): p["xl"][int(rng.integers(0, N)), g, 14, CAP - 1] = 22
    for g in (0, 1, 2):
        cb = p["cb"][g]; few = 63 * cb[rng.integers(1, len(cb), 4)].T
        if g == 0: p["xl"][:, g] = few[:, rng.integers(0, 4, (N, L))].transpose(1, 0, 2)
        else:
            p["xl"][:, g] = few[:, :1]
            if g == 2:
                for a in range(N): p["xl"][a, g, :, int(rng.integers(0, L))] = rng.integers(0, 64, 16)
            else: store(p, g, np.full((16, 1), 255), [0], few[:, :1])
    for a in range(N):
        it = rng.integers(1, 64, 16); bb = int(np.add.reduce(co[a, 0, :, 1] * (it >> 2))) & (B - 1)
        p["gen"][a, 0, :, Q - 9] = it; p["hlp"][a, 0, 0, bb] = Q - 9
        ls = np.array([0, 9, L - 1]); p["xl"][a, 0][:, ls] = it[:, None]; p["wl"][a, 0, ls] = Q - 7
    return pack(p)
def check_inputs(d):
    bad = []
    for k, lo, hi in (("gen", 0, 63), ("hlp", 0, Q - 1), ("xl", 0, 63), ("wl", 0, Q - 1), ("xst", 0, 255), ("vst", 0, Q - 1), ("co", 0, 255)):
        a = np.asarray(d[k]).astype(np.float64)
        if not (np.all(a >= lo) and np.all(a <= hi)): bad.append("range of " + k)
        elif np.any(a != np.floor(a)): bad.append("whole numbers in " + k)
    c = np.asarray(d["co"]).astype(np.float64)[..., 2]
    if np.any(c != c[:1]): bad.append("column 2 of co alike on all ranks")
    return bad
def reference(gen, hlp, xl, wl, xst, vst, co):
    G = gen.astype(np.float32).astype(np.int32).reshape(N, 8, 16, Q); S = hlp.astype(np.int32).reshape(N, 8, 16, B)
    x = xl.astype(np.float32).astype(np.int32).reshape(N, 8, 16, L); W = wl.astype(np.int32)
    X = xst.astype(np.float32).astype(np.int32).reshape(N, 8, 16, H); V = vst.astype(np.int32)
    cc = co.astype(np.float32).astype(np.int32).reshape(N, 8, 16, 3); cw, ca, cp = cc[..., 0:1], cc[..., 1:2], cc[..., 2:3]
    A = np.zeros((N, 8), np.int64)
    for t in range(TR):
        for step in range(ST):
            b = np.add.reduce(ca * (x >> 2), axis=2) & (B - 1)
            hs = np.take_along_axis(S, b[:, :, None, :], 3)
            y = np.take_along_axis(G, hs.reshape(N, 8, 1, 16 * L), 3).reshape(N, 8, 16, 16, L)
            y = np.abs(x[:, :, :, None, :] - y)
            sc = np.add.reduce(cw[..., None] * y, axis=2)
            k = np.argmin(sc, axis=2)
            go = np.min(sc, axis=2) < np.add.reduce(cw * x, axis=2)
            yk = np.take_along_axis(y, k[:, :, None, None, :], 3)[:, :, :, 0]
            s = np.take_along_axis(hs, k[:, :, None, :], 2)[:, :, 0]
            x = np.where(go[:, :, None], yk, x)
            W = np.where(go, ((W * s >> 5) + W + 37 * s) & (Q - 1), W)
        f = np.add.reduce(cp * (x >> 2), axis=2); to = f & (N - 1); pl = (f >> LN) & (H - 1)
        ret = np.full((N, 8, L), -1, np.int32)
        for d in range(N):
            m = to == d; sent = m & (np.add.accumulate(m.astype(np.int32), axis=2) <= CAP)
            dist = np.add.reduce(np.abs(np.take_along_axis(X[d][None], pl[:, :, None, :], 3) - x), axis=2)
            kn = sent & (dist <= (A[d] & 7)[None, :, None]); un = sent & ~kn
            ret = np.where(kn, np.take_along_axis(V[d][None], pl, 2), ret)
            A[d] = np.count_nonzero(kn, axis=(0, 2))
            for g in range(8):
                aa, ll = np.nonzero(un[:, g])
                u, first = np.unique(pl[aa, g, ll], return_index=True); aa, ll = aa[first], ll[first]
                X[d, g][:, u] = x[aa, g, :, ll].T; V[d, g, u] = W[aa, g, ll]
        up = (ret >= 0) & (ret != W); new = ((ret * W >> 5) + ret + W) & (Q - 1)
        for r in range(N):
            for g in range(8):
                ll = np.nonzero(up[r, g])[0]
                u, first = np.unique(b[r, g, ll], return_index=True); ll = ll[first]
                S[r, g, (ll + t) & 15, u] = new[r, g, ll]
        x = 63 - np.abs(x - np.take_along_axis(G, W[:, :, None, :], 3))
    sh = np.add.reduce(S * np.arange(1, 17, dtype=np.int32)[:, None], axis=2)
    return {"yx": x.reshape(N, 128, L).astype(np.float32).astype(BF), "yw": W.astype(np.float32), "ys": X.reshape(N, 128, H).astype(np.float32).astype(BF),
            "yv": V.astype(np.float32), "yh": sh.astype(np.float32)}

@@ -1,0 +1,712 @@
+from concourse.bass import DstId, RemoteDMATransfer
+from concourse.mybir import AluOpType as A, ActivationFunctionType as F
+
+N, Q, H, L, CAP, TR, ST = 4, 4096, 1024, 256, 64, 4, 3
+MAGIC = 12582912.0
+BIGK = 32768.0
+FR = 16384.0
+f32, b16, i32, u16 = "float32", "bfloat16", "int32", "uint16"
+
+SB = {
+    "Gz": (4112, b16), "hi": (4096, i32), "SW": (4352, f32), "YH": (4352, f32), "XW": (4352, f32),
+    "xs": (1024, b16), "vi": (1024, i32), "vf": (1024, f32), "wi": (256, i32), "wf": (256, f32),
+    "cb": (16, b16), "cf": (8, f32),
+    "x0": (256, b16), "x1": (256, b16), "x2": (256, b16), "x3": (256, b16), "q0": (256, b16), "q1": (256, b16),
+    "xT": (256, b16), "gA": (2048, b16), "gB": (2048, b16), "mA": (2048, b16), "mB": (2048, b16),
+    "bj": (32, i32), "bI": (32, i32), "bu": (16, u16), "hu": (256, u16), "hf": (256, f32),
+    "us": (272, f32), "nf": (272, f32), "es": (272, f32), "em": (256, f32), "su": (16, u16), "dd": (256, b16),
+    "W": (16, i32), "sA": (16, f32), "sB": (16, f32), "pA": (16, i32), "pB": (16, i32), "pC": (16, f32), "pD": (16, i32),
+    "fj": (32, i32), "fk": (32, i32), "fy": (32, i32), "fx": (32, i32), "fu": (16, u16), "own": (16, i32),
+    "oh": (64, b16), "le": (64, f32), "iq": (64, f32), "th": (64, f32), "ta": (32, f32), "tb": (16, f32), "thr": (64, f32),
+    "xa": (256, b16), "ad": (256, b16), "pr": (256, f32), "we": (256, f32),
+    "t1": (16, f32), "t2": (16, f32), "vt": (16, f32), "e1": (16, f32), "e2": (16, f32), "e3": (16, f32), "isq": (16, f32),
+    "base": (16, f32), "bD": (16, f32), "ne": (16, f32), "dl": (16, f32), "kn": (16, f32), "k1": (16, f32), "key": (16, f32),
+    "za": (16, i32), "zb": (16, i32), "zc": (16, f32), "zf": (16, f32),
+    "EB": (256, f32), "EM": (256, f32), "ZB": (256, f32), "kO": (16, f32), "kR": (256, u16), "E": (4096, b16),
+    "K": (256, f32), "oS": (16, f32), "oU": (16, u16), "oa": (16, f32), "ob": (16, f32), "zm": (256, f32), "hm": (256, f32), "yn": (256, f32),
+    "k4": (64, b16), "PAY": (4096, f32), "MET": (768, f32), "mu": (192, u16), "ca": (32, f32), "ci": (32, i32),
+    "jm": (256, f32), "ja": (256, b16), "yv8": (1024, f32),
+    "pi": (4, i32), "pc": (8, f32), "JJ": (272, f32), "EK": (272, f32), "NK": (272, f32), "NEG": (256, b16),
+    "vv": (136, f32), "v2": (136, f32), "If": (128, f32), "Ib": (384, b16), "cst": (384, b16), "GB": (16, f32), "Gb": (64, b16),
+    "BD": (256, b16), "kw": (128, f32), "R": (2048, b16), "DM": (136, f32), "DLT": (136, f32), "RST": (256, f32),
+    "ls": (32, u16), "J": (48, f32), "dc": (64, f32), "DT": (32, f32), "Aw": (288, b16), "CA": (64, f32), "sT": (128, f32),
+}
+SCRATCH, WHERE = {}, {}
+for _k, (_n, _d) in SB.items():
+    if _n <= 64:
+        _at = SCRATCH.get("pool_" + _d, ("sbuf", [128, 0], _d))[1][1]
+        WHERE[_k] = ("pool_" + _d, _at)
+        SCRATCH["pool_" + _d] = ("sbuf", [128, _at + (_n + 31) // 32 * 32], _d)
+    else:
+        WHERE[_k] = (_k, 0)
+        SCRATCH[_k] = ("sbuf", [128, _n], _d)
+for _b in range(8):
+    SCRATCH["ps%d" % _b] = ("psum", [128, 512], f32)
+NDMA = 40
+SEMAPHORES = ["cV", "cS", "cP", "cG"] + ["d%d" % _i for _i in range(NDMA)] + ["ar%d" % _i for _i in range(9)]
+
+HOP = 90.0
+
+
+def build(g, core, T, topo, rank):
+    ops = []
+    hist = {}
+    ndma = [0]
+    narr = [0]
+    low = ["i"]
+
+    def ap(name, lo=0, hi=None, step=1, p0=0, p1=128, ps=1):
+        tn, at = WHERE.get(name, (name, 0))
+        t = T[tn]
+        if hi is None:
+            hi = SB[name][0]
+        rows = slice(p0, p1, ps) if ps != 1 else slice(p0, p1)
+        a = t[rows, at + lo:at + hi:step] if step != 1 else t[rows, at + lo:at + hi]
+        return (a, [(name, lo, hi)], len(range(lo, hi, step)), "")
+
+    def ind(w, o):
+        return (w[0].indirect(o[0]), w[1], 16 * o[2], "ind", o[1])
+
+    def two(a):
+        return a[1][0][0] in SB and SB[a[1][0][0]][1] in (b16, u16)
+
+    def psum(a):
+        return a[1][0][0].startswith("ps")
+
+    def add(eng, fn, outs, ins, dur, lat=0.0, tok=None, extra=()):
+        i = len(ops)
+        deps = {}
+        for e in extra:
+            deps[e] = True
+        acc = []
+        for a in outs:
+            acc += [(r, True) for r in a[1]]
+            if a[3]:
+                acc += [(r, False) for r in a[4]]
+        for a in ins:
+            if isinstance(a, tuple):
+                acc += [(r, False) for r in a[1]]
+                if a[3]:
+                    acc += [(r, False) for r in a[4]]
+        for (name, lo, hi), w in acc:
+            h = hist.setdefault(name, [])
+            if name.startswith("ps"):
+                if h and h[-1] != i:
+                    j = h[-1]
+                    deps[j] = deps.get(j, False) or ops[j]["eng"] != eng
+                continue
+            for j, l2, h2, w2 in h:
+                if j != i and l2 < hi and lo < h2 and (w or w2):
+                    deps[j] = True
+        for (name, lo, hi), w in acc:
+            h = hist[name]
+            if name.startswith("ps"):
+                h.append(i)
+                continue
+            if w:
+                h[:] = [e for e in h if not (lo <= e[1] and e[2] <= hi)]
+            h.append((i, lo, hi, w))
+        ops.append(dict(eng=eng, fn=fn, deps=deps, dur=dur, lat=lat, tok=tok, nm=acc[0][0], low=low[0],
+                        ty=low[0][:1] + eng + acc[0][0][0][:2] + (str(acc[0][0][1] % 256 // 8) if eng == "P" else "")))
+        return i
+
+    prev = {}
+
+    def chain(k, i):
+        if k in prev and prev[k] not in ops[i]["deps"]:
+            ops[i]["deps"][prev[k]] = False
+        prev[k] = i
+
+    def val(s):
+        return s[0] if isinstance(s, tuple) else s
+
+    def vcost(o, ins, k):
+        if o[3]:
+            return 50 + 3.2 * o[2]
+        if ins[0][3]:
+            return 50 + 1.3 * o[2]
+        return 50 + max(50, 0.83 * k * o[2])
+
+    def cp(o, i):
+        return add("V", lambda: g.vector.tensor_copy(o[0], i[0]), [o], [i], vcost(o, [i], 0.5 if two(o) and two(i) else 1))
+
+    def ts(o, i, s1, o0, s2=None, o1=None):
+        if o1 is None:
+            fn = lambda: g.vector.tensor_scalar(o[0], i[0], val(s1), None, o0)
+        else:
+            fn = lambda: g.vector.tensor_scalar(o[0], i[0], val(s1), val(s2), o0, o1)
+        return add("V", fn, [o], [i, s1, s2], vcost(o, [i], 0.5 if two(o) and two(i) else 1))
+
+    def tt(o, a, b, op):
+        return add("V", lambda: g.vector.tensor_tensor(o[0], a[0], b[0], op), [o], [a, b], vcost(o, [a], 1 if psum(a) or psum(b) else 2))
+
+    def scan(o, a, b, o0, o1):
+        return add("V", lambda: g.vector.tensor_tensor_scan(o[0], a[0], b[0], 0.0, o0, o1), [o], [a, b], vcost(o, [a], 1))
+
+    def ms(o, c):
+        return add("V", lambda: g.vector.memset(o[0], c), [o], [], vcost(o, [o], 0.5 if two(o) else 1))
+
+    def act(o, i, func=F.Identity, bias=0.0, scale=1.0):
+        return add("S", lambda: g.scalar.activation(o[0], i[0], func, bias=bias, scale=scale), [o], [i],
+                   65 + (1.3 if i[3] else 0.83) * max(o[2], 50))
+
+    def mm(o, l, r, st=True, sp=True):
+        return add("P", lambda: g.tensor.matmul(o[0], l[0], r[0], st, sp), [o], [l, r],
+                   10 + 0.5 * max(min(64, l[2]), r[2]) * (1 if two(l) else 4), lat=60.0)
+
+    def iota(o, pat, base, cm):
+        if SB[o[1][0][0]][1] == i32:
+            fn = lambda: g.iota(o[0], pat, base, cm)
+        else:
+            fn = lambda: g.iota(o[0], pat, base, cm, allow_small_or_imprecise_dtypes=True)
+        return add("G", fn, [o], [], 130 + 1.7 * o[2])
+
+    dclock = [0.0]
+
+    def dma(eng, o, i, nbytes, load):
+        s = "d%d" % ndma[0]
+        ndma[0] += 1
+        q = g.sync if eng == "Y" else g.scalar
+        lat = 2000 + nbytes / 150.0
+        if load:
+            dclock[0] += nbytes / 150.0
+            lat = 2000 + dclock[0]
+            return add(eng, lambda: q.dma_start(o[0], i).then_inc(T.sem[s], 16), [o], [], 60, lat=lat, tok=(s, 16))
+        return add(eng, lambda: q.dma_start(o, i[0]).then_inc(T.sem[s], 16), [], [i], 60, lat=lat, tok=(s, 16))
+
+    others = [c for c in T.cores if c != core]
+    common = [e for e in topo.engines(core, others[0]) if all(e in topo.engines(core, c) for c in others)]
+    ne = 1
+    while ne * 2 <= len(common):
+        ne *= 2
+    emask = sum(1 << e for e in common[:ne])
+    dsts = [DstId(rid=topo.addr(c)[0], pnc=topo.addr(c)[1]) for c in others]
+
+    def share(name, base, width, nbytes):
+        s = "d%d" % ndma[0]
+        ndma[0] += 1
+        r = "ar%d" % narr[0]
+        narr[0] += 1
+        a = ap(name, base + rank * width, base + (rank + 1) * width)
+        fn = lambda: g.remote_dma_fused([RemoteDMATransfer(dst_ids=dsts, dma_engine_mask=emask, remote_sem=T.sem[r],
+                                                           src=a[0], dsts=[a[0]] * len(dsts))], local_sem=T.sem[s])
+        i = add("G", fn, [], [a], 1000, lat=1500 + 3 * nbytes / 150.0, tok=(s, ne))
+        land = [ap(name, base + d * width, base + (d + 1) * width) for d in range(N) if d != rank]
+        add("X", None, land, [], 0, lat=300.0, tok=(r, ne * len(others)), extra=[i])
+
+    def P(b, lo, hi, step=1, p1=128):
+        return ap("ps%d" % b, lo, hi, step, 0, p1)
+
+    dma("S", ap("cb", 0, 3), T.co[:], 1e3, True)
+    dma("S", ap("x0"), T.xl[:], 65e3, True)
+    dma("S", ap("wi", p1=8), T.wl[:], 8e3, True)
+    NCH = 8
+    CW = Q // NCH
+    for j in range(NCH):
+        dma("Y", ap("hi", j * CW, (j + 1) * CW), T.hlp[:, j * CW:(j + 1) * CW], 128 * 4 * CW, True)
+        if j == 3:
+            dma("S", ap("Gz", 16, 4112), T.gen[:], 1.05e6, True)
+    dma("Y", ap("xs"), T.xst[:], 262e3, True)
+    dma("Y", ap("vi", p1=8), T.vst[:], 32e3, True)
+
+    iota(ap("pi", 0, 2), [[0, 2]], 0, 1)
+    iota(ap("JJ"), [[0, 17], [1, 16]], 0, 0)
+    ts(ap("pi", 2, 3), ap("pi", 0, 1), 15, A.bitwise_and)
+    ts(ap("pi", 3, 4), ap("pi", 1, 2), 4, A.arith_shift_right)
+    cp(ap("pc", 0, 2), ap("pi", 2, 4))
+    pm, pd = ap("pc", 0, 1), ap("pc", 1, 2)
+    ts(ap("pc", 2, 3), pm, 1.0, A.add)
+    cp(ap("cf", 0, 3), ap("cb", 0, 3))
+    GBf, S0f = ap("GB", 0, 8), ap("GB", 8, 16)
+    ts(GBf, ap("JJ", 0, 8), pd, A.is_equal)
+    W1, W2, ablk, cblk, GBb, nS0 = [ap("Gb", 8 * i, 8 * i + 8) for i in range(6)]
+    ts(ablk, GBf, ap("cf", 1, 2), A.mult)
+    ts(cblk, GBf, ap("cf", 2, 3), A.mult)
+    ms(ap("Aw"), 0.0)
+    cp(ap("Aw", 15, 128, 16), ablk)
+    cp(ap("Aw", 159, 272, 16), cblk)
+    ones, zeros, c192 = ap("cst", 0, 128), ap("cst", 128, 256), ap("cst", 256, 384)
+    ms(c192, 192.0)
+    for o, nm, n8 in ((0, ablk, 0), (144, cblk, 32)):
+        bk = 6 if o == 0 else 7
+        for m in range(16):
+            mm(P(bk, 0, 16), ap("Aw", o + 15 - m, o + 143 - m), ap("cst", 256, 272), m == 0, m == 15)
+        mm(P(bk, 16, 24), c192, nm)
+        if o == 0:
+            act(ap("CA", 0, 16), P(bk, 8, 24))
+            act(ap("CA", 16, 24), P(bk, 16, 24))
+            act(ap("CA", 24, 32), P(bk, 0, 8))
+        else:
+            act(ap("CA", 32, 56), P(bk, 0, 24))
+            act(ap("CA", 56, 64), P(bk, 16, 24))
+    iota(ap("vv", 0, 128), [[1, 128]], 0, -1)
+    If, Ib, nIb, LT = ap("If"), ap("Ib", 0, 128), ap("Ib", 128, 256), ap("Ib", 256, 384)
+    ts(If, ap("vv", 0, 128), 0.0, A.is_equal)
+    ts(Ib, ap("vv", 0, 128), 0.0, A.is_equal)
+    iota(ap("R"), [[1, 128], [0, 16]], 0, -1)
+    ts(ap("R"), ap("R"), 0.0, A.is_equal)
+    ts(nIb, ap("vv", 0, 128), 0.0, A.is_equal, -1.0, A.mult)
+    ts(LT, ap("vv", 0, 128), 0.0, A.is_ge)
+    ts(ap("v2", 0, 128), ap("vv", 0, 128), 0.0, A.is_gt)
+    iota(ap("jm", 0, 128), [[1, 8], [0, 16]], 0, 0)
+    BDB, LTB = ap("BD", 0, 128), ap("BD", 128, 256)
+    ts(BDB, ap("jm", 0, 128), pd, A.is_equal, BIGK, A.mult)
+    ts(ap("kw"), ap("jm", 0, 128), pd, A.is_equal, ap("pc", 2, 3), A.mult)
+    tt(LTB, BDB, ap("v2", 0, 128), A.mult)
+    iota(ap("vv"), [[-16, 8], [-1, 17]], 0, 1)
+    ts(ap("DM"), ap("vv"), -1.0, A.is_equal)
+    ts(ap("v2"), ap("vv"), 0.0, A.is_equal)
+    cp(S0f, ap("v2", 0, 136, 17))
+    ts(nS0, ap("v2", 0, 136, 17), -1.0, A.mult)
+    ms(ap("v2", 16, 136, 17), 0.0)
+    tt(ap("DM"), ap("DM"), ap("v2"), A.subtract)
+    ms(ap("DLT"), -1.0)
+    ms(ap("DLT", 0, 136, 17), 33554432.0)
+    ms(ap("DLT", 16, 136, 17), 16.0)
+    ms(zeros, 0.0)
+    ms(ones, 1.0)
+    ms(ap("Gz", 0, 16), 0.0)
+    ts(W1, GBf, ap("cf", 0, 1), A.mult, 32.0, A.mult)
+    ts(W2, GBf, ap("cf", 0, 1), A.mult, -64.0, A.mult)
+    cp(GBb, GBf)
+    ts(ap("EK"), ap("JJ"), pm, A.is_equal)
+    ts(ap("NK"), ap("JJ"), pm, A.not_equal)
+    ts(ap("NEG"), ap("NK", 0, 256), -33554432.0, A.mult)
+    lc, l17, l4 = ap("ls", 0, 16), ap("ls", 16, 24), ap("ls", 24, 28)
+    cp(lc, ap("JJ", 0, 16))
+    ts(l17, ap("JJ", 0, 8), 17.0, A.mult, 16.0, A.add)
+    ts(ap("J", 0, 16), ap("JJ", 0, 16), 16.0, A.mult, pm, A.add)
+    dumO, dumX = ap("J", 16, 32), ap("J", 32, 48)
+    ts(dumO, ap("J", 0, 16), 4096.0, A.add)
+    ts(dumX, ap("J", 0, 16), 12288.0, A.add)
+    cp(ap("za", 0, 4), ap("J", 0, 4))
+    ts(ap("zb", 0, 4), ap("za", 0, 4), 2, A.arith_shift_right)
+    cp(l4, ap("zb", 0, 4))
+    iota(ap("dc"), [[0, 16], [1, 4]], 0, 0)
+    DT, DT2 = ap("DT", 0, 16), ap("DT", 16, 32)
+    iota(DT, [[128, 2], [0, 8]], 16384, 1)
+    iota(DT2, [[128, 2], [0, 8]], 8192, 1)
+    iota(ap("sT"), [[1, 128]], 0, -16)
+    ts(ap("sT"), ap("sT"), 0.0, A.is_equal)
+    ms(ap("RST"), 0.0)
+    ms(ap("RST", 0, 256, 16), -67108864.0)
+    ms(ap("we"), 0.0)
+    ms(ap("thr"), 0.5)
+    for nm in ("SW", "YH", "XW"):
+        ms(ap(nm, 4096, 4352), 0.0)
+
+    W = ap("W")
+    cp(ap("wf", p1=8), ap("wi", p1=8))
+    for h in range(2):
+        mm(P(6, 8 * h, 8 * h + 8), ap("wf", 128 * h, 128 * h + 128, p1=8), ap("If", 0, 8, p1=8))
+    cp(W, P(6, 0, 16))
+    for j in range(NCH):
+        cp(ap("SW", j * CW, (j + 1) * CW), ap("hi", j * CW, (j + 1) * CW))
+    for j in range(4):
+        ts(ap("vf", 256 * j, 256 * j + 256, p1=8), ap("vi", 256 * j, 256 * j + 256, p1=8), -2047.5, A.add, 1.0 / FR, A.mult)
+
+    def sums(j):
+        bk = 2 + j % 2
+        for u in range(2):
+            mm(P(bk, 256 * u, 256 * u + 256), ap("kw"), ap("SW", 512 * j + 256 * u, 512 * j + 256 * u + 256))
+        act(ap("YH", 512 * j, 512 * j + 512), P(bk, 0, 512))
+
+    def store(j):
+        bk = 2 + j % 2
+        mm(P(bk, 0, 512), Ib, ap("xs", 512 * j, 512 * j + 512), True, False)
+        for u in range(2):
+            mm(P(bk, 256 * u, 256 * u + 256), ap("sT", p1=8), ap("vf", 512 * j + 256 * u, 512 * j + 256 * u + 256, p1=8), False, u == 1)
+        act(ap("XW", H * rank + 512 * j, H * rank + 512 * j + 512), P(bk, 0, 512))
+
+    for j in range(6):
+        sums(j)
+
+    xv, qv, rb = [0], [0], [0]
+    for h in range(2):
+        act(ap("q0", 128 * h, 128 * h + 128), ap("x0", 128 * h, 128 * h + 128), scale=0.25, bias=191.625)
+
+    def step_half(h, last, xo, xn, qo, qn):
+        lo, hi = 128 * h, 128 * h + 128
+        kb, mb = 2 + h, 4 + h
+        late = False
+        gn, mn = "gA" if h == 0 else "gB", "mA" if h == 0 else "mB"
+        oc, tc = (0, 8) if h == 0 else (8, 0)
+        mm(P(kb, 256, 384), ap(xo, lo, hi), Ib)
+        act(ap("xT", lo, hi), P(kb, 256, 384))
+        for m in range(16):
+            mm(P(mb, oc, oc + 8), ap("Aw", 15 - m, 143 - m), ap(qo, lo + m, hi, 16), m == 0, m == 15)
+        a0, a1 = (oc, oc + 8)
+        if last:
+            mm(P(mb, tc, tc + 8), ap(qo, lo, hi), ablk)
+            a0, a1 = 0, 16
+        b0, b1 = 16 * h + a0, 16 * h + a1
+        tt(ap("bj", b0, b1), P(mb, a0, a1), ap("CA", b0, b1), A.subtract)
+        ts(ap("bI", b0, b1), ap("bj", b0, b1), 4095, A.bitwise_and)
+        bu = ap("bu", 8 * h, 8 * h + 8)
+        cp(bu, ap("bI", 24 * h, 24 * h + 8))
+        cp(ap("hu", lo, hi), ind(ap("SW", 0, 4096), bu))
+        act(ap("hf", lo, hi), ind(ap("SW", 0, 4096), bu), bias=16.0)
+        if not late:
+            mm(P(mb, 272, 408), ap("hf", lo, hi), ap("DM"))
+        for j in range(4):
+            bk = 6 * h + j % 2
+            mm(P(bk, 0, 512), ap("xT", lo, hi), ap("R", 512 * j, 512 * j + 512))
+            gj = ap(gn, 512 * j, 512 * j + 512)
+            chain("g", act(gj, ind(ap("Gz", 16, 4112), ap("hu", lo + 32 * j, lo + 32 * j + 32))))
+            chain("m", tt(ap(mn, 512 * j, 512 * j + 512), gj, P(bk, 0, 512), A.min))
+        mm(P(kb, 0, 136), zeros, ap("R", 0, 136), True, False)
+        for k in range(16):
+            mm(P(kb, k, 136, 17), ap(gn, k, 2048, 16), W1, False, False)
+        for k in range(16):
+            mm(P(kb, k, 136, 17), ap(mn, k, 2048, 16), W2, False, k == 15)
+        s0, s1 = 136 * h, 136 * h + 136
+        scan(ap("us", s0, s1), ap("DLT"), P(kb, 0, 136), A.add, A.min)
+        tt(ap("nf", s0, s1), ap("us", s0, s1), P(kb, 0, 136), A.not_equal)
+        scan(ap("es", s0, s1), P(mb, 272, 408), ap("nf", s0, s1), A.add, A.mult)
+        tt(ap("em", lo, hi), ind(ap("es", s0, s1), l17), ap("EK", 0, 128), A.mult)
+        mm(P(mb, 256, 264), ap("em", lo, hi), GBf)
+        su = ap("su", 8 * h, 8 * h + 8)
+        cp(su, P(mb, 256, 264))
+        tt(ap("dd", lo, hi), ind(ap("Gz"), su), ap(xo, lo, hi), A.subtract)
+        act(ap(xn, lo, hi), ap("dd", lo, hi), F.Abs)
+        act(ap(qn, lo, hi), ap(xn, lo, hi), scale=0.25, bias=191.625)
+
+    def nextx():
+        xo, qo = "x%d" % (xv[0] % 4), "q%d" % (qv[0] % 2)
+        xv[0] += 1
+        qv[0] += 1
+        return xo, "x%d" % (xv[0] % 4), qo, "q%d" % (qv[0] % 2)
+
+    for t in range(TR):
+        fin = t == TR - 1
+        for s in range(ST):
+            xo, xn, qo, qn = nextx()
+            for h in range(2):
+                low[0] = "AB"[h] + str(s)
+                step_half(h, s == ST - 1, xo, xn, qo, qn)
+            low[0] = "w%d" % s
+            if t == 0 and s == 0:
+                store(0)
+                store(1)
+                share("XW", 0, H, 524e3)
+            if t == 0 and s == 1:
+                sums(6)
+                sums(7)
+            e = ap("es", 16, 272, 17)
+            act(ap("sA"), e, F.Relu, bias=-16.0)
+            act(ap("sB"), e, F.Relu, bias=-592.0, scale=37.0)
+            tt(ap("pA"), W, ap("sA"), A.mult)
+            tt(ap("pC"), W, ap("sB"), A.add)
+            ts(ap("pB"), ap("pA"), 5, A.arith_shift_right)
+            tt(ap("pD"), ap("pB"), ap("pC"), A.add)
+            ts(W, ap("pD"), 4095, A.bitwise_and)
+        xo, xn, qo, qn = nextx()
+        x = ap(xo)
+        low[0] = "r"
+        tt(ap("hm"), ind(ap("SW", 0, 4096), ap("bu")), ap("NK", t, t + 256), A.mult)
+        for m in range(16):
+            mm(P(2, 0, 16), ap("Aw", 159 - m, 287 - m), ap(qo, m, 256, 16), m == 0, m == 15)
+        for h in range(2):
+            mm(P(2, 16 + 8 * h, 24 + 8 * h), ap(qo, 128 * h, 128 * h + 128), cblk)
+        tt(ap("fj"), P(2, 0, 32), ap("CA", 32, 64), A.subtract)
+        ts(ap("fk"), ap("fj"), 4095, A.bitwise_and)
+        ts(ap("fy"), ap("fk"), 4097.0, A.mult)
+        ts(ap("fx"), ap("fy"), 2, A.arith_shift_right, 4095, A.bitwise_and)
+        cp(ap("fu"), ap("fx", 0, 16))
+        idx = ap("fx", 16, 32)
+        ts(ap("own"), ap("fj", 16, 32), 3, A.bitwise_and)
+        XWw = ap("XW", 0, 4096)
+        tt(ap("xa"), ind(XWw, ap("fu")), x, A.subtract)
+        act(ap("pr"), ind(XWw, ap("fu")))
+        act(ap("ad"), ap("xa"), F.Abs)
+        tt(ap("oh"), ind(ap("own"), l4), ap("dc"), A.is_equal)
+        mm(P(6, 0, 32), LT, ap("oh", 0, 32))
+        mm(P(6, 32, 64), LT, ap("oh", 32, 64), True, False)
+        mm(P(6, 32, 64), ones, ap("oh", 0, 32), False, True)
+        ts(ap("le"), P(6, 0, 64), CAP + 0.5, A.is_lt)
+        tt(ap("iq"), ap("le"), ap("oh"), A.mult)
+        tt(ap("th"), ap("iq"), ap("thr"), A.mult)
+        tt(ap("ta"), ap("th", 0, 64, 2), ap("th", 1, 64, 2), A.add)
+        tt(ap("tb"), ap("ta", 0, 32, 2), ap("ta", 1, 32, 2), A.add)
+        ts(ap("we", 0, 256, 16), W, -2047.5, A.add, 1.0 / FR, A.mult)
+        mm(P(7, 0, 256), Ib, x, True, False)
+        for h in range(2):
+            mm(P(7, 128 * h, 128 * h + 128), ap("we", 128 * h, 128 * h + 128), If, False, h == 1)
+        act(ap("PAY", 1024 * t + 256 * rank, 1024 * t + 256 * rank + 256), P(7, 0, 256))
+        share("PAY", 1024 * t, 256, 131e3)
+        tt(ap("jm"), ind(W, lc), ap("EK", 0, 256), A.mult)
+        for h in range(2):
+            lo, hi = 128 * h, 128 * h + 128
+            mm(P(4 + h, 256, 264), ap("jm", lo, hi), GBf)
+            su = ap("su", 8 * h, 8 * h + 8)
+            cp(su, P(4 + h, 256, 264))
+            tt(ap("dd", lo, hi), ind(ap("Gz", 16, 4112), su), ap(xo, lo, hi), A.subtract)
+            act(ap("ja", lo, hi), ap("dd", lo, hi), F.Abs)
+            act(ap(xn, lo, hi), ap("ja", lo, hi), scale=-1.0, bias=63.0)
+            if not fin:
+                act(ap(qn, lo, hi), ap("ja", lo, hi), scale=-0.25, bias=207.375)
+        for h in range(2):
+            mm(P(2, 8 * h, 8 * h + 8), ap("pr", 128 * h, 128 * h + 128), S0f)
+        ts(ap("t1"), P(2, 0, 16), MAGIC, A.add, MAGIC, A.subtract)
+        tt(ap("t2"), P(2, 0, 16), ap("t1"), A.subtract)
+        vt = ap("vt")
+        ts(vt, ap("t2"), FR, A.mult, 2047.5, A.add)
+        for h in range(2):
+            mm(P(3, 256 + 8 * h, 264 + 8 * h), ap("ad", 128 * h, 128 * h + 128), GBb)
+        tt(ap("e1"), idx, DT2, A.subtract)
+        ts(ap("isq"), ap("tb"), 0.25, A.is_gt)
+        tt(ap("e2"), ap("isq"), ap("e1"), A.mult)
+        tt(ap("base"), ap("e2"), DT, A.add)
+        tt(ap("bD"), ap("bI", 8, 24), DT, A.subtract)
+        tt(ap("ne"), vt, W, A.not_equal)
+        tt(ap("e3"), ap("ne"), ap("bD"), A.mult)
+        tt(ap("dl"), ap("e3"), ap("e1"), A.subtract)
+        tt(ap("kn"), P(3, 256, 272), ap("tb"), A.is_lt)
+        tt(ap("k1"), ap("kn"), ap("dl"), A.mult)
+        key = ap("key")
+        tt(key, ap("k1"), ap("base"), A.add)
+        tt(ap("za"), vt, W, A.mult)
+        tt(ap("zc"), vt, W, A.add)
+        ts(ap("zb"), ap("za"), 5, A.arith_shift_right)
+        tt(ap("za"), ap("zb"), ap("zc"), A.add)
+        ts(ap("zb"), ap("za"), 4095, A.bitwise_and)
+        cp(ap("zf"), ap("zb"))
+        act(ap("EB"), ind(key, lc))
+        tt(ap("EM"), ind(key, lc), ap("EK", 0, 256), A.mult)
+        for h in range(2):
+            mm(P(2, 128 * h, 128 * h + 128), ap("EB", 128 * h, 128 * h + 128), If)
+        for h in range(2):
+            mm(P(6, 8 * h, 8 * h + 8), ap("EM", 128 * h, 128 * h + 128), GBf)
+        cp(ap("kR"), P(2, 0, 256))
+        act(ap("kO"), P(6, 0, 16))
+        act(ap("ZB"), ind(ap("zf"), lc))
+        mm(P(3, 0, 256), Ib, ap("NEG"), True, False)
+        for h in range(2):
+            mm(P(3, 128 * h, 128 * h + 128), ap("EB", 128 * h, 128 * h + 128), If, False, False)
+        for h in range(2):
+            mm(P(7, 128 * h, 128 * h + 128), ap("ZB", 128 * h, 128 * h + 128), If)
+        for c in range(16):
+            ts(ap("E", 256 * c + 16 * c, 256 * c + 256), ap("kR", 16 * c, 256), ap("kO", c, c + 1), A.is_equal)
+            mm(P(3, 16 * c, 16 * c + 16), LTB, ap("E", 272 * c, 272 * c + 16), False, c == 15)
+            if c < 15:
+                mm(P(3, 16 * c + 16, 256), BDB, ap("E", 272 * c + 16, 256 * c + 256), False, False)
+        tt(ap("zm"), P(7, 0, 256), ap("EK", t, t + 256), A.mult)
+        scan(ap("K"), ap("RST"), P(3, 0, 256), A.add, A.max)
+        Kd = ap("K", 15, 256, 16)
+        tt(ap("oS"), Kd, dumO, A.min)
+        cp(ap("oU"), ap("oS"))
+        if not fin:
+            tt(ind(ap("SW"), ap("oU")), ap("zm"), ap("hm"), A.add)
+        mw = 16 if fin else 48
+        mb = 192 * t + mw * rank
+        ts(ap("oa"), Kd, 8192.0, A.is_lt, BIGK, A.mult)
+        tt(ap("ob"), ap("oa"), Kd, A.add)
+        tt(ap("MET", mb, mb + 16), ap("ob"), dumX, A.min)
+        if not fin:
+            tt(ap("k4"), ind(ap("kn"), l4), ap("iq"), A.mult)
+            mm(P(6, 0, 32), ones, ap("k4", 0, 32), True, False)
+            mm(P(6, 0, 32), ones, ap("k4", 32, 64), False, True)
+            act(ap("MET", mb + 16, mb + 48), P(6, 0, 32))
+        share("MET", 192 * t, mw, 512 * mw)
+        mm(P(7, 0, 256), ap("kw"), ap("zm"), True, False)
+        mm(P(7, 0, 256), ap("kw"), ap("hm"), False, True)
+        act(ap("yn"), P(7, 0, 256))
+        cp(ind(ap("YH"), ap("oU")), ap("yn"))
+        ts(ap("mu", 0, 4 * mw), ap("MET", 192 * t, 192 * t + 4 * mw), 8192.0, A.subtract)
+        for a in range(N - 1, -1, -1):
+            cp(ind(ap("XW"), ap("mu", mw * a, mw * a + 16)), ap("PAY", 1024 * t + 256 * a, 1024 * t + 256 * a + 256))
+        if not fin:
+            c = [ap("MET", 192 * t + 48 * a + 16, 192 * t + 48 * a + 48) for a in range(N)]
+            tt(ap("ca"), c[0], c[1], A.add)
+            tt(ap("ta"), c[2], c[3], A.add)
+            tt(ap("ci"), ap("ca"), ap("ta"), A.add)
+            ts(ap("ci"), ap("ci"), 7, A.bitwise_and)
+            for h in range(2):
+                ts(ap("thr", 32 * h, 32 * h + 32), ap("ci"), 0.5, A.add)
+
+    dma("Y", T.yx[:], ap(xn), 65e3, False)
+    cp(ap("sA"), W)
+    for h in range(2):
+        mm(P(0, 128 * h, 128 * h + 128, p1=8), ap("sA", 8 * h, 8 * h + 8), If)
+    act(ap("wf", p1=8), P(0, 0, 256, p1=8))
+    dma("Y", T.yw[:], ap("wf", p1=8), 8e3, False)
+    dma("Y", T.yh[:], ap("YH", 0, 4096, ps=16), 131e3, False)
+    for j in range(4):
+        lo, hi = 256 * j, 256 * j + 256
+        src = ap("XW", H * rank + lo, H * rank + hi)
+        ts(ap("xs", lo, hi), src, MAGIC, A.add, MAGIC, A.subtract)
+        mm(P(j % 2, 0, 256, p1=8), S0f, src, True, False)
+        mm(P(j % 2, 0, 256, p1=8), nS0, ap("xs", lo, hi), False, True)
+        act(ap("yv8", lo, hi, p1=8), P(j % 2, 0, 256, p1=8), scale=FR, bias=2047.5)
+        if j % 2 == 1:
+            dma("Y", T.ys[:, lo - 256:hi], ap("xs", lo - 256, hi), 131e3, False)
+    dma("Y", T.yv[:], ap("yv8", p1=8), 32e3, False)
+    return ops
+
+
+def schedule(ops):
+    n = len(ops)
+    succ = [[] for _ in range(n)]
+    for i, o in enumerate(ops):
+        for j in o["deps"]:
+            succ[j].append(i)
+    bl = [0.0] * n
+    for i in range(n - 1, -1, -1):
+        o = ops[i]
+        bl[i] = o["dur"] + max([0.0] + [bl[k] + ((HOP + o["lat"]) if ops[k]["deps"][i] else 0.0) for k in succ[i]] + [o["lat"]])
+    left = [len(o["deps"]) for o in ops]
+    rdy = [0.0] * n
+    ready = {}
+    for i in range(n):
+        if left[i] == 0:
+            ready.setdefault(ops[i]["eng"], []).append(i)
+    free = {}
+    order = []
+    fin = [0.0] * n
+    while len(order) < n:
+        best = None
+        for e, lst in ready.items():
+            if lst:
+                t0 = max(free.get(e, 0.0), min(rdy[i] for i in lst))
+                if best is None or t0 < best[0]:
+                    best = (t0, e)
+        t0, e = best
+        lst = ready[e]
+        i = max([k for k in lst if rdy[k] <= t0], key=lambda k: (bl[k], -k))
+        late = [k for k in lst if t0 < rdy[k] < t0 + LOOK * ops[i]["dur"] and bl[k] > bl[i] + ops[i]["dur"]]
+        if late:
+            i = min(late, key=lambda k: (rdy[k], -bl[k]))
+        lst.remove(i)
+        st = max(t0, rdy[i])
+        end = st + ops[i]["dur"]
+        if e != "X":
+            free[e] = end
+        fin[i] = end + ops[i]["lat"]
+        ops[i]["st"] = st
+        order.append(i)
+        for k in succ[i]:
+            rdy[k] = max(rdy[k], (fin[i] + HOP) if ops[k]["deps"][i] else end)
+            left[k] -= 1
+            if left[k] == 0:
+                ready.setdefault(ops[k]["eng"], []).append(k)
+    return order, max(fin)
+
+
+def place(ops, pred, succ, prio):
+    n = len(ops)
+    left = [len(p) for p in pred]
+    st = [0.0] * n
+    busy = {}
+    ready = sorted([(prio[i], i) for i in range(n) if left[i] == 0], reverse=True)
+    while ready:
+        i = ready.pop()[1]
+        d = ops[i]["dur"]
+        t = 0.0
+        for j, lag in pred[i]:
+            t = max(t, st[j] + ops[j]["dur"] + lag)
+        if d > 0:
+            iv = busy.setdefault(ops[i]["eng"], [])
+            lo, hi = 0, len(iv)
+            while lo < hi:
+                mid = (lo + hi) // 2
+                if iv[mid][1] <= t:
+                    lo = mid + 1
+                else:
+                    hi = mid
+            while lo < len(iv) and iv[lo][0] < t + d:
+                t = max(t, iv[lo][1])
+                lo += 1
+            iv.insert(lo, (t, t + d))
+        st[i] = t
+        for k, lag in succ[i]:
+            left[k] -= 1
+            if left[k] == 0:
+                e = (prio[k], k)
+                lo, hi = 0, len(ready)
+                while lo < hi:
+                    mid = (lo + hi) // 2
+                    if ready[mid] > e:
+                        lo = mid + 1
+                    else:
+                        hi = mid
+                ready.insert(lo, e)
+    return st
+
+
+def schedule(ops):
+    n = len(ops)
+    pred = [[(j, (HOP + ops[j]["lat"]) if w else 0.0) for j, w in o["deps"].items()] for o in ops]
+    succ = [[] for _ in range(n)]
+    for i in range(n):
+        for j, lag in pred[i]:
+            succ[j].append((i, lag))
+    bl = [0.0] * n
+    for i in range(n - 1, -1, -1):
+        bl[i] = ops[i]["dur"] + max([ops[i]["lat"]] + [bl[k] + lag for k, lag in succ[i]])
+    prio = [-bl[i] + 100.0 * (OFF.get(ops[i]["ty"], 0) + OFF.get(ops[i]["low"], 0)) for i in range(n)]
+    best = None
+    for it in range(PASSES):
+        st = place(ops, pred, succ, prio)
+        end = max(st[i] + ops[i]["dur"] + ops[i]["lat"] for i in range(n))
+        if best is None or end < best[0]:
+            best = (end, st)
+        if it == PASSES - 1:
+            break
+        back = place(ops, succ, pred, [-(st[i] + ops[i]["dur"] + ops[i]["lat"]) for i in range(n)])
+        prio = [-(back[i] + ops[i]["dur"]) for i in range(n)]
+    end, st = best
+    for i in range(n):
+        ops[i]["st"] = st[i]
+    return sorted(range(n), key=lambda i: (st[i], i)), end
+
+
+PASSES = 3
+OFF = {'B0': 16, 'B1': 15, 'B2': 15, 'ASgA': 10, 'BSgB': 10, 'ASq0': 6, 'AVbj': 3, 'rVsu': 58, 'BVnf': -117, 'wSYH': 28,
+       'iYxs': 45, 'APps2': -20, 'BVem': -36, 'BVes': -14, 'BVus': -26}
+
+
+def rank_program(g, core, T, topo):
+    rank = T.rank_of(core)
+    if rank is None:
+        return
+    ops = build(g, core, T, topo, rank)
+    order, _ = schedule(ops)
+    queue = {"V": g.vector, "S": g.scalar, "P": g.tensor, "G": g, "Y": g.sync}
+    pos = {i: k for k, i in enumerate(order)}
+    need = set()
+    for o in ops:
+        last = {}
+        for j, w in o["deps"].items():
+            if w and ops[j]["tok"] is None:
+                e = ops[j]["eng"]
+                if e not in last or pos[j] > pos[last[e]]:
+                    last[e] = j
+        o["last"] = list(last.values())
+        need.update(o["last"])
+    count = {}
+    seen = {}
+    total = {}
+    for i in order:
+        o = ops[i]
+        e = o["eng"]
+        if e == "X":
+            total[o["tok"][0]] = o["tok"][1]
+            continue
+        toks = [ops[j]["tok"] for j, w in o["deps"].items() if w and ops[j]["tok"] is not None and j not in o["last"]]
+        toks += [ops[j]["tok"] for j in o["last"]]
+        for s, v in toks:
+            if seen.get((e, s), 0) < v:
+                queue[e].wait_ge(T.sem[s], v)
+                seen[(e, s)] = v
+        ins = o["fn"]()
+        if o["tok"] is not None:
+            total[o["tok"][0]] = o["tok"][1]
+        elif i in need:
+            s = "c" + e
+            count[s] = count.get(s, 0) + 1
+            ins.then_inc(T.sem[s], 1)
+            o["tok"] = (s, count[s])
+            total[s] = count[s]
+    for s, v in total.items():
+        if seen.get(("G", s), 0) < v:
+            g.wait_ge(T.sem[s], v)

@@ -1,3 +1,4 @@
+import numpy as np
 from concourse.bass import DstId, RemoteDMATransfer
 from concourse.mybir import AluOpType as A, ActivationFunctionType as F
 
@@ -14,22 +15,24 @@ SB = {
     "x0": (256, b16), "x1": (256, b16), "x2": (256, b16), "x3": (256, b16), "q0": (256, b16), "q1": (256, b16),
     "xT": (256, b16), "gA": (2048, b16), "gB": (2048, b16), "mA": (2048, b16), "mB": (2048, b16),
     "bj": (32, i32), "bI": (32, i32), "bu": (16, u16), "hu": (256, u16), "hf": (256, f32),
-    "us": (272, f32), "nf": (272, f32), "es": (272, f32), "em": (256, f32), "su": (16, u16), "dd": (256, b16),
+    "us": (288, f32), "nf": (288, f32), "es": (288, f32), "em": (256, f32), "su": (16, u16), "dd": (256, b16),
     "W": (16, i32), "sA": (16, f32), "sB": (16, f32), "pA": (16, i32), "pB": (16, i32), "pC": (16, f32), "pD": (16, i32),
     "fj": (32, i32), "fk": (32, i32), "fy": (32, i32), "fx": (32, i32), "fu": (16, u16), "own": (16, i32),
     "oh": (64, b16), "le": (64, f32), "iq": (64, f32), "th": (64, f32), "ta": (32, f32), "tb": (16, f32), "thr": (64, f32),
     "xa": (256, b16), "ad": (256, b16), "pr": (256, f32), "we": (256, f32),
-    "t1": (16, f32), "t2": (16, f32), "vt": (16, f32), "e1": (16, f32), "e2": (16, f32), "e3": (16, f32), "isq": (16, f32),
+    "t1": (16, f32), "t2": (16, f32), "vt": (16, f32), "e1": (16, f32), "e2": (16, f32), "e3": (16, f32), "isq": (32, f32),
     "base": (16, f32), "bD": (16, f32), "ne": (16, f32), "dl": (16, f32), "kn": (16, f32), "k1": (16, f32), "key": (16, f32),
     "za": (16, i32), "zb": (16, i32), "zc": (16, f32), "zf": (16, f32),
     "EB": (256, f32), "EM": (256, f32), "ZB": (256, f32), "kO": (16, f32), "kR": (256, u16), "E": (4096, b16),
-    "K": (256, f32), "oS": (16, f32), "oU": (16, u16), "oa": (16, f32), "ob": (16, f32), "zm": (256, f32), "hm": (256, f32), "yn": (256, f32),
+    "K": (256, f32), "oS": (16, f32), "oU": (64, u16), "oa": (16, f32), "ob": (16, f32), "zm": (256, f32), "hm": (256, f32), "yn": (256, f32),
     "k4": (64, b16), "PAY": (4096, f32), "MET": (768, f32), "mu": (192, u16), "ca": (32, f32), "ci": (32, i32),
     "jm": (256, f32), "ja": (256, b16), "yv8": (1024, f32),
     "pi": (4, i32), "pc": (8, f32), "JJ": (272, f32), "EK": (272, f32), "NK": (272, f32), "NEG": (256, b16),
-    "vv": (136, f32), "v2": (136, f32), "If": (128, f32), "Ib": (384, b16), "cst": (384, b16), "GB": (16, f32), "Gb": (64, b16),
+    "vv": (136, f32), "v2": (136, f32), "If": (128, f32), "Ib": (384, b16), "cst": (384, b16), "GB": (24, f32), "Gb": (64, b16),
+    "v3": (144, f32), "DN": (144, f32), "DLN": (144, f32), "RC": (144, b16), "CR": (288, b16), "BF": (128, f32), "nIf": (128, f32),
+    "AF": (128, b16), "KA": (256, f32), "ch": (256, b16), "sn": (256, f32),
     "BD": (256, b16), "kw": (128, f32), "R": (2048, b16), "DM": (136, f32), "DLT": (136, f32), "RST": (256, f32),
-    "ls": (32, u16), "J": (48, f32), "dc": (64, f32), "DT": (32, f32), "Aw": (288, b16), "CA": (64, f32), "sT": (128, f32),
+    "ls": (64, u16), "J": (48, f32), "dc": (64, f32), "DT": (32, f32), "Aw": (288, b16), "CA": (64, f32), "sT": (128, f32),
 }
 SCRATCH, WHERE = {}, {}
 for _k, (_n, _d) in SB.items():
@@ -169,9 +172,9 @@ def build(g, core, T, topo, rank):
         q = g.sync if eng == "Y" else g.scalar
         lat = 2000 + nbytes / 150.0
         if load:
-            dclock[0] += nbytes / 150.0
+            dclock[0] += nbytes / 300.0
             lat = 2000 + dclock[0]
-            return add(eng, lambda: q.dma_start(o[0], i).then_inc(T.sem[s], 16), [o], [], 60, lat=lat, tok=(s, 16))
+            return chain(eng, add(eng, lambda: q.dma_start(o[0], i).then_inc(T.sem[s], 16), [o], [], 60, lat=lat, tok=(s, 16)))
         return add(eng, lambda: q.dma_start(o, i[0]).then_inc(T.sem[s], 16), [], [i], 60, lat=lat, tok=(s, 16))
 
     others = [c for c in T.cores if c != core]
@@ -253,6 +256,8 @@ def build(g, core, T, topo, rank):
     ts(BDB, ap("jm", 0, 128), pd, A.is_equal, BIGK, A.mult)
     ts(ap("kw"), ap("jm", 0, 128), pd, A.is_equal, ap("pc", 2, 3), A.mult)
     tt(LTB, BDB, ap("v2", 0, 128), A.mult)
+    if BSCAN:
+        ts(ap("AF"), ap("jm", 0, 128), pd, A.is_equal, ap("cf", 1, 2), A.mult)
     iota(ap("vv"), [[-16, 8], [-1, 17]], 0, 1)
     ts(ap("DM"), ap("vv"), -1.0, A.is_equal)
     ts(ap("v2"), ap("vv"), 0.0, A.is_equal)
@@ -288,6 +293,32 @@ def build(g, core, T, topo, rank):
     iota(DT2, [[128, 2], [0, 8]], 8192, 1)
     iota(ap("sT"), [[1, 128]], 0, -16)
     ts(ap("sT"), ap("sT"), 0.0, A.is_equal)
+    BG = 33554432.0
+    l18, KC, nGBf = ap("ls", 32, 40), ap("Gb", 48, 56), ap("GB", 16, 24)
+    ts(l18, ap("JJ", 0, 8), 18.0, A.mult, 17.0, A.add)
+    ts(KC, GBf, pm, A.mult)
+    nW1 = ap("Gb", 56, 64)
+    if AV:
+        ts(nW1, W1, -1.0, A.mult)
+    ts(nGBf, GBf, -1.0, A.mult)
+    ts(ap("nIf"), If, -1.0, A.mult)
+    ts(ap("BF"), BDB, 1.0 / BIGK, A.mult)
+    iota(ap("v3"), [[-16, 8], [-1, 18]], 0, 1)
+    ts(ap("DN"), ap("v3"), -1.0, A.is_equal)
+    ts(ap("v3"), ap("v3"), 0.0, A.is_equal)
+    ms(ap("v3", 16, 144, 18), 0.0)
+    ms(ap("v3", 17, 144, 18), 0.0)
+    ms(ap("DN", 17, 144, 18), 0.0)
+    tt(ap("DN"), ap("DN"), ap("v3"), A.subtract)
+    ts(ap("RC"), ap("v3"), BG, A.mult)
+    ts(ap("RC", 16, 144, 18), GBf, -BG, A.mult)
+    ms(ap("CR"), 0.0)
+    ms(ap("CR", 16, 144, 18), BG / 128)
+    ms(ap("CR", 161, 288, 18), 0.125)
+    ms(ap("DLN"), -1.0)
+    ms(ap("DLN", 0, 144, 18), BG)
+    ms(ap("DLN", 16, 144, 18), 15.0)
+    ms(ap("DLN", 17, 144, 18), 1.0)
     ms(ap("RST"), 0.0)
     ms(ap("RST", 0, 256, 16), -67108864.0)
     ms(ap("we"), 0.0)
@@ -306,7 +337,7 @@ def build(g, core, T, topo, rank):
         ts(ap("vf", 256 * j, 256 * j + 256, p1=8), ap("vi", 256 * j, 256 * j + 256, p1=8), -2047.5, A.add, 1.0 / FR, A.mult)
 
     def sums(j):
-        bk = 2 + j % 2
+        bk = j % 2
         for u in range(2):
             mm(P(bk, 256 * u, 256 * u + 256), ap("kw"), ap("SW", 512 * j + 256 * u, 512 * j + 256 * u + 256))
         act(ap("YH", 512 * j, 512 * j + 512), P(bk, 0, 512))
@@ -317,9 +348,6 @@ def build(g, core, T, topo, rank):
         for u in range(2):
             mm(P(bk, 256 * u, 256 * u + 256), ap("sT", p1=8), ap("vf", 512 * j + 256 * u, 512 * j + 256 * u + 256, p1=8), False, u == 1)
         act(ap("XW", H * rank + 512 * j, H * rank + 512 * j + 512), P(bk, 0, 512))
-
-    for j in range(6):
-        sums(j)
 
     xv, qv, rb = [0], [0], [0]
     for h in range(2):
@@ -333,14 +361,25 @@ def build(g, core, T, topo, rank):
         oc, tc = (0, 8) if h == 0 else (8, 0)
         mm(P(kb, 256, 384), ap(xo, lo, hi), Ib)
         act(ap("xT", lo, hi), P(kb, 256, 384))
-        for m in range(16):
-            mm(P(mb, oc, oc + 8), ap("Aw", 15 - m, 143 - m), ap(qo, lo + m, hi, 16), m == 0, m == 15)
         a0, a1 = (oc, oc + 8)
-        if last:
-            mm(P(mb, tc, tc + 8), ap(qo, lo, hi), ablk)
-            a0, a1 = 0, 16
-        b0, b1 = 16 * h + a0, 16 * h + a1
-        tt(ap("bj", b0, b1), P(mb, a0, a1), ap("CA", b0, b1), A.subtract)
+        if BSCAN:
+            mm(P(mb, 128, 256), Ib, ap("NEG", 0, 128), True, False)
+            mm(P(mb, 128, 256), ap("AF"), ap(qo, lo, hi), False, True)
+            scan(ap("KA", lo, hi), ap("RST", 0, 128), P(mb, 128, 256), A.add, A.max)
+            tt(ap("bj", 24 * h, 24 * h + 8), ap("KA", lo + 15, hi, 16), ap("CA", 24 * h, 24 * h + 8), A.subtract)
+            if last:
+                mm(P(mb, tc, tc + 8), ap(qo, lo, hi), ablk)
+                tt(ap("bj", 8 + 8 * h, 16 + 8 * h), P(mb, tc, tc + 8), ap("CA", 8 + 8 * h, 16 + 8 * h), A.subtract)
+                ts(ap("bI", 8 + 8 * h, 16 + 8 * h), ap("bj", 8 + 8 * h, 16 + 8 * h), 4095, A.bitwise_and)
+            b0, b1 = 16 * h + a0, 16 * h + a1
+        else:
+            for m in range(16):
+                mm(P(mb, oc, oc + 8), ap("Aw", 15 - m, 143 - m), ap(qo, lo + m, hi, 16), m == 0, m == 15)
+            if last:
+                mm(P(mb, tc, tc + 8), ap(qo, lo, hi), ablk)
+                a0, a1 = 0, 16
+            b0, b1 = 16 * h + a0, 16 * h + a1
+            tt(ap("bj", b0, b1), P(mb, a0, a1), ap("CA", b0, b1), A.subtract)
         ts(ap("bI", b0, b1), ap("bj", b0, b1), 4095, A.bitwise_and)
         bu = ap("bu", 8 * h, 8 * h + 8)
         cp(bu, ap("bI", 24 * h, 24 * h + 8))
@@ -348,12 +387,14 @@ def build(g, core, T, topo, rank):
         act(ap("hf", lo, hi), ind(ap("SW", 0, 4096), bu), bias=16.0)
         if not late:
             mm(P(mb, 272, 408), ap("hf", lo, hi), ap("DM"))
-        for j in range(4):
+        c0 = 0
+        for j, cw in enumerate(CHUNKS):
             bk = 6 * h + j % 2
-            mm(P(bk, 0, 512), ap("xT", lo, hi), ap("R", 512 * j, 512 * j + 512))
-            gj = ap(gn, 512 * j, 512 * j + 512)
-            chain("g", act(gj, ind(ap("Gz", 16, 4112), ap("hu", lo + 32 * j, lo + 32 * j + 32))))
-            chain("m", tt(ap(mn, 512 * j, 512 * j + 512), gj, P(bk, 0, 512), A.min))
+            mm(P(bk, 0, cw), ap("xT", lo, hi), ap("R", c0, c0 + cw))
+            gj = ap(gn, c0, c0 + cw)
+            chain("g", act(gj, ind(ap("Gz", 16, 4112), ap("hu", lo + c0 // 16, lo + (c0 + cw) // 16))))
+            chain("m", tt(ap(mn, c0, c0 + cw), gj, P(bk, 0, cw), A.min))
+            c0 += cw
         mm(P(kb, 0, 136), zeros, ap("R", 0, 136), True, False)
         for k in range(16):
             mm(P(kb, k, 136, 17), ap(gn, k, 2048, 16), W1, False, False)
@@ -369,6 +410,77 @@ def build(g, core, T, topo, rank):
         cp(su, P(mb, 256, 264))
         tt(ap("dd", lo, hi), ind(ap("Gz"), su), ap(xo, lo, hi), A.subtract)
         act(ap(xn, lo, hi), ap("dd", lo, hi), F.Abs)
+        if QV:
+            ts(ap(qn, lo, hi), ap(xn, lo, hi), 0.25, A.mult, 191.625, A.add)
+        else:
+            act(ap(qn, lo, hi), ap(xn, lo, hi), scale=0.25, bias=191.625)
+
+    def ahead(h, xo, qo):
+        lo, hi = 128 * h, 128 * h + 128
+        mb = 4 + h
+        gn, mn = "gA" if h == 0 else "gB", "mA" if h == 0 else "mB"
+        mm(P(mb, 384, 512), ap(xo, lo, hi), Ib)
+        act(ap("xT", lo, hi), P(mb, 384, 512))
+        for m in range(16):
+            mm(P(mb, 0, 8), ap("Aw", 15 - m, 143 - m), ap(qo, lo + m, hi, 16), m == 0, m == 15)
+        b0 = 24 * h
+        tt(ap("bj", b0, b0 + 8), P(mb, 0, 8), ap("CA", b0, b0 + 8), A.subtract)
+        ts(ap("bI", b0, b0 + 8), ap("bj", b0, b0 + 8), 4095, A.bitwise_and)
+        bu = ap("bu", 8 * h, 8 * h + 8)
+        cp(bu, ap("bI", b0, b0 + 8))
+        cp(ap("hu", lo, hi), ind(ap("SW", 0, 4096), bu))
+        act(ap("hf", lo, hi), ind(ap("SW", 0, 4096), bu))
+        mm(P(mb, 0, 288), ones, ap("CR"), True, False)
+        mm(P(mb, 144, 288), ap("hf", lo, hi), ap("DN"), False, False)
+        cw = AHEAD
+        if h in AV:
+            mm(P(mb, 16, 144, 18), ap(xo, lo, hi), nW1, False, False)
+        else:
+            mm(P(mb, 17, 144, 18), ap(xo, lo, hi), W1, False, False)
+        for j in range(2048 // cw):
+            bk = j % 2
+            gj = ap(gn, cw * j, cw * j + cw)
+            chain("g", act(gj, ind(ap("Gz", 16, 4112), ap("hu", lo + cw // 16 * j, lo + cw // 16 * (j + 1)))))
+            mm(P(bk, 0, cw), ap("xT", lo, hi), ap("R", cw * j, cw * j + cw), True, h in AV)
+            if h in AV:
+                tt(ap(mn, cw * j, cw * j + cw), gj, P(bk, 0, cw), A.min)
+            else:
+                mm(P(bk, 0, cw), nIb, gj, False, True)
+                act(ap(mn, cw * j, cw * j + cw), P(bk, 0, cw), F.Abs)
+        if h in AV:
+            for k in range(16):
+                mm(P(mb, k, 144, 18), ap(gn, k, 2048, 16), W1, False, False)
+        for k in range(16):
+            mm(P(mb, k, 144, 18), ap(mn, k, 2048, 16), W2 if h in AV else W1, False, False)
+
+    def amend(h, xo, xn, qn):
+        lo, hi = 128 * h, 128 * h + 128
+        mb = 4 + h
+        bu = ap("bu", 8 * h, 8 * h + 8)
+        ch, sn = ap("ch", lo, hi), ap("sn", lo, hi)
+        tt(ch, ind(ap("SW", 0, 4096), bu), ap("hf", lo, hi), A.not_equal)
+        tt(sn, ind(ap("SW", 0, 4096), bu), ch, A.mult)
+        mm(P(2 + h, 0, 128), Ib, ap("NEG", 0, 128), True, False)
+        mm(P(2 + h, 0, 128), ap("BF"), sn, False, True)
+        scan(ap("KA", lo, hi), ap("RST", 0, 128), P(2 + h, 0, 128), A.add, A.max)
+        su = ap("su", 8 * h, 8 * h + 8)
+        cp(su, ap("KA", lo + 15, hi, 16))
+        tt(ap("dd", lo, hi), ind(ap("Gz", 16, 4112), su), ap(xo, lo, hi), A.subtract)
+        act(ap("ja", lo, hi), ap("dd", lo, hi), F.Abs)
+        mm(P(mb, 0, 144), ch, ap("RC"), False, False)
+        mm(P(mb, 16, 144, 18), ch, KC, False, False)
+        mm(P(mb, 160, 288, 18), sn, nGBf, False, False)
+        mm(P(mb, 161, 288, 18), sn, GBf, False, False)
+        mm(P(mb, 16, 144, 18), ap("ja", lo, hi), W1, False, True)
+        s0, s1 = 144 * h, 144 * h + 144
+        scan(ap("us", s0, s1), ap("DLN"), P(mb, 0, 144), A.add, A.min)
+        tt(ap("nf", s0, s1), ap("us", s0, s1), P(mb, 0, 144), A.not_equal)
+        scan(ap("es", s0, s1), P(mb, 144, 288), ap("nf", s0, s1), A.add, A.mult)
+        tt(ap("em", lo, hi), ind(ap("es", s0, s1), l18), ap("EK", 0, 128), A.mult)
+        mm(P(mb, 256, 264), ap("em", lo, hi), GBf)
+        cp(su, P(mb, 256, 264))
+        tt(ap("dd", lo, hi), ind(ap("Gz"), su), ap(xo, lo, hi), A.subtract)
+        act(ap(xn, lo, hi), ap("dd", lo, hi), F.Abs)
         act(ap(qn, lo, hi), ap(xn, lo, hi), scale=0.25, bias=191.625)
 
     def nextx():
@@ -381,18 +493,20 @@ def build(g, core, T, topo, rank):
         fin = t == TR - 1
         for s in range(ST):
             xo, xn, qo, qn = nextx()
+            early = AHEAD and t > 0 and s == 0
             for h in range(2):
                 low[0] = "AB"[h] + str(s)
-                step_half(h, s == ST - 1, xo, xn, qo, qn)
+                if early:
+                    low[0] = "CD"[h]
+                    amend(h, xo, xn, qn)
+                else:
+                    step_half(h, s == ST - 1, xo, xn, qo, qn)
             low[0] = "w%d" % s
             if t == 0 and s == 0:
                 store(0)
                 store(1)
                 share("XW", 0, H, 524e3)
-            if t == 0 and s == 1:
-                sums(6)
-                sums(7)
-            e = ap("es", 16, 272, 17)
+            e = ap("es", 17, 288, 18) if early else ap("es", 16, 272, 17)
             act(ap("sA"), e, F.Relu, bias=-16.0)
             act(ap("sB"), e, F.Relu, bias=-592.0, scale=37.0)
             tt(ap("pA"), W, ap("sA"), A.mult)
@@ -402,8 +516,12 @@ def build(g, core, T, topo, rank):
             ts(W, ap("pD"), 4095, A.bitwise_and)
         xo, xn, qo, qn = nextx()
         x = ap(xo)
+        if fin:
+            low[0] = "y"
+            for j in range(8):
+                sums(j)
         low[0] = "r"
-        tt(ap("hm"), ind(ap("SW", 0, 4096), ap("bu")), ap("NK", t, t + 256), A.mult)
+        act(ap("hm"), ind(ap("SW", 0, 4096), ap("bu")))
         for m in range(16):
             mm(P(2, 0, 16), ap("Aw", 159 - m, 287 - m), ap(qo, m, 256, 16), m == 0, m == 15)
         for h in range(2):
@@ -434,6 +552,7 @@ def build(g, core, T, topo, rank):
             mm(P(7, 128 * h, 128 * h + 128), ap("we", 128 * h, 128 * h + 128), If, False, h == 1)
         act(ap("PAY", 1024 * t + 256 * rank, 1024 * t + 256 * rank + 256), P(7, 0, 256))
         share("PAY", 1024 * t, 256, 131e3)
+        low[0] = "J"
         tt(ap("jm"), ind(W, lc), ap("EK", 0, 256), A.mult)
         for h in range(2):
             lo, hi = 128 * h, 128 * h + 128
@@ -445,20 +564,27 @@ def build(g, core, T, topo, rank):
             act(ap(xn, lo, hi), ap("ja", lo, hi), scale=-1.0, bias=63.0)
             if not fin:
                 act(ap(qn, lo, hi), ap("ja", lo, hi), scale=-0.25, bias=207.375)
+        if AHEAD and not fin:
+            for h in range(2):
+                low[0] = "EF"[h]
+                ahead(h, xn, qn)
+        low[0] = "r"
+        mm(P(2, 0, 16), ap("nIf"), ap("we", 0, 256, 16), True, False)
         for h in range(2):
-            mm(P(2, 8 * h, 8 * h + 8), ap("pr", 128 * h, 128 * h + 128), S0f)
+            mm(P(2, 8 * h, 8 * h + 8), ap("pr", 128 * h, 128 * h + 128), S0f, False, h == 1)
         ts(ap("t1"), P(2, 0, 16), MAGIC, A.add, MAGIC, A.subtract)
+        tt(ap("ne"), P(2, 0, 16), ap("t1"), A.not_equal)
         tt(ap("t2"), P(2, 0, 16), ap("t1"), A.subtract)
         vt = ap("vt")
-        ts(vt, ap("t2"), FR, A.mult, 2047.5, A.add)
+        act(ap("isq", 16, 32), ap("t2"), scale=FR)
+        tt(vt, ap("isq", 16, 32), W, A.add)
         for h in range(2):
             mm(P(3, 256 + 8 * h, 264 + 8 * h), ap("ad", 128 * h, 128 * h + 128), GBb)
         tt(ap("e1"), idx, DT2, A.subtract)
-        ts(ap("isq"), ap("tb"), 0.25, A.is_gt)
-        tt(ap("e2"), ap("isq"), ap("e1"), A.mult)
+        ts(ap("isq", 0, 16), ap("tb"), 0.25, A.is_gt)
+        tt(ap("e2"), ap("isq", 0, 16), ap("e1"), A.mult)
         tt(ap("base"), ap("e2"), DT, A.add)
         tt(ap("bD"), ap("bI", 8, 24), DT, A.subtract)
-        tt(ap("ne"), vt, W, A.not_equal)
         tt(ap("e3"), ap("ne"), ap("bD"), A.mult)
         tt(ap("dl"), ap("e3"), ap("e1"), A.subtract)
         tt(ap("kn"), P(3, 256, 272), ap("tb"), A.is_lt)
@@ -483,8 +609,9 @@ def build(g, core, T, topo, rank):
         mm(P(3, 0, 256), Ib, ap("NEG"), True, False)
         for h in range(2):
             mm(P(3, 128 * h, 128 * h + 128), ap("EB", 128 * h, 128 * h + 128), If, False, False)
+        mm(P(7, 0, 256), ap("nIf"), ap("hm"), True, False)
         for h in range(2):
-            mm(P(7, 128 * h, 128 * h + 128), ap("ZB", 128 * h, 128 * h + 128), If)
+            mm(P(7, 128 * h, 128 * h + 128), ap("ZB", 128 * h, 128 * h + 128), If, False, h == 1)
         for c in range(16):
             ts(ap("E", 256 * c + 16 * c, 256 * c + 256), ap("kR", 16 * c, 256), ap("kO", c, c + 1), A.is_equal)
             mm(P(3, 16 * c, 16 * c + 16), LTB, ap("E", 272 * c, 272 * c + 16), False, c == 15)
@@ -494,9 +621,10 @@ def build(g, core, T, topo, rank):
         scan(ap("K"), ap("RST"), P(3, 0, 256), A.add, A.max)
         Kd = ap("K", 15, 256, 16)
         tt(ap("oS"), Kd, dumO, A.min)
-        cp(ap("oU"), ap("oS"))
+        oU = ap("oU", 16 * t, 16 * t + 16)
+        cp(oU, ap("oS"))
         if not fin:
-            tt(ind(ap("SW"), ap("oU")), ap("zm"), ap("hm"), A.add)
+            tt(ind(ap("SW"), oU), ap("zm"), ap("hm"), A.add)
         mw = 16 if fin else 48
         mb = 192 * t + mw * rank
         ts(ap("oa"), Kd, 8192.0, A.is_lt, BIGK, A.mult)
@@ -508,13 +636,17 @@ def build(g, core, T, topo, rank):
             mm(P(6, 0, 32), ones, ap("k4", 32, 64), False, True)
             act(ap("MET", mb + 16, mb + 48), P(6, 0, 32))
         share("MET", 192 * t, mw, 512 * mw)
-        mm(P(7, 0, 256), ap("kw"), ap("zm"), True, False)
-        mm(P(7, 0, 256), ap("kw"), ap("hm"), False, True)
-        act(ap("yn"), P(7, 0, 256))
-        cp(ind(ap("YH"), ap("oU")), ap("yn"))
+        if fin:
+            mm(P(7, 0, 256), ap("kw"), ap("hm"), True, False)
+            mm(P(7, 0, 256), ap("kw"), ap("zm"), False, True)
+            act(ap("yn"), P(7, 0, 256))
+            cp(ind(ap("YH"), oU), ap("yn"))
         ts(ap("mu", 0, 4 * mw), ap("MET", 192 * t, 192 * t + 4 * mw), 8192.0, A.subtract)
         for a in range(N - 1, -1, -1):
-            cp(ind(ap("XW"), ap("mu", mw * a, mw * a + 16)), ap("PAY", 1024 * t + 256 * a, 1024 * t + 256 * a + 256))
+            w = 16 if fin else 16 // PIECES
+            for u in range(0, 16, w):
+                p0 = 1024 * t + 256 * a + 16 * u
+                cp(ind(ap("XW"), ap("mu", mw * a + u, mw * a + u + w)), ap("PAY", p0, p0 + 16 * w))
         if not fin:
             c = [ap("MET", 192 * t + 48 * a + 16, 192 * t + 48 * a + 48) for a in range(N)]
             tt(ap("ca"), c[0], c[1], A.add)
@@ -655,14 +787,38 @@ def schedule(ops):
         back = place(ops, succ, pred, [-(st[i] + ops[i]["dur"] + ops[i]["lat"]) for i in range(n)])
         prio = [-(back[i] + ops[i]["dur"]) for i in range(n)]
     end, st = best
+    if n in DONE:
+        st = place(ops, pred, succ, DONE[n])
+    else:
+        rng = np.random.RandomState(SEED)
+        for it in range(POLISH):
+            a, w, sg = rng.rand() * end, (2000, 4000, 8000)[rng.randint(3)], (150, 400, 1000)[rng.randint(3)]
+            z = rng.randn(n).tolist()
+            s2 = place(ops, pred, succ, [s + sg * z[i] if a < s < a + w and ops[i]["eng"] != "P" else s for i, s in enumerate(st)])
+            e2 = max(s2[i] + ops[i]["dur"] + ops[i]["lat"] for i in range(n))
+            if e2 <= end:
+                end, st = e2, s2
+        if POLISH:
+            DONE[n] = st
     for i in range(n):
         ops[i]["st"] = st[i]
     return sorted(range(n), key=lambda i: (st[i], i)), end
 
 
+PIECES = 4
+AHEAD = 512
 PASSES = 3
-OFF = {'B0': 16, 'B1': 15, 'B2': 15, 'ASgA': 10, 'BSgB': 10, 'ASq0': 6, 'AVbj': 3, 'rVsu': 58, 'BVnf': -117, 'wSYH': 28,
-       'iYxs': 45, 'APps2': -20, 'BVem': -36, 'BVes': -14, 'BVus': -26}
+OFF = {'B0':17,'B1':15,'B2':15,'ASgA':-53,'BSgB':12,'ASq0':10,'AVbj':8,'wSYH':26,'BVus':-233,'D':-26,'rVvt':2,'BPps2':12,'AVmA':4,'AVus':-128,'rVfk':-141,'C':-141,'BPps0':-9,'FSmB':37,'rVzc':22,'EShf':48,'rVow':-83,'JSx0':-80,'JVsu':23,'APps1':-157,'EPps0':-114,'FShf':-128,'rSyv':193,'rPps4':6,'BPps1':-1,'ESmA':33,'rVSW':-385,'ASq1':65,'rPps0':5,'rVkR':68,'APps2':-159,'rVwe':-124,'rVoS':48,'DVdd':49,'w0':-6,'FVbj':105,'iVNK':32,'wVpA':-50,'FPps0':11,'AVhu':20,'BSq1':-9,'EVbj':56,'BSx2':-185,'rVYH':121,'BVdd':-57,'A0':-110,'iVIf':48,'iVwe':-194,'AShf':-12,'rVe1':15,'ESxT':45,'rVfu':-65,'AVdd':-3,'BShf':-16,'iVkw':122,'iSYH':65,'rVza':42,'rVne':1,'BSq0':-29,'rVtb':1,'rVe2':-27,'r':1}
+OFF = {'B0':32,'B1':13,'B2':15,'ASgA':-53,'BSgB':14,'ASq0':11,'AVbj':26,'D':-28,'rVvt':2,'BPps2':-52,'AVmA':4,'rVfk':-90,'C':-150,'BPps0':-9,'rVzc':29,'rVow':-9,'APps1':-145,'FShf':-96,'rSyv':178,'rPps4':9,'BPps1':-1,'ESmA':73,'rVSW':-416,'rVkR':77,'DVdd':51,'w0':-23,'FVbj':146,'FPps0':-85,'BSq1':-11,'BSx2':-130,'BVdd':-162,'A0':-293,'iVIf':45,'ESxT':149,'BShf':-38,'rVza':33,'rVne':1,'BSq0':-51,'rVtb':1,'r':-9,'wSsB':18,'wVW':38,'iVR':-16,'BVem':-25,'rVta':2,'rPps2':44,'yPps0':21,'rSkO':85,'w2':-38,'BVhu':-54,'AVes':5,'BVes':-14,'rVzm':86,'w1':-48,'BVsu':-9,'y':16,'J':25,'rVt2':3,'BVmB':8,'JVjm':122,'CPps0':-18,'BVnf':-88}
+OFF = {'B0':32,'B1':16,'B2':15,'ASgA':-161,'BSgB':16,'ASq0':6,'AVbj':25,'D':-24,'rVvt':1,'BPps2':-76,'AVmA':3,'rVfk':-16,'C':-103,'BPps0':-12,'rVzc':15,'rVow':-20,'rSyv':197,'rPps4':8,'BPps1':-69,'ESmA':157,'rVSW':-75,'rVkR':85,'DVdd':51,'w0':-13,'FVbj':253,'FPps0':-41,'BSq1':-173,'BSx2':-240,'BVdd':-129,'ESxT':86,'BSq0':-121,'r':18,'BVem':-7,'rVta':1,'rPps2':64,'yPps0':93,'rSkO':99,'BVhu':-20,'BVes':-91,'w1':-162,'BVsu':-340,'y':-13,'J':25,'rVt2':2,'BVmB':6,'JVjm':125,'CPps0':-226,'BVnf':-37,'rVwe':120,'iVwe':-77,'CVes':77,'iVDL':-98,'rVmu':-95,'iGsT':-130,'rXME':49,'iVGb':36,'iVRC':-69,'i':3,'FSmB':-44,'wVpC':59,'FSgB':-17,'A1':3,'iVnI':-216,'AVdd':7,'wVpB':50,'rVe1':33,'rVdl':-16,'APps0':1,'rVe3':10,'FPps18':27,'rVe2':-89,'BSx1':-124}
+OFF = {'B0':32,'B1':16,'B2':12,'BSgB':11,'ASq0':5,'AVbj':33,'D':-27,'rVvt':63,'BPps2':-121,'AVmA':4,'C':-104,'BPps0':-17,'rVzc':42,'rVow':-156,'rSyv':382,'BPps1':-75,'ESmA':210,'rVSW':-136,'rVkR':119,'DVdd':56,'w0':-9,'FVbj':268,'FPps0':-245,'BSq1':-172,'BSx2':-409,'BVdd':-196,'ESxT':138,'BSq0':-160,'r':16,'BVem':-79,'rVta':75,'yPps0':95,'BVhu':-58,'BVes':-119,'w1':-64,'BVsu':-249,'J':11,'BVmB':4,'JVjm':25,'CPps0':-398,'BVnf':-230,'rVwe':57,'CVes':83,'rXME':38,'iVGb':39,'FSmB':-227,'FSgB':-14,'A1':3,'AVdd':5,'wVpB':21,'rVe1':73,'rVdl':-37,'APps0':-1,'rVe3':71,'rVe2':-88,'BSx1':-42,'rVzm':88,'rVfy':4,'AShf':-52,'A0':-354,'FPps2':32,'BSx3':86,'BSxT':11,'AVnf':-286,'FShf':-116,'BVbI':-75,'CVch':-161,'rVbD':14,'rVzb':47,'E':-46,'iVIb':44,'iVpi':96,'rVfj':85,'JVdd':48,'wSsB':21,'iGvv':-65,'rVth':33,'rPps0':20,'APps1':-238,'BVus':-52,'wVpD':44,'iGR':-167,'iVCR':167,'EVbI':145,'EShf':-218,'BVbu':-12,'rVne':48,'A2':-5,'APps2':-17}
+DONE = {}
+SEED = 1
+POLISH = 3000
+AV = ()
+QV = 0
+BSCAN = 0
+CHUNKS = (512, 512, 512, 512)
 
 
 def rank_program(g, core, T, topo):

@@ -5,50 +5,66 @@ from concourse.mybir import AluOpType as A, ActivationFunctionType as F
 N, Q, H, L, CAP, TR, ST = 4, 4096, 1024, 256, 64, 4, 3
 MAGIC = 12582912.0
 BIGK = 32768.0
-FR = 16384.0
+UP = 32.0
+BG = 33554432.0
+FLO = 191.5 + 2.0 ** -13
+TOP = 4096.0 * 192
+CS = 16384.0
 f32, b16, i32, u16 = "float32", "bfloat16", "int32", "uint16"
 
 SB = {
-    "Gz": (4112, b16), "hi": (4096, i32), "SW": (4352, f32), "YH": (4352, f32), "XW": (4352, f32),
-    "xs": (1024, b16), "vi": (1024, i32), "vf": (1024, f32), "wi": (256, i32), "wf": (256, f32),
-    "cb": (16, b16), "cf": (8, f32),
-    "x0": (256, b16), "x1": (256, b16), "x2": (256, b16), "x3": (256, b16), "q0": (256, b16), "q1": (256, b16),
+    "Gz": (4112, b16), "hi": (4096, i32), "SW": (4352, f32), "YH": (4352, f32), "XW": (4352, f32), "SG": (4096, f32),
+    "xs": (1024, b16), "vi": (128, i32), "vd": (128, i32), "vb": (128, b16), "vf": (1024, b16), "wd": (32, i32),
+    "S2": (16, f32), "r1": (128, f32), "r2": (128, f32), "rd": (128, b16), "wi": (256, i32), "wf": (256, f32),
+    "cb": (16, b16), "cf": (8, f32), "cj": (8, i32),
+    "x0": (256, b16), "x1": (256, b16), "x2": (256, b16), "x3": (256, b16), "q0": (256, b16), "q1": (256, b16), "q2": (256, b16),
     "xT": (256, b16), "gA": (2048, b16), "gB": (2048, b16), "mA": (2048, b16), "mB": (2048, b16),
-    "bj": (32, i32), "bI": (32, i32), "bu": (16, u16), "hu": (256, u16), "hf": (256, f32),
+    "rr": (32, b16), "rf": (32, b16), "cm": (8, f32), "pf": (32, f32), "rw": (512, b16), "EM": (256, f32), "bj": (32, i32), "bI": (32, i32), "bu": (16, u16),
+    "hu": (256, u16), "hf": (256, f32), "hl": (256, f32),
     "us": (288, f32), "nf": (288, f32), "es": (288, f32), "em": (256, f32), "su": (16, u16), "dd": (256, b16),
-    "W": (16, i32), "sA": (16, f32), "sB": (16, f32), "pA": (16, i32), "pB": (16, i32), "pC": (16, f32), "pD": (16, i32),
-    "fj": (32, i32), "fk": (32, i32), "fy": (32, i32), "fx": (32, i32), "fu": (16, u16), "own": (16, i32),
-    "oh": (64, b16), "le": (64, f32), "iq": (64, f32), "th": (64, f32), "ta": (32, f32), "tb": (16, f32), "thr": (64, f32),
-    "xa": (256, b16), "ad": (256, b16), "pr": (256, f32), "we": (256, f32),
-    "t1": (16, f32), "t2": (16, f32), "vt": (16, f32), "e1": (16, f32), "e2": (16, f32), "e3": (16, f32), "isq": (32, f32),
-    "base": (16, f32), "bD": (16, f32), "ne": (16, f32), "dl": (16, f32), "kn": (16, f32), "k1": (16, f32), "key": (16, f32),
-    "za": (16, i32), "zb": (16, i32), "zc": (16, f32), "zf": (16, f32),
-    "EB": (256, f32), "EM": (256, f32), "ZB": (256, f32), "kO": (16, f32), "kR": (256, u16), "E": (4096, b16),
-    "K": (256, f32), "oS": (16, f32), "oU": (64, u16), "oa": (16, f32), "ob": (16, f32), "zm": (256, f32), "hm": (256, f32), "yn": (256, f32),
-    "k4": (64, b16), "PAY": (4096, f32), "MET": (768, f32), "mu": (192, u16), "ca": (32, f32), "ci": (32, i32),
+    "W": (16, i32), "sA": (16, f32), "sB": (16, f32), "pA": (16, f32), "pC": (16, f32), "pD": (16, i32),
+    "fu": (16, u16), "r4": (64, b16), "oh": (64, b16), "iq": (64, b16), "th": (64, b16), "thr": (64, i32), "ci": (64, i32),
+    "xa": (256, f32), "ad": (256, b16), "we": (256, b16),
+    "ne": (32, b16), "D1": (48, f32), "key": (48, f32), "wz": (48, f32),
+    "za": (16, f32), "zi": (16, i32), "zb": (16, i32), "zf": (16, f32),
+    "EB": (256, f32), "ZB": (256, f32), "KO": (256, f32), "kR": (256, u16), "E": (4096, b16),
+    "K": (256, f32), "oS": (16, f32), "oU": (64, u16), "ab": (16, f32), "zm": (256, f32), "yn": (256, f32),
+    "k4": (64, b16), "PAY": (4096, f32), "MET": (1280, f32), "mu": (64, u16),
     "jm": (256, f32), "ja": (256, b16), "yv8": (1024, f32),
-    "pi": (4, i32), "pc": (8, f32), "JJ": (272, f32), "EK": (272, f32), "NK": (272, f32), "NEG": (256, b16),
-    "vv": (136, f32), "v2": (136, f32), "If": (128, f32), "Ib": (384, b16), "cst": (384, b16), "GB": (24, f32), "Gb": (64, b16),
+    "pi": (4, i32), "pc": (8, f32), "JJ": (272, f32), "EK": (272, f32), "NEG": (256, b16),
+    "vv": (136, f32), "v2": (136, f32), "If": (128, f32), "Ib": (1024, b16), "cst": (512, b16),
+    "GB": (24, f32), "Gb": (64, b16), "c4": (96, b16),
     "v3": (144, f32), "DN": (144, f32), "DLN": (144, f32), "RC": (144, b16), "CR": (288, b16), "BF": (128, f32), "nIf": (128, f32),
-    "AF": (128, b16), "KA": (256, f32), "ch": (256, b16), "sn": (256, f32),
+    "AF": (256, b16), "KA": (256, f32), "ch": (256, b16), "sn": (256, f32), "C16": (136, b16), "CD": (48, b16), "CAT": (48, f32),
     "BD": (256, b16), "kw": (128, f32), "R": (2048, b16), "DM": (136, f32), "DLT": (136, f32), "RST": (256, f32),
-    "ls": (64, u16), "J": (48, f32), "dc": (64, f32), "DT": (32, f32), "Aw": (288, b16), "CA": (64, f32), "sT": (128, f32),
+    "ls": (64, u16), "J": (32, f32), "dc": (64, f32), "Aw": (288, b16), "sT": (128, b16), "sU": (256, f32), "j8": (128, f32), "j4": (32, f32),
 }
+CUBE = {"iq": 32, "th": 32, "MET": 80, "E": 256}
 SCRATCH, WHERE = {}, {}
 for _k, (_n, _d) in SB.items():
-    if _n <= 64:
+    if _k in CUBE:
+        SCRATCH[_k] = ("sbuf", [128, _n // CUBE[_k], CUBE[_k]], _d)
+    elif _n <= 64:
         _at = SCRATCH.get("pool_" + _d, ("sbuf", [128, 0], _d))[1][1]
         WHERE[_k] = ("pool_" + _d, _at)
         SCRATCH["pool_" + _d] = ("sbuf", [128, _at + (_n + 31) // 32 * 32], _d)
     else:
         WHERE[_k] = (_k, 0)
         SCRATCH[_k] = ("sbuf", [128, _n], _d)
-for _b in range(8):
-    SCRATCH["ps%d" % _b] = ("psum", [128, 512], f32)
+for _b in range(4):
+    SCRATCH["pp%d" % _b] = ("psum", [128, 1024], f32)
 NDMA = 40
 SEMAPHORES = ["cV", "cS", "cP", "cG"] + ["d%d" % _i for _i in range(NDMA)] + ["ar%d" % _i for _i in range(9)]
 
-HOP = 90.0
+HOP = 55.0
+OPT = dict(
+    mod="I", moda="I", modr="I", rnd="V", ko="V",
+    byv=((), (), (), ()), cut=((0, 128),),
+    step=("VVVV",) * 4,
+    ahead=("SSSS", "SSSS"),
+    gch=((0,), (1,), (2,), (3,)), vch=((0,), (1,), (2,), (3,)), ach=((0,), (1,), (2,), (3,)),
+    ecut=(3, 6, 10, 14, 16), xw="SSSS", ys8="VVVS", raw=1, ys=(0, 0, 8), dd="VVVV", xa="V", drow=50, dbw=450.0, scan=1.6, wc=15, vf=30, sf=40, pe=0.4, pl=100.0, gt=1.15, gc=1.25, pp=10, first=4000, schain=1, paylate=0, ser=0, pieces=2, splitw=1, eb="SS", zb="S", d1="V", ebh=1, lay="GGSS", sg="S", hch=(2048, 2048),
+)
 
 
 def build(g, core, T, topo, rank):
@@ -59,13 +75,30 @@ def build(g, core, T, topo, rank):
     low = ["i"]
 
     def ap(name, lo=0, hi=None, step=1, p0=0, p1=128, ps=1):
-        tn, at = WHERE.get(name, (name, 0))
-        t = T[tn]
         if hi is None:
             hi = SB[name][0]
         rows = slice(p0, p1, ps) if ps != 1 else slice(p0, p1)
+        if name in CUBE:
+            w = CUBE[name]
+            if lo // w == (hi - 1) // w:
+                a = T[name][rows, lo // w, lo % w:lo % w + hi - lo]
+            else:
+                a = T[name][rows, lo // w:hi // w, 0:w]
+            return (a, [(name, lo, hi)], hi - lo, "")
+        tn, at = WHERE[name]
+        t = T[tn]
         a = t[rows, at + lo:at + hi:step] if step != 1 else t[rows, at + lo:at + hi]
         return (a, [(name, lo, hi)], len(range(lo, hi, step)), "")
+
+    def cube(name, r0, r1, lo, hi):
+        w = CUBE[name]
+        return (T[name][0:128, r0:r1, lo:hi], [(name, r * w + lo, r * w + hi) for r in range(r0, r1)], (r1 - r0) * (hi - lo), "")
+
+    def P(b, lo, hi, step=1, p0=0, p1=128):
+        at = 512 * (b % 2)
+        t = T["pp%d" % (b // 2)]
+        a = t[p0:p1, at + lo:at + hi:step] if step != 1 else t[p0:p1, at + lo:at + hi]
+        return (a, [("ps%d" % (b + j), 0, 512) for j in range((hi + 511) // 512)], len(range(lo, hi, step)), "")
 
     def ind(w, o):
         return (w[0].indirect(o[0]), w[1], 16 * o[2], "ind", o[1])
@@ -76,7 +109,7 @@ def build(g, core, T, topo, rank):
     def psum(a):
         return a[1][0][0].startswith("ps")
 
-    def add(eng, fn, outs, ins, dur, lat=0.0, tok=None, extra=()):
+    def add(eng, fns, outs, ins, dur, lat=0.0, tok=None, extra=()):
         i = len(ops)
         deps = {}
         for e in extra:
@@ -109,8 +142,9 @@ def build(g, core, T, topo, rank):
             if w:
                 h[:] = [e for e in h if not (lo <= e[1] and e[2] <= hi)]
             h.append((i, lo, hi, w))
-        ops.append(dict(eng=eng, fn=fn, deps=deps, dur=dur, lat=lat, tok=tok, nm=acc[0][0], low=low[0],
-                        ty=low[0][:1] + eng + acc[0][0][0][:2] + (str(acc[0][0][1] % 256 // 8) if eng == "P" else "")))
+        if dur and any(deps.values()):
+            dur += OPT["wc"]
+        ops.append(dict(eng=eng, fns=fns, deps=deps, dur=dur, lat=lat, tok=tok, nm=acc[0][0], low=low[0]))
         return i
 
     prev = {}
@@ -127,42 +161,56 @@ def build(g, core, T, topo, rank):
         if o[3]:
             return 50 + 3.2 * o[2]
         if ins[0][3]:
-            return 50 + 1.3 * o[2]
-        return 50 + max(50, 0.83 * k * o[2])
+            return 50 + 1.3 * o[2] * OPT["gt" if k == 2 else "gc"]
+        return OPT["vf"] + 0.83 * max(64, k * o[2]) + (OPT["pp"] if any(psum(a) for a in ins) else 0)
 
     def cp(o, i):
-        return add("V", lambda: g.vector.tensor_copy(o[0], i[0]), [o], [i], vcost(o, [i], 0.5 if two(o) and two(i) else 1))
+        return add("V", [lambda: g.vector.tensor_copy(o[0], i[0])], [o], [i], vcost(o, [i], 0.5 if two(o) and two(i) else 1))
 
     def ts(o, i, s1, o0, s2=None, o1=None):
         if o1 is None:
             fn = lambda: g.vector.tensor_scalar(o[0], i[0], val(s1), None, o0)
         else:
             fn = lambda: g.vector.tensor_scalar(o[0], i[0], val(s1), val(s2), o0, o1)
-        return add("V", fn, [o], [i, s1, s2], vcost(o, [i], 0.5 if two(o) and two(i) else 1))
+        return add("V", [fn], [o], [i, s1, s2], vcost(o, [i], 0.5 if two(o) and two(i) else 1))
 
     def tt(o, a, b, op):
-        return add("V", lambda: g.vector.tensor_tensor(o[0], a[0], b[0], op), [o], [a, b], vcost(o, [a], 1 if psum(a) or psum(b) else 2))
+        return add("V", [lambda: g.vector.tensor_tensor(o[0], a[0], b[0], op)], [o], [a, b], vcost(o, [a, b], 1 if psum(a) or psum(b) else 2))
 
     def scan(o, a, b, o0, o1):
-        return add("V", lambda: g.vector.tensor_tensor_scan(o[0], a[0], b[0], 0.0, o0, o1), [o], [a, b], vcost(o, [a], 1))
+        return add("V", [lambda: g.vector.tensor_tensor_scan(o[0], a[0], b[0], 0.0, o0, o1)], [o], [a, b], vcost(o, [a, b], OPT["scan"]))
 
     def ms(o, c):
-        return add("V", lambda: g.vector.memset(o[0], c), [o], [], vcost(o, [o], 0.5 if two(o) else 1))
+        return add("V", [lambda: g.vector.memset(o[0], c)], [o], [], vcost(o, [o], 0.5 if two(o) else 1))
 
     def act(o, i, func=F.Identity, bias=0.0, scale=1.0):
-        return add("S", lambda: g.scalar.activation(o[0], i[0], func, bias=bias, scale=scale), [o], [i],
-                   65 + (1.3 if i[3] else 0.83) * max(o[2], 50))
+        return add("S", [lambda: g.scalar.activation(o[0], i[0], func, bias=val(bias), scale=scale)], [o], [i, bias],
+                   65 + 1.3 * o[2] if i[3] else OPT["sf"] + 0.83 * max(o[2], 64) + (OPT["pp"] if psum(i) else 0))
+
+    def affine(eng, o, i, scale, bias):
+        return act(o, i, bias=bias, scale=scale) if eng == "S" else ts(o, i, scale, A.mult, bias, A.add)
+
+    def mms(lst):
+        fns = [(lambda m=m: g.tensor.matmul(m[0][0], m[1][0], m[2][0], m[3], m[4])) for m in lst]
+        dur = sum(5 + OPT["pe"] * max(min(64, m[1][2]), m[2][2]) * (1 if two(m[1]) else 4) for m in lst)
+        return add("P", fns, [m[0] for m in lst], [a for m in lst for a in m[1:3]], dur, lat=OPT["pl"])
 
     def mm(o, l, r, st=True, sp=True):
-        return add("P", lambda: g.tensor.matmul(o[0], l[0], r[0], st, sp), [o], [l, r],
-                   10 + 0.5 * max(min(64, l[2]), r[2]) * (1 if two(l) else 4), lat=60.0)
+        return mms([(o, l, r, st, sp)])
 
     def iota(o, pat, base, cm):
         if SB[o[1][0][0]][1] == i32:
             fn = lambda: g.iota(o[0], pat, base, cm)
         else:
             fn = lambda: g.iota(o[0], pat, base, cm, allow_small_or_imprecise_dtypes=True)
-        return add("G", fn, [o], [], 130 + 1.7 * o[2])
+        return add("G", [fn], [o], [], 130 + 1.7 * o[2])
+
+    def sel(o, i, pat, op, base, cm):
+        return add("G", [lambda: g.affine_select(o[0], i[0], pat, op, 0.0, base, cm)], [o], [i], 170 + 1.7 * o[2])
+
+    def fill(o, c):
+        i = ap("R", 0, o[2]) if two(o) else ap("JJ", 0, o[2])
+        return add("G", [lambda: g.affine_select(o[0], i[0], [[0, o[2]]], A.is_gt, c, 0, 0)], [o], [i], 170 + 1.7 * o[2])
 
     dclock = [0.0]
 
@@ -170,12 +218,10 @@ def build(g, core, T, topo, rank):
         s = "d%d" % ndma[0]
         ndma[0] += 1
         q = g.sync if eng == "Y" else g.scalar
-        lat = 2000 + nbytes / 150.0
         if load:
-            dclock[0] += nbytes / 300.0
-            lat = 2000 + dclock[0]
-            return chain(eng, add(eng, lambda: q.dma_start(o[0], i).then_inc(T.sem[s], 16), [o], [], 60, lat=lat, tok=(s, 16)))
-        return add(eng, lambda: q.dma_start(o, i[0]).then_inc(T.sem[s], 16), [], [i], 60, lat=lat, tok=(s, 16))
+            dclock[0] += OPT["drow"] + nbytes / OPT["dbw"]
+            return chain(eng, add(eng, [lambda: q.dma_start(o[0], i).then_inc(T.sem[s], 16)], [o], [], 60, lat=1500 + dclock[0], tok=(s, 16)))
+        return add(eng, [lambda: q.dma_start(o, i[0]).then_inc(T.sem[s], 16)], [], [i], 60, lat=2300 + nbytes / 300.0, tok=(s, 16))
 
     others = [c for c in T.cores if c != core]
     common = [e for e in topo.engines(core, others[0]) if all(e in topo.engines(core, c) for c in others)]
@@ -185,32 +231,29 @@ def build(g, core, T, topo, rank):
     emask = sum(1 << e for e in common[:ne])
     dsts = [DstId(rid=topo.addr(c)[0], pnc=topo.addr(c)[1]) for c in others]
 
-    def share(name, base, width, nbytes):
+    def share(name, base, pitch, width, after=()):
         s = "d%d" % ndma[0]
         ndma[0] += 1
         r = "ar%d" % narr[0]
         narr[0] += 1
-        a = ap(name, base + rank * width, base + (rank + 1) * width)
+        a = ap(name, base + rank * pitch, base + rank * pitch + width)
         fn = lambda: g.remote_dma_fused([RemoteDMATransfer(dst_ids=dsts, dma_engine_mask=emask, remote_sem=T.sem[r],
                                                            src=a[0], dsts=[a[0]] * len(dsts))], local_sem=T.sem[s])
-        i = add("G", fn, [], [a], 1000, lat=1500 + 3 * nbytes / 150.0, tok=(s, ne))
-        land = [ap(name, base + d * width, base + (d + 1) * width) for d in range(N) if d != rank]
-        add("X", None, land, [], 0, lat=300.0, tok=(r, ne * len(others)), extra=[i])
+        i = add("G", [fn], [], [a], 1000, lat=2000 + (OPT["first"] if narr[0] == 1 else 0) + 3 * (256 if two(a) else 512) * width / 150.0,
+                tok=(s, ne), extra=after)
+        land = [ap(name, base + d * pitch, base + d * pitch + width) for d in range(N) if d != rank]
+        add("X", [], land, [], 0, lat=300.0, tok=(r, ne * len(others)), extra=[i])
 
-    def P(b, lo, hi, step=1, p1=128):
-        return ap("ps%d" % b, lo, hi, step, 0, p1)
-
-    dma("S", ap("cb", 0, 3), T.co[:], 1e3, True)
-    dma("S", ap("x0"), T.xl[:], 65e3, True)
-    dma("S", ap("wi", p1=8), T.wl[:], 8e3, True)
-    NCH = 8
-    CW = Q // NCH
-    for j in range(NCH):
-        dma("Y", ap("hi", j * CW, (j + 1) * CW), T.hlp[:, j * CW:(j + 1) * CW], 128 * 4 * CW, True)
-        if j == 3:
-            dma("S", ap("Gz", 16, 4112), T.gen[:], 1.05e6, True)
+    dma("Y", ap("cb", 0, 3), T.co[:], 1e3, True)
+    dma("Y", ap("x0"), T.xl[:], 65e3, True)
+    c0 = 0
+    for cw in OPT["hch"]:
+        dma("Y", ap("hi", c0, c0 + cw), T.hlp[:, c0:c0 + cw], 512 * cw, True)
+        c0 += cw
+    dma("Y", ap("Gz", 16, 4112), T.gen[:], 1.05e6, True)
+    dma("Y", ap("vi", 0, 64), T.vst[:], 32e3, True)
     dma("Y", ap("xs"), T.xst[:], 262e3, True)
-    dma("Y", ap("vi", p1=8), T.vst[:], 32e3, True)
+    dma("Y", ap("wi", p1=8), T.wl[:], 8e3, True)
 
     iota(ap("pi", 0, 2), [[0, 2]], 0, 1)
     iota(ap("JJ"), [[0, 17], [1, 16]], 0, 0)
@@ -220,89 +263,104 @@ def build(g, core, T, topo, rank):
     pm, pd = ap("pc", 0, 1), ap("pc", 1, 2)
     ts(ap("pc", 2, 3), pm, 1.0, A.add)
     cp(ap("cf", 0, 3), ap("cb", 0, 3))
-    GBf, S0f = ap("GB", 0, 8), ap("GB", 8, 16)
+    cw_, ca_, cc_ = ap("cf", 0, 1), ap("cf", 1, 2), ap("cf", 2, 3)
+    GBf, S0f, nGBf = ap("GB", 0, 8), ap("GB", 8, 16), ap("GB", 16, 24)
     ts(GBf, ap("JJ", 0, 8), pd, A.is_equal)
-    W1, W2, ablk, cblk, GBb, nS0 = [ap("Gb", 8 * i, 8 * i + 8) for i in range(6)]
-    ts(ablk, GBf, ap("cf", 1, 2), A.mult)
-    ts(cblk, GBf, ap("cf", 2, 3), A.mult)
+    W1, W1n, W2, ablk, cblk, G17, nS0, KC = [ap("Gb", 8 * i, 8 * i + 8) for i in range(8)]
+    ts(ablk, GBf, ca_, A.mult)
+    ts(cblk, GBf, cc_, A.mult)
     ms(ap("Aw"), 0.0)
     cp(ap("Aw", 15, 128, 16), ablk)
     cp(ap("Aw", 159, 272, 16), cblk)
-    ones, zeros, c192 = ap("cst", 0, 128), ap("cst", 128, 256), ap("cst", 256, 384)
-    ms(c192, 192.0)
-    for o, nm, n8 in ((0, ablk, 0), (144, cblk, 32)):
-        bk = 6 if o == 0 else 7
-        for m in range(16):
-            mm(P(bk, 0, 16), ap("Aw", o + 15 - m, o + 143 - m), ap("cst", 256, 272), m == 0, m == 15)
-        mm(P(bk, 16, 24), c192, nm)
-        if o == 0:
-            act(ap("CA", 0, 16), P(bk, 8, 24))
-            act(ap("CA", 16, 24), P(bk, 16, 24))
-            act(ap("CA", 24, 32), P(bk, 0, 8))
-        else:
-            act(ap("CA", 32, 56), P(bk, 0, 24))
-            act(ap("CA", 56, 64), P(bk, 16, 24))
-    iota(ap("vv", 0, 128), [[1, 128]], 0, -1)
-    If, Ib, nIb, LT = ap("If"), ap("Ib", 0, 128), ap("Ib", 128, 256), ap("Ib", 256, 384)
-    ts(If, ap("vv", 0, 128), 0.0, A.is_equal)
-    ts(Ib, ap("vv", 0, 128), 0.0, A.is_equal)
-    iota(ap("R"), [[1, 128], [0, 16]], 0, -1)
-    ts(ap("R"), ap("R"), 0.0, A.is_equal)
-    ts(nIb, ap("vv", 0, 128), 0.0, A.is_equal, -1.0, A.mult)
-    ts(LT, ap("vv", 0, 128), 0.0, A.is_ge)
-    ts(ap("v2", 0, 128), ap("vv", 0, 128), 0.0, A.is_gt)
-    iota(ap("jm", 0, 128), [[1, 8], [0, 16]], 0, 0)
+    ones, zeros, n192, n200 = [ap("cst", 128 * i, 128 * i + 128) for i in range(4)]
+    ms(ones, 1.0)
+    ms(zeros, 0.0)
+    ms(n192, -192.0)
+    ms(n200, -200.0)
+    iota(ap("j8"), [[1, 8], [0, 16]], 0, 0)
+    AF, CF = ap("AF", 0, 128), ap("AF", 128, 256)
+    ts(AF, ap("j8"), pd, A.is_equal, ca_, A.mult)
+    ts(CF, ap("j8"), pd, A.is_equal, cc_, A.mult)
+    If, nIf = ap("If"), ap("nIf")
+    Ib, nIb, n12, n17, LT, n8, I5, I11 = [ap("Ib", 128 * i, 128 * i + 128) for i in range(8)]
+    diag = [[1, 128]]
+    sel(Ib, ones, diag, A.is_equal, 0, -1)
+    ts(n12, Ib, -4096.0, A.mult)
+    iota(ap("yv8", 0, 128), [[1, 128]], 0, 0)
+    cp(ap("kR", 0, 128), ap("yv8", 0, 128))
+    for j in range(2):
+        act(ap("R", 1024 * j, 1024 * j + 1024), ind(Ib, ap("kR", 64 * j, 64 * j + 64)))
+    act(If, Ib)
+    act(nIf, Ib, scale=-1.0)
+    act(I5, Ib, scale=32.0)
+    act(I11, Ib, scale=2048.0)
+    act(nIb, Ib, scale=-1.0)
+    act(n17, Ib, scale=-2.0 ** 17)
+    sel(LT, ones, diag, A.is_gt, 0, -1)
     BDB, LTB = ap("BD", 0, 128), ap("BD", 128, 256)
-    ts(BDB, ap("jm", 0, 128), pd, A.is_equal, BIGK, A.mult)
-    ts(ap("kw"), ap("jm", 0, 128), pd, A.is_equal, ap("pc", 2, 3), A.mult)
-    tt(LTB, BDB, ap("v2", 0, 128), A.mult)
-    if BSCAN:
-        ts(ap("AF"), ap("jm", 0, 128), pd, A.is_equal, ap("cf", 1, 2), A.mult)
+    ts(BDB, ap("j8"), pd, A.is_equal, BIGK, A.mult)
+    sel(LTB, BDB, diag, A.is_gt, 0, -1)
+    act(n8, Ib, scale=-256.0)
+    tt(LT, LT, n8, A.add)
+    ts(ap("kw"), ap("j8"), pd, A.is_equal, ap("pc", 2, 3), A.mult)
+    act(ap("BF"), BDB, scale=1.0 / BIGK)
     iota(ap("vv"), [[-16, 8], [-1, 17]], 0, 1)
     ts(ap("DM"), ap("vv"), -1.0, A.is_equal)
     ts(ap("v2"), ap("vv"), 0.0, A.is_equal)
-    cp(S0f, ap("v2", 0, 136, 17))
-    ts(nS0, ap("v2", 0, 136, 17), -1.0, A.mult)
+    S2 = ap("S2")
+    for j in range(2):
+        act(ap("S2", j, 16, 2), ap("v2", j, 136, 17), scale=256.0)
     ms(ap("v2", 16, 136, 17), 0.0)
     tt(ap("DM"), ap("DM"), ap("v2"), A.subtract)
     ms(ap("DLT"), -1.0)
-    ms(ap("DLT", 0, 136, 17), 33554432.0)
+    ms(ap("DLT", 0, 136, 17), BG)
     ms(ap("DLT", 16, 136, 17), 16.0)
-    ms(zeros, 0.0)
-    ms(ones, 1.0)
     ms(ap("Gz", 0, 16), 0.0)
-    ts(W1, GBf, ap("cf", 0, 1), A.mult, 32.0, A.mult)
-    ts(W2, GBf, ap("cf", 0, 1), A.mult, -64.0, A.mult)
-    cp(GBb, GBf)
+    ts(W1, GBf, cw_, A.mult, 32.0, A.mult)
+    act(W1n, W1, scale=-1.0)
+    act(W2, W1, scale=2.0)
+    act(G17, GBf, scale=2.0 ** 17)
     ts(ap("EK"), ap("JJ"), pm, A.is_equal)
-    ts(ap("NK"), ap("JJ"), pm, A.not_equal)
-    ts(ap("NEG"), ap("NK", 0, 256), -33554432.0, A.mult)
-    lc, l17, l4 = ap("ls", 0, 16), ap("ls", 16, 24), ap("ls", 24, 28)
+    act(ap("NEG"), ap("EK", 0, 256), scale=BG, bias=-BG)
+    lc, l17, l18, l3 = ap("ls", 0, 16), ap("ls", 16, 24), ap("ls", 32, 40), ap("ls", 48, 64)
     cp(lc, ap("JJ", 0, 16))
     ts(l17, ap("JJ", 0, 8), 17.0, A.mult, 16.0, A.add)
-    ts(ap("J", 0, 16), ap("JJ", 0, 16), 16.0, A.mult, pm, A.add)
-    dumO, dumX = ap("J", 16, 32), ap("J", 32, 48)
-    ts(dumO, ap("J", 0, 16), 4096.0, A.add)
-    ts(dumX, ap("J", 0, 16), 12288.0, A.add)
-    cp(ap("za", 0, 4), ap("J", 0, 4))
-    ts(ap("zb", 0, 4), ap("za", 0, 4), 2, A.arith_shift_right)
-    cp(l4, ap("zb", 0, 4))
-    iota(ap("dc"), [[0, 16], [1, 4]], 0, 0)
-    DT, DT2 = ap("DT", 0, 16), ap("DT", 16, 32)
-    iota(DT, [[128, 2], [0, 8]], 16384, 1)
-    iota(DT2, [[128, 2], [0, 8]], 8192, 1)
-    iota(ap("sT"), [[1, 128]], 0, -16)
-    ts(ap("sT"), ap("sT"), 0.0, A.is_equal)
-    BG = 33554432.0
-    l18, KC, nGBf = ap("ls", 32, 40), ap("Gb", 48, 56), ap("GB", 16, 24)
     ts(l18, ap("JJ", 0, 8), 18.0, A.mult, 17.0, A.add)
+    ts(l3, ap("JJ", 0, 16), 3.0, A.mult, 2.0, A.add)
+    ts(ap("J", 0, 16), ap("JJ", 0, 16), 16.0, A.mult, pm, A.add)
+    dumO = ap("J", 16, 32)
+    act(dumO, ap("J", 0, 16), bias=4096.0)
+    iota(ap("dc"), [[0, 2], [1, 4], [0, 8]], -760, 0)
+    iota(ap("sU", 0, 128), [[1, 128]], 0, -16)
+    ts(ap("sU", 128, 256), ap("sU", 0, 128), -127.0, A.is_equal)
+    ts(ap("sU", 0, 128), ap("sU", 0, 128), 0.0, A.is_equal)
+    tt(ap("sT"), ap("sU", 0, 128), ap("sU", 128, 256), A.add)
+    ts(ap("cj", 0, 1), cc_, 2.0, A.add)
+    ts(ap("cj", 1, 2), ap("cj", 0, 1), 3, A.bitwise_and)
+    ts(ap("cf", 3, 4), ap("cj", 1, 2), -2.0, A.add)
+    iota(ap("j4"), [[0, 4], [1, 8]], 0, 0)
+    c4, G4 = ap("c4", 0, 64), ap("c4", 64, 96)
+    ts(G4, ap("j4"), pd, A.is_equal)
+    for h in range(2):
+        ts(ap("c4", 32 * h, 32 * h + 32), G4, ap("cf", 3, 4), A.mult)
+    ms = fill
+    ms(ap("CD", 0, 48, 3), 2.0 ** 20 / 128)
+    ms(ap("CD", 1, 48, 3), 8192.0 / 128)
+    ms(ap("CD", 2, 48, 3), 2.0 ** 16 / 128)
+    mms([(P(7, 0, 8), n192, ablk, True, True), (P(7, 8, 16), n192, cblk, True, True)])
+    for h in range(2):
+        act(ap("CAT", 24 * h, 24 * h + 24, 3), P(7, 0, 8), bias=TOP)
+        act(ap("CAT", 24 * h + 2, 24 * h + 24, 3), P(7, 8, 16), bias=TOP + CS + 2.0 ** 17)
+    ms(ap("CAT", 1, 48, 3), 2.0 ** 20)
+    mms([(P(6, 2 * j, 2 * j + 2), (AF, CF)[j], ap("cst", 256, 258), True, True) for j in range(2)])
+    for j in range(2):
+        act(ap("cm", 4 * j, 4 * j + 1), P(6, 2 * j, 2 * j + 1))
+        act(ap("cm", 4 * j + 1, 4 * j + 2), P(6, 2 * j, 2 * j + 1), scale=2.0 ** -12, bias=FLO)
+        act(ap("cm", 4 * j + 2, 4 * j + 3), P(6, 2 * j, 2 * j + 1), bias=TOP)
+    ms(ap("C16"), 0.0)
+    ms(ap("C16", 16, 136, 17), 0.125)
     ts(KC, GBf, pm, A.mult)
-    nW1 = ap("Gb", 56, 64)
-    if AV:
-        ts(nW1, W1, -1.0, A.mult)
-    ts(nGBf, GBf, -1.0, A.mult)
-    ts(ap("nIf"), If, -1.0, A.mult)
-    ts(ap("BF"), BDB, 1.0 / BIGK, A.mult)
+    act(nGBf, GBf, scale=-1.0)
     iota(ap("v3"), [[-16, 8], [-1, 18]], 0, 1)
     ts(ap("DN"), ap("v3"), -1.0, A.is_equal)
     ts(ap("v3"), ap("v3"), 0.0, A.is_equal)
@@ -310,8 +368,8 @@ def build(g, core, T, topo, rank):
     ms(ap("v3", 17, 144, 18), 0.0)
     ms(ap("DN", 17, 144, 18), 0.0)
     tt(ap("DN"), ap("DN"), ap("v3"), A.subtract)
-    ts(ap("RC"), ap("v3"), BG, A.mult)
-    ts(ap("RC", 16, 144, 18), GBf, -BG, A.mult)
+    act(ap("RC"), ap("v3"), scale=BG)
+    act(ap("RC", 16, 144, 18), GBf, scale=-BG)
     ms(ap("CR"), 0.0)
     ms(ap("CR", 16, 144, 18), BG / 128)
     ms(ap("CR", 161, 288, 18), 0.125)
@@ -320,408 +378,439 @@ def build(g, core, T, topo, rank):
     ms(ap("DLN", 16, 144, 18), 15.0)
     ms(ap("DLN", 17, 144, 18), 1.0)
     ms(ap("RST"), 0.0)
-    ms(ap("RST", 0, 256, 16), -67108864.0)
+    ms(ap("RST", 0, 256, 16), -2 * BG)
+    act(ap("KO"), ap("RST"))
     ms(ap("we"), 0.0)
-    ms(ap("thr"), 0.5)
+    iota(ap("thr"), [[0, 64]], 0, 0)
     for nm in ("SW", "YH", "XW"):
         ms(ap(nm, 4096, 4352), 0.0)
 
     W = ap("W")
     cp(ap("wf", p1=8), ap("wi", p1=8))
-    for h in range(2):
-        mm(P(6, 8 * h, 8 * h + 8), ap("wf", 128 * h, 128 * h + 128, p1=8), ap("If", 0, 8, p1=8))
-    cp(W, P(6, 0, 16))
-    for j in range(NCH):
-        cp(ap("SW", j * CW, (j + 1) * CW), ap("hi", j * CW, (j + 1) * CW))
-    for j in range(4):
-        ts(ap("vf", 256 * j, 256 * j + 256, p1=8), ap("vi", 256 * j, 256 * j + 256, p1=8), -2047.5, A.add, 1.0 / FR, A.mult)
+    mms([(P(6, 8 * h, 8 * h + 8), ap("wf", 128 * h, 128 * h + 128, p1=8), ap("If", 0, 8, p1=8), True, True) for h in range(2)])
+    ts(W, P(6, 0, 16), 32.0, A.mult)
+    for j in range(8):
+        cp(ap("SW", j * 512, (j + 1) * 512), ap("hi", j * 512, (j + 1) * 512))
+    ts(ap("vd", 0, 64), ap("vi", 0, 64), 63, A.bitwise_and)
+    ts(ap("vd", 64, 128), ap("vi", 0, 64), 6, A.arith_shift_right)
+    ts(ap("vb"), ap("vd"), 1.0 / 256, A.mult, -0.125, A.add)
+    for j in range(2):
+        s = "d%d" % ndma[0]
+        ndma[0] += 1
+        o, i = ap("vf", p0=8 * j, p1=8 * j + 8), ap("vb", 64 * j, 64 * j + 64)
+        fn = lambda o=o, i=i, s=s: g.sync.dma_start(o[0], i[0]).then_inc(T.sem[s], 16)
+        add("Y", [fn], [ap("vf", j, j + 1)], [i], 60, lat=2600, tok=(s, 16))
 
-    def sums(j):
-        bk = j % 2
+    def sums(j, bk):
         for u in range(2):
             mm(P(bk, 256 * u, 256 * u + 256), ap("kw"), ap("SW", 512 * j + 256 * u, 512 * j + 256 * u + 256))
         act(ap("YH", 512 * j, 512 * j + 512), P(bk, 0, 512))
 
-    def store(j):
-        bk = 2 + j % 2
-        mm(P(bk, 0, 512), Ib, ap("xs", 512 * j, 512 * j + 512), True, False)
-        for u in range(2):
-            mm(P(bk, 256 * u, 256 * u + 256), ap("sT", p1=8), ap("vf", 512 * j + 256 * u, 512 * j + 256 * u + 256, p1=8), False, u == 1)
-        act(ap("XW", H * rank + 512 * j, H * rank + 512 * j + 512), P(bk, 0, 512))
+    def store():
+        for j in range(2):
+            bk = 6 + j
+            mm(P(bk, 0, 512), Ib, ap("xs", 512 * j, 512 * j + 512), True, False)
+            v = ap("vf", 512 * j, 512 * j + 512, p1=16)
+            mm(P(bk, 0, 512), ap("sT", p1=16), (v[0], ap("vf")[1]) + v[2:], False, True)
+            affine(OPT["sg"], ap("SG", H * rank + 512 * j, H * rank + 512 * j + 512), P(bk, 0, 512), 1.0, UP)
+        share("SG", 0, H, H)
+        chain("lay", len(ops) - 2)
+        for d in [(rank + e) % N for e in range(N)]:
+            if OPT["lay"][(d - rank) % N] == "G":
+                chain("lay", sel(ap("XW", d, 4096, 4), ap("SG", H * d, H * d + H), [[0, H]], A.is_ge, 0, 0))
+            else:
+                for u in range(2):
+                    act(ap("XW", 2048 * u + d, 2048 * u + 2048, 4), ap("SG", H * d + 512 * u, H * d + 512 * u + 512))
 
-    xv, qv, rb = [0], [0], [0]
+    xv, qv = [0], [0]
     for h in range(2):
         act(ap("q0", 128 * h, 128 * h + 128), ap("x0", 128 * h, 128 * h + 128), scale=0.25, bias=191.625)
 
-    def step_half(h, last, xo, xn, qo, qn):
+    def modulo(eng, bk, n, more, first, o, blk, q, r, out):
+        qn, lo, hi = q
+        w = hi - lo
+        col = [ap("cm", 4 * more + j, 4 * more + j + 1) for j in range(3)]
+        if eng in "IC":
+            mms([(P(bk, 0, n), ap("Aw", o + 15 - m, o + 143 - m), ap(qn, lo + m, hi, 16), m == 0, m == 15) for m in range(16)])
+            src = P(bk, 0, n)
+            if eng == "C":
+                act(ap("rw", blk, blk + n), src, bias=col[1], scale=2.0 ** -12)
+                act(ap("pf", blk, blk + n), src, bias=col[2])
+                mms([(src, n12, ap("rw", blk, blk + n), True, False), (src, If, ap("pf", blk, blk + n), False, True)])
+                cp(out, src)
+                return
+        else:
+            if eng == "F":
+                mm(P(bk, 16, 16 + w), first, ap(qn, lo, hi))
+                act(ap("rw", lo, hi), P(bk, 16, 16 + w), bias=col[1], scale=2.0 ** -12)
+                mms([(P(r, 384, 384 + w), Ib, ap("NEG", 0, w), True, False), (P(r, 384, 384 + w), first, ap(qn, lo, hi), False, False)])
+                mm(P(r, 384, 384 + w), n12, ap("rw", lo, hi), False, True)
+                scan(ap("KA", lo, hi), ap("RST", 0, w), P(r, 384, 384 + w), A.add, A.max)
+                ts(out, ap("KA", lo + 15, hi, 16), col[2], A.add)
+                return
+            mm(P(bk, 16, 16 + w), Ib, ap("NEG", 0, w), True, False)
+            mm(P(bk, 16, 16 + w), first, ap(qn, lo, hi), False, True)
+            kn = "K" if more else "KA"
+            scan(ap(kn, lo, hi), ap("RST", 0, w), P(bk, 16, 16 + w), A.add, A.max)
+            src = ap(kn, lo + 15, hi, 16)
+        ts(ap("bj", blk, blk + n), src, col[0], A.add)
+        ts(ap("bI", blk, blk + n), ap("bj", blk, blk + n), 4095, A.bitwise_and)
+        cp(out, ap("bI", blk, blk + n))
+
+    def spans(modes, m):
+        out = []
+        for j in range(4):
+            if modes[j] == m:
+                if out and out[-1][1] == 32 * j and out[-1][0] != 32 and not (out[-1][0] == 32 * (j - 1) == 96):
+                    out[-1][1] += 32
+                else:
+                    out.append([32 * j, 32 * j + 32])
+        return out
+
+    def compare(h, modes, banks, gch, vch, byv=()):
+        lo = 128 * h
+        gn, mn = ("gA", "mA") if h == 0 else ("gB", "mB")
+        fn = F.Abs if "V" not in modes else F.Relu
+        done = -1
+        for j in range(4):
+            if j in byv:
+                cp(ap(gn, 512 * j, 512 * j + 512), ind(ap("Gz", 16, 4112), ap("hu", lo + 32 * j, lo + 32 * j + 32)))
+        for js in vch:
+            j0, j1 = js[0], js[-1] + 1
+            for gs in gch:
+                if gs[0] < j1 + (modes[j0] == "S") + (4 if j0 in byv else 0) and gs[0] > done:
+                    done = gs[0]
+                    if done not in byv:
+                        chain("g", act(ap(gn, 512 * gs[0], 512 * gs[-1] + 512), ind(ap("Gz", 16, 4112), ap("hu", lo + 32 * gs[0], lo + 32 * gs[-1] + 32))))
+            for j in js:
+                on_v = modes[j] == "V"
+                mm(P(banks + j % 2, 0, 512), ap("xT", lo, lo + 128), ap("R", 512 * j, 512 * j + 512), True, on_v)
+                if not on_v:
+                    mm(P(banks + j % 2, 0, 512), nIb, ap(gn, 512 * j, 512 * j + 512), False, True)
+            src = P(banks + j0 % 2, 0, 512 * (j1 - j0))
+            if modes[j0] == "V":
+                tt(ap(mn, 512 * j0, 512 * j1), ap(gn, 512 * j0, 512 * j1), src, A.max)
+            else:
+                i = act(ap(mn, 512 * j0, 512 * j1), src, fn, scale=-1.0)
+                if OPT["schain"]:
+                    chain("g", i)
+        return gn, mn
+
+    def choose(h, kb, mb, at, n, dl, ll, xo, xn, qn):
+        lo, hi = 128 * h, 128 * h + 128
+        s0, s1 = n * h, n * h + n
+        scan(ap("us", s0, s1), dl, P(kb, 0, n), A.add, A.min)
+        tt(ap("nf", s0, s1), ap("us", s0, s1), P(kb, 0, n), A.not_equal)
+        scan(ap("es", s0, s1), P(mb, at, at + n), ap("nf", s0, s1), A.add, A.mult)
+        tt(ap("em", lo, hi), ind(ap("es", s0, s1), ll), ap("EK", 0, 128), A.mult)
+        mm(P(mb, 416, 424), ap("em", lo, hi), GBf)
+        su = ap("su", 8 * h, 8 * h + 8)
+        cp(su, P(mb, 416, 424))
+        apart(OPT["dd"][0 if n == 136 else 1], ap(xn, lo, hi), ap("Gz"), su, xo, h, P(2 + h, 256, 384))
+        act(ap(qn, lo, hi), ap(xn, lo, hi), scale=0.25, bias=191.625)
+
+    def apart(eng, out, win, su, xo, h, bank):
+        lo, hi = 128 * h, 128 * h + 128
+        if eng == "V":
+            tt(ap("dd", lo, hi), ind(win, su), ap(xo, lo, hi), A.subtract)
+            act(out, ap("dd", lo, hi), F.Abs)
+        else:
+            mm(bank, nIb, ap(xo, lo, hi), True, False)
+            act(ap("dd", lo, hi), ind(win, su))
+            mm(bank, Ib, ap("dd", lo, hi), False, True)
+            act(out, bank, F.Abs)
+
+    def step_half(h, last, raw, xo, xn, qo, qn):
         lo, hi = 128 * h, 128 * h + 128
         kb, mb = 2 + h, 4 + h
-        late = False
-        gn, mn = "gA" if h == 0 else "gB", "mA" if h == 0 else "mB"
-        oc, tc = (0, 8) if h == 0 else (8, 0)
+        modes = OPT["step"][2 * last + h]
         mm(P(kb, 256, 384), ap(xo, lo, hi), Ib)
         act(ap("xT", lo, hi), P(kb, 256, 384))
-        a0, a1 = (oc, oc + 8)
-        if BSCAN:
-            mm(P(mb, 128, 256), Ib, ap("NEG", 0, 128), True, False)
-            mm(P(mb, 128, 256), ap("AF"), ap(qo, lo, hi), False, True)
-            scan(ap("KA", lo, hi), ap("RST", 0, 128), P(mb, 128, 256), A.add, A.max)
-            tt(ap("bj", 24 * h, 24 * h + 8), ap("KA", lo + 15, hi, 16), ap("CA", 24 * h, 24 * h + 8), A.subtract)
-            if last:
-                mm(P(mb, tc, tc + 8), ap(qo, lo, hi), ablk)
-                tt(ap("bj", 8 + 8 * h, 16 + 8 * h), P(mb, tc, tc + 8), ap("CA", 8 + 8 * h, 16 + 8 * h), A.subtract)
-                ts(ap("bI", 8 + 8 * h, 16 + 8 * h), ap("bj", 8 + 8 * h, 16 + 8 * h), 4095, A.bitwise_and)
-            b0, b1 = 16 * h + a0, 16 * h + a1
-        else:
-            for m in range(16):
-                mm(P(mb, oc, oc + 8), ap("Aw", 15 - m, 143 - m), ap(qo, lo + m, hi, 16), m == 0, m == 15)
-            if last:
-                mm(P(mb, tc, tc + 8), ap(qo, lo, hi), ablk)
-                a0, a1 = 0, 16
-            b0, b1 = 16 * h + a0, 16 * h + a1
-            tt(ap("bj", b0, b1), P(mb, a0, a1), ap("CA", b0, b1), A.subtract)
-        ts(ap("bI", b0, b1), ap("bj", b0, b1), 4095, A.bitwise_and)
         bu = ap("bu", 8 * h, 8 * h + 8)
-        cp(bu, ap("bI", 24 * h, 24 * h + 8))
-        cp(ap("hu", lo, hi), ind(ap("SW", 0, 4096), bu))
-        act(ap("hf", lo, hi), ind(ap("SW", 0, 4096), bu), bias=16.0)
-        if not late:
+        modulo(OPT["mod"], mb, 8, 0, AF, 0, 8 * h, (qo, lo, hi), kb, bu)
+        cp(ap("hu", lo, hi), ind(ap("hi" if raw else "SW", 0, 4096), bu))
+        if raw:
+            ts(ap("hf", lo, hi), ind(ap("hi"), bu), 16.0, A.add)
             mm(P(mb, 272, 408), ap("hf", lo, hi), ap("DM"))
-        c0 = 0
-        for j, cw in enumerate(CHUNKS):
-            bk = 6 * h + j % 2
-            mm(P(bk, 0, cw), ap("xT", lo, hi), ap("R", c0, c0 + cw))
-            gj = ap(gn, c0, c0 + cw)
-            chain("g", act(gj, ind(ap("Gz", 16, 4112), ap("hu", lo + c0 // 16, lo + (c0 + cw) // 16))))
-            chain("m", tt(ap(mn, c0, c0 + cw), gj, P(bk, 0, cw), A.min))
-            c0 += cw
-        mm(P(kb, 0, 136), zeros, ap("R", 0, 136), True, False)
-        for k in range(16):
-            mm(P(kb, k, 136, 17), ap(gn, k, 2048, 16), W1, False, False)
-        for k in range(16):
-            mm(P(kb, k, 136, 17), ap(mn, k, 2048, 16), W2, False, k == 15)
-        s0, s1 = 136 * h, 136 * h + 136
-        scan(ap("us", s0, s1), ap("DLT"), P(kb, 0, 136), A.add, A.min)
-        tt(ap("nf", s0, s1), ap("us", s0, s1), P(kb, 0, 136), A.not_equal)
-        scan(ap("es", s0, s1), P(mb, 272, 408), ap("nf", s0, s1), A.add, A.mult)
-        tt(ap("em", lo, hi), ind(ap("es", s0, s1), l17), ap("EK", 0, 128), A.mult)
-        mm(P(mb, 256, 264), ap("em", lo, hi), GBf)
-        su = ap("su", 8 * h, 8 * h + 8)
-        cp(su, P(mb, 256, 264))
-        tt(ap("dd", lo, hi), ind(ap("Gz"), su), ap(xo, lo, hi), A.subtract)
-        act(ap(xn, lo, hi), ap("dd", lo, hi), F.Abs)
-        if QV:
-            ts(ap(qn, lo, hi), ap(xn, lo, hi), 0.25, A.mult, 191.625, A.add)
+        elif last:
+            mms([(P(mb, 8, 16), n192, ablk, True, False), (P(mb, 8, 16), ap(qo, lo, hi), ablk, False, True)])
+            act(ap("rr", 16 * h + 8, 16 * h + 16), P(mb, 8, 16), scale=2.0 ** -12, bias=FLO)
+            act(ap("hl", lo, hi), ind(ap("SW", 0, 4096), bu))
+            mms([(P(mb, 272, 408), ones, ap("C16"), True, False), (P(mb, 272, 408), ap("hl", lo, hi), ap("DM"), False, True)])
         else:
-            act(ap(qn, lo, hi), ap(xn, lo, hi), scale=0.25, bias=191.625)
+            act(ap("hf", lo, hi), ind(ap("SW", 0, 4096), bu), bias=16.0)
+            mm(P(mb, 272, 408), ap("hf", lo, hi), ap("DM"))
+        gn, mn = compare(h, modes, 6 * h, OPT["gch"], OPT["vch"], OPT["byv"][2 * last + h])
+        mms([(P(kb, 0, 136), zeros, ap("R", 0, 136), True, False)]
+            + [(P(kb, 16, 136, 17, p0, p1), ap(xo, lo + p0, lo + p1), W2, False, False) for p0, p1 in spans(modes, "V")])
+        cuts = OPT["cut"]
+        for p0, p1 in cuts:
+            mms([(P(kb, k, 136, 17, p0, p1), ap(gn, 16 * p0 + k, 16 * p1, 16), W1n, False, False) for k in range(16)])
+        for p0, p1 in cuts:
+            mms([(P(kb, k, 136, 17, p0, p1), ap(mn, 16 * p0 + k, 16 * p1, 16), W2, False, k == 15 and p1 == 128) for k in range(16)])
+        choose(h, kb, mb, 272, 136, ap("DLT"), l17, xo, xn, qn)
 
     def ahead(h, xo, qo):
         lo, hi = 128 * h, 128 * h + 128
         mb = 4 + h
-        gn, mn = "gA" if h == 0 else "gB", "mA" if h == 0 else "mB"
+        modes = OPT["ahead"][h]
         mm(P(mb, 384, 512), ap(xo, lo, hi), Ib)
         act(ap("xT", lo, hi), P(mb, 384, 512))
-        for m in range(16):
-            mm(P(mb, 0, 8), ap("Aw", 15 - m, 143 - m), ap(qo, lo + m, hi, 16), m == 0, m == 15)
-        b0 = 24 * h
-        tt(ap("bj", b0, b0 + 8), P(mb, 0, 8), ap("CA", b0, b0 + 8), A.subtract)
-        ts(ap("bI", b0, b0 + 8), ap("bj", b0, b0 + 8), 4095, A.bitwise_and)
         bu = ap("bu", 8 * h, 8 * h + 8)
-        cp(bu, ap("bI", b0, b0 + 8))
+        modulo(OPT["moda"], mb, 8, 0, AF, 0, 8 * h, (qo, lo, hi), mb, bu)
         cp(ap("hu", lo, hi), ind(ap("SW", 0, 4096), bu))
         act(ap("hf", lo, hi), ind(ap("SW", 0, 4096), bu))
-        mm(P(mb, 0, 288), ones, ap("CR"), True, False)
-        mm(P(mb, 144, 288), ap("hf", lo, hi), ap("DN"), False, False)
-        cw = AHEAD
-        if h in AV:
-            mm(P(mb, 16, 144, 18), ap(xo, lo, hi), nW1, False, False)
+        run = [(P(mb, 0, 288), ones, ap("CR"), True, False)]
+        if "V" not in modes:
+            run += [(P(mb, 17, 144, 18), ap(xo, lo, hi), W1, False, False)]
         else:
-            mm(P(mb, 17, 144, 18), ap(xo, lo, hi), W1, False, False)
-        for j in range(2048 // cw):
-            bk = j % 2
-            gj = ap(gn, cw * j, cw * j + cw)
-            chain("g", act(gj, ind(ap("Gz", 16, 4112), ap("hu", lo + cw // 16 * j, lo + cw // 16 * (j + 1)))))
-            mm(P(bk, 0, cw), ap("xT", lo, hi), ap("R", cw * j, cw * j + cw), True, h in AV)
-            if h in AV:
-                tt(ap(mn, cw * j, cw * j + cw), gj, P(bk, 0, cw), A.min)
-            else:
-                mm(P(bk, 0, cw), nIb, gj, False, True)
-                act(ap(mn, cw * j, cw * j + cw), P(bk, 0, cw), F.Abs)
-        if h in AV:
-            for k in range(16):
-                mm(P(mb, k, 144, 18), ap(gn, k, 2048, 16), W1, False, False)
-        for k in range(16):
-            mm(P(mb, k, 144, 18), ap(mn, k, 2048, 16), W2 if h in AV else W1, False, False)
+            run += [(P(mb, 17, 144, 18, p0, p1), ap(xo, lo + p0, lo + p1), W2, False, False) for p0, p1 in spans(modes, "V")]
+            run += [(P(mb, 16, 144, 18, p0, p1), ap(xo, lo + p0, lo + p1), W1, False, False) for p0, p1 in spans(modes, "V")]
+            run += [(P(mb, 16, 144, 18, p0, p1), ap(xo, lo + p0, lo + p1), W1n, False, False) for p0, p1 in spans(modes, "S")]
+        mms(run)
+        mm(P(mb, 144, 288), ap("hf", lo, hi), ap("DN"), False, False)
+        gn, mn = compare(h, modes, 0, OPT["gch"], OPT["ach"])
+        if "V" in modes:
+            mms([(P(mb, k, 144, 18), ap(gn, k, 2048, 16), W1n, False, False) for k in range(16)])
+        mms([(P(mb, k, 144, 18), ap(mn, k, 2048, 16), W2 if "V" in modes else W1, False, False) for k in range(16)])
 
     def amend(h, xo, xn, qn):
         lo, hi = 128 * h, 128 * h + 128
         mb = 4 + h
         bu = ap("bu", 8 * h, 8 * h + 8)
         ch, sn = ap("ch", lo, hi), ap("sn", lo, hi)
+        mm(P(2 + h, 0, 128), Ib, ap("NEG", 0, 128), True, False)
         tt(ch, ind(ap("SW", 0, 4096), bu), ap("hf", lo, hi), A.not_equal)
         tt(sn, ind(ap("SW", 0, 4096), bu), ch, A.mult)
-        mm(P(2 + h, 0, 128), Ib, ap("NEG", 0, 128), True, False)
         mm(P(2 + h, 0, 128), ap("BF"), sn, False, True)
         scan(ap("KA", lo, hi), ap("RST", 0, 128), P(2 + h, 0, 128), A.add, A.max)
         su = ap("su", 8 * h, 8 * h + 8)
         cp(su, ap("KA", lo + 15, hi, 16))
-        tt(ap("dd", lo, hi), ind(ap("Gz", 16, 4112), su), ap(xo, lo, hi), A.subtract)
-        act(ap("ja", lo, hi), ap("dd", lo, hi), F.Abs)
-        mm(P(mb, 0, 144), ch, ap("RC"), False, False)
-        mm(P(mb, 16, 144, 18), ch, KC, False, False)
-        mm(P(mb, 160, 288, 18), sn, nGBf, False, False)
-        mm(P(mb, 161, 288, 18), sn, GBf, False, False)
+        apart(OPT["dd"][2], ap("ja", lo, hi), ap("Gz", 16, 4112), su, xo, h, P(2 + h, 128, 256))
+        mms([(P(mb, 0, 144), ch, ap("RC"), False, False), (P(mb, 16, 144, 18), ch, KC, False, False)])
+        mms([(P(mb, 160, 288, 18), sn, nGBf, False, False), (P(mb, 161, 288, 18), sn, GBf, False, False)])
         mm(P(mb, 16, 144, 18), ap("ja", lo, hi), W1, False, True)
-        s0, s1 = 144 * h, 144 * h + 144
-        scan(ap("us", s0, s1), ap("DLN"), P(mb, 0, 144), A.add, A.min)
-        tt(ap("nf", s0, s1), ap("us", s0, s1), P(mb, 0, 144), A.not_equal)
-        scan(ap("es", s0, s1), P(mb, 144, 288), ap("nf", s0, s1), A.add, A.mult)
-        tt(ap("em", lo, hi), ind(ap("es", s0, s1), l18), ap("EK", 0, 128), A.mult)
-        mm(P(mb, 256, 264), ap("em", lo, hi), GBf)
-        cp(su, P(mb, 256, 264))
-        tt(ap("dd", lo, hi), ind(ap("Gz"), su), ap(xo, lo, hi), A.subtract)
-        act(ap(xn, lo, hi), ap("dd", lo, hi), F.Abs)
-        act(ap(qn, lo, hi), ap(xn, lo, hi), scale=0.25, bias=191.625)
+        choose(h, mb, mb, 144, 144, ap("DLN"), l18, xo, xn, qn)
+
+    def words(lo, hi, e):
+        w = ap("W", lo, hi)
+        act(ap("sA", lo, hi), e, F.Relu, bias=-0.5, scale=1.0 / 32)
+        act(ap("sB", lo, hi), ap("sA", lo, hi), bias=-5.0 * 2 ** 20, scale=1184.0 * 32)
+        tt(ap("pA", lo, hi), w, ap("sA", lo, hi), A.mult)
+        tt(ap("pC", lo, hi), w, ap("sB", lo, hi), A.add)
+        tt(ap("pD", lo, hi), ap("pA", lo, hi), ap("pC", lo, hi), A.add)
+        ts(w, ap("pD", lo, hi), 4095 * 32, A.bitwise_and)
 
     def nextx():
-        xo, qo = "x%d" % (xv[0] % 4), "q%d" % (qv[0] % 2)
+        xo, qo = "x%d" % (xv[0] % 4), "q%d" % (qv[0] % 3)
         xv[0] += 1
         qv[0] += 1
-        return xo, "x%d" % (xv[0] % 4), qo, "q%d" % (qv[0] % 2)
+        return xo, "x%d" % (xv[0] % 4), qo, "q%d" % (qv[0] % 3)
 
+    half = [(128 * h, 128 * h + 128) for h in range(2)]
     for t in range(TR):
         fin = t == TR - 1
         for s in range(ST):
             xo, xn, qo, qn = nextx()
-            early = AHEAD and t > 0 and s == 0
+            early = t > 0 and s == 0
             for h in range(2):
                 low[0] = "AB"[h] + str(s)
                 if early:
                     low[0] = "CD"[h]
                     amend(h, xo, xn, qn)
                 else:
-                    step_half(h, s == ST - 1, xo, xn, qo, qn)
+                    step_half(h, s == ST - 1, t == 0 and s < OPT["raw"], xo, xn, qo, qn)
+                if fin and h == 1 and s < 2:
+                    low[0] = "y"
+                    for j in range(sum(OPT["ys"][:s]), sum(OPT["ys"][:s + 1])):
+                        sums(j, (6, 7, 0, 1)[j % 4] if s == 0 else j % 2)
+                if t == 0 and s == 0 and h == 0:
+                    low[0] = "s"
+                    store()
             low[0] = "w%d" % s
-            if t == 0 and s == 0:
-                store(0)
-                store(1)
-                share("XW", 0, H, 524e3)
-            e = ap("es", 17, 288, 18) if early else ap("es", 16, 272, 17)
-            act(ap("sA"), e, F.Relu, bias=-16.0)
-            act(ap("sB"), e, F.Relu, bias=-592.0, scale=37.0)
-            tt(ap("pA"), W, ap("sA"), A.mult)
-            tt(ap("pC"), W, ap("sB"), A.add)
-            ts(ap("pB"), ap("pA"), 5, A.arith_shift_right)
-            tt(ap("pD"), ap("pB"), ap("pC"), A.add)
-            ts(W, ap("pD"), 4095, A.bitwise_and)
+            n = 18 if early else 17
+            if s == ST - 1 and OPT["splitw"] and not fin:
+                for h in range(2):
+                    words(8 * h, 8 * h + 8, ap("es", 8 * n * h + n - 1, 8 * n * (h + 1), n))
+            else:
+                words(0, 16, ap("es", n - 1, 16 * n, n))
+        ql = qo
         xo, xn, qo, qn = nextx()
         x = ap(xo)
-        if fin:
-            low[0] = "y"
-            for j in range(8):
-                sums(j)
-        low[0] = "r"
-        act(ap("hm"), ind(ap("SW", 0, 4096), ap("bu")))
-        for m in range(16):
-            mm(P(2, 0, 16), ap("Aw", 159 - m, 287 - m), ap(qo, m, 256, 16), m == 0, m == 15)
-        for h in range(2):
-            mm(P(2, 16 + 8 * h, 24 + 8 * h), ap(qo, 128 * h, 128 * h + 128), cblk)
-        tt(ap("fj"), P(2, 0, 32), ap("CA", 32, 64), A.subtract)
-        ts(ap("fk"), ap("fj"), 4095, A.bitwise_and)
-        ts(ap("fy"), ap("fk"), 4097.0, A.mult)
-        ts(ap("fx"), ap("fy"), 2, A.arith_shift_right, 4095, A.bitwise_and)
-        cp(ap("fu"), ap("fx", 0, 16))
-        idx = ap("fx", 16, 32)
-        ts(ap("own"), ap("fj", 16, 32), 3, A.bitwise_and)
-        XWw = ap("XW", 0, 4096)
-        tt(ap("xa"), ind(XWw, ap("fu")), x, A.subtract)
-        act(ap("pr"), ind(XWw, ap("fu")))
-        act(ap("ad"), ap("xa"), F.Abs)
-        tt(ap("oh"), ind(ap("own"), l4), ap("dc"), A.is_equal)
-        mm(P(6, 0, 32), LT, ap("oh", 0, 32))
-        mm(P(6, 32, 64), LT, ap("oh", 32, 64), True, False)
-        mm(P(6, 32, 64), ones, ap("oh", 0, 32), False, True)
-        ts(ap("le"), P(6, 0, 64), CAP + 0.5, A.is_lt)
-        tt(ap("iq"), ap("le"), ap("oh"), A.mult)
-        tt(ap("th"), ap("iq"), ap("thr"), A.mult)
-        tt(ap("ta"), ap("th", 0, 64, 2), ap("th", 1, 64, 2), A.add)
-        tt(ap("tb"), ap("ta", 0, 32, 2), ap("ta", 1, 32, 2), A.add)
-        ts(ap("we", 0, 256, 16), W, -2047.5, A.add, 1.0 / FR, A.mult)
-        mm(P(7, 0, 256), Ib, x, True, False)
-        for h in range(2):
-            mm(P(7, 128 * h, 128 * h + 128), ap("we", 128 * h, 128 * h + 128), If, False, h == 1)
-        act(ap("PAY", 1024 * t + 256 * rank, 1024 * t + 256 * rank + 256), P(7, 0, 256))
-        share("PAY", 1024 * t, 256, 131e3)
-        low[0] = "J"
-        tt(ap("jm"), ind(W, lc), ap("EK", 0, 256), A.mult)
-        for h in range(2):
-            lo, hi = 128 * h, 128 * h + 128
-            mm(P(4 + h, 256, 264), ap("jm", lo, hi), GBf)
+        for h, (lo, hi) in enumerate(half):
+            low[0] = "JK"[h]
+            tt(ap("jm", lo, hi), ind(ap("W", 8 * h, 8 * h + 8), ap("ls", 0, 8)), ap("EK", 0, 128), A.mult)
+            mm(P(4 + h, 416, 424), ap("jm", lo, hi), GBf)
             su = ap("su", 8 * h, 8 * h + 8)
-            cp(su, P(4 + h, 256, 264))
-            tt(ap("dd", lo, hi), ind(ap("Gz", 16, 4112), su), ap(xo, lo, hi), A.subtract)
-            act(ap("ja", lo, hi), ap("dd", lo, hi), F.Abs)
+            ts(su, P(4 + h, 416, 424), 1.0 / 32, A.mult)
+            apart(OPT["dd"][3], ap("ja", lo, hi), ap("Gz", 16, 4112), su, xo, h, P(4 + h, 0, 128))
             act(ap(xn, lo, hi), ap("ja", lo, hi), scale=-1.0, bias=63.0)
             if not fin:
                 act(ap(qn, lo, hi), ap("ja", lo, hi), scale=-0.25, bias=207.375)
-        if AHEAD and not fin:
-            for h in range(2):
                 low[0] = "EF"[h]
                 ahead(h, xn, qn)
+        if fin:
+            low[0] = "y"
+            for j in range(sum(OPT["ys"][:2]), 8):
+                sums(j, (0, 1, 0, 1, 4, 5, 0, 1)[j])
         low[0] = "r"
-        mm(P(2, 0, 16), ap("nIf"), ap("we", 0, 256, 16), True, False)
-        for h in range(2):
-            mm(P(2, 8 * h, 8 * h + 8), ap("pr", 128 * h, 128 * h + 128), S0f, False, h == 1)
-        ts(ap("t1"), P(2, 0, 16), MAGIC, A.add, MAGIC, A.subtract)
-        tt(ap("ne"), P(2, 0, 16), ap("t1"), A.not_equal)
-        tt(ap("t2"), P(2, 0, 16), ap("t1"), A.subtract)
-        vt = ap("vt")
-        act(ap("isq", 16, 32), ap("t2"), scale=FR)
-        tt(vt, ap("isq", 16, 32), W, A.add)
-        for h in range(2):
-            mm(P(3, 256 + 8 * h, 264 + 8 * h), ap("ad", 128 * h, 128 * h + 128), GBb)
-        tt(ap("e1"), idx, DT2, A.subtract)
-        ts(ap("isq", 0, 16), ap("tb"), 0.25, A.is_gt)
-        tt(ap("e2"), ap("isq", 0, 16), ap("e1"), A.mult)
-        tt(ap("base"), ap("e2"), DT, A.add)
-        tt(ap("bD"), ap("bI", 8, 24), DT, A.subtract)
-        tt(ap("e3"), ap("ne"), ap("bD"), A.mult)
-        tt(ap("dl"), ap("e3"), ap("e1"), A.subtract)
-        tt(ap("kn"), P(3, 256, 272), ap("tb"), A.is_lt)
-        tt(ap("k1"), ap("kn"), ap("dl"), A.mult)
-        key = ap("key")
-        tt(key, ap("k1"), ap("base"), A.add)
-        tt(ap("za"), vt, W, A.mult)
-        tt(ap("zc"), vt, W, A.add)
-        ts(ap("zb"), ap("za"), 5, A.arith_shift_right)
-        tt(ap("za"), ap("zb"), ap("zc"), A.add)
-        ts(ap("zb"), ap("za"), 4095, A.bitwise_and)
-        cp(ap("zf"), ap("zb"))
-        act(ap("EB"), ind(key, lc))
-        tt(ap("EM"), ind(key, lc), ap("EK", 0, 256), A.mult)
-        for h in range(2):
-            mm(P(2, 128 * h, 128 * h + 128), ap("EB", 128 * h, 128 * h + 128), If)
-        for h in range(2):
-            mm(P(6, 8 * h, 8 * h + 8), ap("EM", 128 * h, 128 * h + 128), GBf)
-        cp(ap("kR"), P(2, 0, 256))
-        act(ap("kO"), P(6, 0, 16))
-        act(ap("ZB"), ind(ap("zf"), lc))
+        modulo(OPT["modr"], 2, 16, 1, CF, 144, 16, (qo, 0, 256), 2, ap("fu"))
+        for h, (lo, hi) in enumerate(half):
+            mms([(P(6, 16 + 8 * h, 24 + 8 * h), n192, cblk, True, False), (P(6, 16 + 8 * h, 24 + 8 * h), ap(qo, lo, hi), cblk, False, True)])
+        affine(OPT["rnd"], ap("rf", 16, 32), P(6, 16, 32), 2.0 ** -12, FLO)
+        if OPT["xa"] == "V":
+            tt(ap("xa"), ind(ap("XW", 0, 4096), ap("fu")), x, A.subtract)
+            act(ap("ad"), ap("xa"), F.Abs, bias=-UP)
+        else:
+            mm(P(2, 256, 512), nIb, x, True, False)
+            act(ap("xa"), ind(ap("XW", 0, 4096), ap("fu")))
+            mm(P(2, 256, 512), If, ap("xa"), False, True)
+            act(ap("ad"), P(2, 256, 512), F.Abs)
+        run = [(P(3, 0, 64), n200, c4, True, False)] + [(P(3, 32 * h, 32 * h + 32), ap(qo, lo, hi), ap("c4", 0, 32), False, False) for h, (lo, hi) in enumerate(half)]
+        mms(run[:2] + [run[2][:4] + (True,)])
+        affine(OPT["rnd"], ap("r4"), P(3, 0, 64), 1.0, 758.5)
+        mms(run + [(P(3, 0, 64), nIb, ap("r4"), False, True)])
+        tt(ap("oh"), P(3, 0, 64), ap("dc"), A.is_equal)
+        mms([(P(6, 0, 32), LT, ap("oh", 0, 32), True, True), (P(6, 32, 64), LT, ap("oh", 32, 64), True, False),
+             (P(6, 32, 64), ones, ap("oh", 0, 32), False, True)])
+        ts(ap("iq"), P(6, 0, 64), 0.5 - 256 + CAP - 1, A.is_lt)
+        tt(ap("th"), ap("iq"), ap("thr"), A.mult)
+        ts(ap("wd", 0, 16), W, 5, A.arith_shift_right, 63, A.bitwise_and)
+        ts(ap("wd", 16, 32), W, 11, A.arith_shift_right)
+        we = [ap("we", j, 256, 16) for j in range(2)]
+        for j in range(2):
+            ts(we[j], ap("wd", 16 * j, 16 * j + 16), 1.0 / 256, A.mult, -0.125, A.add)
+        cp(ap("wz", 16, 32), W)
+
+        def payload():
+            mms([(P(7, 0, 256), Ib, x, True, False)] + [(P(7, lo, hi), ap("we", lo, hi), Ib, False, h == 1) for h, (lo, hi) in enumerate(half)])
+            act(ap("PAY", 1024 * t + 256 * rank, 1024 * t + 256 * rank + 256), P(7, 0, 256), bias=UP)
+            share("PAY", 1024 * t, 256, 256)
+
+        if fin or not OPT["paylate"]:
+            payload()
+        act(ap("wz", 0, 16), ap("wz", 16, 32), scale=1.0 / 1024)
+        act(ap("wz", 32, 48), ap("wz", 16, 32), scale=2.0, bias=-2.0 ** 19)
+        mms([(P(6, 64, 112), If, ap("CAT"), True, False)]
+            + [(P(6, 64 + 24 * h, 88 + 24 * h, 3), ap(ql, lo, hi), ablk, False, False) for h, (lo, hi) in enumerate(half)]
+            + [(P(6, 64 + 24 * h, 88 + 24 * h, 3), n12, ap("rr", 16 * h + 8, 16 * h + 16), False, False) for h in range(2)]
+            + [(P(6, 66 + 24 * h, 88 + 24 * h, 3), ap(qo, lo, hi), cblk, False, False) for h, (lo, hi) in enumerate(half)]
+            + [(P(6, 66, 112, 3), n12, ap("rf", 16, 32), False, False)])
+        mms([(P(6, 66, 112, 3), n17, cube("iq", 0, 2, 8 * d, 8 * d + 8), False, d == 3) for d in range(N)])
+        affine("S" if fin else OPT["d1"], ap("D1"), P(6, 64, 112), 1.0, 0.0)
+        mms([(P(7, 256, 288), zeros, ap("R", 0, 32), True, False)] + [(P(7, 256 + j, 288, 2), n8, we[j], False, False) for j in range(2)])
+        mms([(P(7, 256 + 16 * h, 272 + 16 * h), ap("xa", lo, hi), S2, False, h == 1) for h, (lo, hi) in enumerate(half)])
+        r1, r2 = ap("r1", 0, 32), ap("r2", 0, 32)
+        ts(r1, P(7, 256, 288), MAGIC, A.add, MAGIC, A.subtract)
+        ts(r2, P(7, 256, 288), 256 * MAGIC, A.add, 256 * MAGIC, A.subtract)
+        tt(ap("ne"), r1, r2, A.not_equal)
+        tt(ap("rd", 0, 32), r1, r2, A.subtract)
+        mms([(P(3, 64, 112), ones, ap("CD"), True, False)]
+            + [(P(3, 66, 112, 3), n17, cube(nm, 0, 2, 8 * d, 8 * d + 8), False, False) for nm in ("iq", "th") for d in range(N)])
+        mms([(P(3, 66 + 24 * h, 88 + 24 * h, 3), ap("ad", lo, hi), G17, False, False) for h, (lo, hi) in enumerate(half)])
+        mms([(P(3, 65, 112, 3), n17, ap("ne", j, 32, 2), False, j == 1) for j in range(2)])
+        scan(ap("key"), P(3, 64, 112), ap("D1"), A.max, A.min)
         mm(P(3, 0, 256), Ib, ap("NEG"), True, False)
-        for h in range(2):
-            mm(P(3, 128 * h, 128 * h + 128), ap("EB", 128 * h, 128 * h + 128), If, False, False)
-        mm(P(7, 0, 256), ap("nIf"), ap("hm"), True, False)
-        for h in range(2):
-            mm(P(7, 128 * h, 128 * h + 128), ap("ZB", 128 * h, 128 * h + 128), If, False, h == 1)
+        tt(ap("EM"), ind(ap("key"), l3), ap("EK", 0, 256), A.mult)
+        mms([(P(6, 8 * h, 8 * h + 8), ap("EM", lo, hi), GBf, True, True) for h, (lo, hi) in enumerate(half)])
+        kO = ap("KO", 15, 256, 16)
+        affine(OPT["ko"], kO, P(6, 0, 16), 1.0, 0.0)
+        for u in range(OPT["ebh"]):
+            w = 16 // OPT["ebh"]
+            o, i = ap("EB", 16 * w * u, 16 * w * (u + 1)), ind(ap("key"), ap("ls", 48 + w * u, 48 + w * (u + 1)))
+            act(o, i) if OPT["eb"][u] == "S" or fin else cp(o, i)
+        for h, (lo, hi) in enumerate(half):
+            mm(P(2, lo, hi), ap("EB", lo, hi), If)
+        cp(ap("kR"), P(2, 0, 256))
+        mm(P(3, 15, 256, 16), If, kO, False, False)
+        mms([(P(7, 288, 320), If, ap("wz", 16, 48), True, False)]
+            + [(P(7, 288 + 16 * u, 304 + 16 * u), (I5, I11)[j], ap("rd", j, 32, 2), False, u + j == 2) for u in range(2) for j in range(2)])
+        tt(ap("za"), P(7, 288, 304), ap("wz", 0, 16), A.mult)
+        tt(ap("zi"), P(7, 304, 320), ap("za"), A.add)
+        ts(ap("zb"), ap("zi"), 5, A.arith_shift_right, 4095, A.bitwise_and)
+        if OPT["zb"] == "V" and not fin:
+            cp(ap("ZB"), ind(ap("zb"), lc))
+        else:
+            cp(ap("zf"), ap("zb"))
+            act(ap("ZB"), ind(ap("zf"), lc))
+        for h, (lo, hi) in enumerate(half):
+            mms([(P(7, lo, hi), nIf, ap("hl", lo, hi), True, False), (P(7, lo, hi), ap("ZB", lo, hi), If, False, True)])
         for c in range(16):
-            ts(ap("E", 256 * c + 16 * c, 256 * c + 256), ap("kR", 16 * c, 256), ap("kO", c, c + 1), A.is_equal)
-            mm(P(3, 16 * c, 16 * c + 16), LTB, ap("E", 272 * c, 272 * c + 16), False, c == 15)
-            if c < 15:
-                mm(P(3, 16 * c + 16, 256), BDB, ap("E", 272 * c + 16, 256 * c + 256), False, False)
+            ts(ap("E", 256 * c, 256 * c + 256 - 16 * c), ap("kR", 16 * c, 256), ap("KO", 16 * c + 15, 16 * c + 16), A.is_equal)
+            if c + 1 in OPT["ecut"]:
+                c0 = max([e for e in (0,) + OPT["ecut"] if e <= c])
+                mms([(P(3, 16 * e + 16, 256), BDB, ap("E", 256 * e + 16, 256 * e + 256 - 16 * e), False, False) for e in range(c0, min(c + 1, 15))]
+                    + [(P(3, 16 * c0, 16 * c + 16), LTB, cube("E", c0, c + 1, 0, 16), False, c == 15)])
         tt(ap("zm"), P(7, 0, 256), ap("EK", t, t + 256), A.mult)
-        scan(ap("K"), ap("RST"), P(3, 0, 256), A.add, A.max)
+        scan(ap("K"), ap("KO"), P(3, 0, 256), A.add, A.max)
         Kd = ap("K", 15, 256, 16)
         tt(ap("oS"), Kd, dumO, A.min)
         oU = ap("oU", 16 * t, 16 * t + 16)
         cp(oU, ap("oS"))
         if not fin:
-            tt(ind(ap("SW"), oU), ap("zm"), ap("hm"), A.add)
-        mw = 16 if fin else 48
-        mb = 192 * t + mw * rank
-        ts(ap("oa"), Kd, 8192.0, A.is_lt, BIGK, A.mult)
-        tt(ap("ob"), ap("oa"), Kd, A.add)
-        tt(ap("MET", mb, mb + 16), ap("ob"), dumX, A.min)
+            tt(ind(ap("SW"), oU), ap("zm"), ap("hl"), A.add)
+        low[0] = "m"
+        if not fin and OPT["paylate"]:
+            payload()
+        mb = 320 * t + 80 * rank
+        act(ap("ab"), Kd, F.Abs, bias=-CS)
+        tt(ap("MET", mb, mb + 16), ap("ab"), dumO, A.min)
         if not fin:
-            tt(ap("k4"), ind(ap("kn"), l4), ap("iq"), A.mult)
-            mm(P(6, 0, 32), ones, ap("k4", 0, 32), True, False)
-            mm(P(6, 0, 32), ones, ap("k4", 32, 64), False, True)
-            act(ap("MET", mb + 16, mb + 48), P(6, 0, 32))
-        share("MET", 192 * t, mw, 512 * mw)
+            mms([(P(6, 128, 192), nIb, ap("th"), True, False), (P(6, 128, 192), nIb, ap("iq"), False, False)]
+                + [(P(6, 128 + 32 * h, 160 + 32 * h), ap("ad", lo, hi), G4, False, h == 1) for h, (lo, hi) in enumerate(half)])
+            ts(ap("k4"), P(6, 128, 192), -0.5, A.is_lt)
+            mms([(P(6, 0, 64), ones, ap("k4"), True, False), (P(6, 0, 32), ones, ap("k4", 32, 64), False, False),
+                 (P(6, 32, 64), ones, ap("k4", 0, 32), False, True)])
+            act(ap("MET", mb + 16, mb + 80), P(6, 0, 64))
+        share("MET", 320 * t, 80, 16 if fin else 80)
         if fin:
-            mm(P(7, 0, 256), ap("kw"), ap("hm"), True, False)
+            mm(P(7, 0, 256), ap("kw"), ap("hl"), True, False)
             mm(P(7, 0, 256), ap("kw"), ap("zm"), False, True)
             act(ap("yn"), P(7, 0, 256))
             cp(ind(ap("YH"), oU), ap("yn"))
-        ts(ap("mu", 0, 4 * mw), ap("MET", 192 * t, 192 * t + 4 * mw), 8192.0, A.subtract)
+        cp(ap("mu"), cube("MET", 4 * t, 4 * t + 4, 0, 16))
         for a in range(N - 1, -1, -1):
-            w = 16 if fin else 16 // PIECES
+            w = 16 if fin else 16 // OPT["pieces"]
             for u in range(0, 16, w):
                 p0 = 1024 * t + 256 * a + 16 * u
-                cp(ind(ap("XW"), ap("mu", mw * a + u, mw * a + u + w)), ap("PAY", p0, p0 + 16 * w))
+                o, i = ind(ap("XW"), ap("mu", 16 * a + u, 16 * a + u + w)), ap("PAY", p0, p0 + 16 * w)
+                if fin or OPT["xw"][a] == "V":
+                    cp(o, i)
+                else:
+                    add("S", [lambda o=o, i=i: g.scalar.activation(o[0], i[0], F.Silu)], [o], [i], 65 + 3.2 * o[2])
         if not fin:
-            c = [ap("MET", 192 * t + 48 * a + 16, 192 * t + 48 * a + 48) for a in range(N)]
-            tt(ap("ca"), c[0], c[1], A.add)
-            tt(ap("ta"), c[2], c[3], A.add)
-            tt(ap("ci"), ap("ca"), ap("ta"), A.add)
-            ts(ap("ci"), ap("ci"), 7, A.bitwise_and)
-            for h in range(2):
-                ts(ap("thr", 32 * h, 32 * h + 32), ap("ci"), 0.5, A.add)
+            mms([(P(6, 0, 64), If, ap("MET", 320 * t + 80 * a + 16, 320 * t + 80 * a + 80), a == 0, a == N - 1) for a in range(N)])
+            cp(ap("ci"), P(6, 0, 64))
+            ts(ap("thr"), ap("ci"), 7, A.bitwise_and)
 
+    low[0] = "o"
     dma("Y", T.yx[:], ap(xn), 65e3, False)
-    cp(ap("sA"), W)
-    for h in range(2):
-        mm(P(0, 128 * h, 128 * h + 128, p1=8), ap("sA", 8 * h, 8 * h + 8), If)
+    ts(ap("sA"), W, 1.0 / 32, A.mult)
+    mms([(P(0, lo, hi, p1=8), ap("sA", 8 * h, 8 * h + 8), If, True, True) for h, (lo, hi) in enumerate(half)])
     act(ap("wf", p1=8), P(0, 0, 256, p1=8))
     dma("Y", T.yw[:], ap("wf", p1=8), 8e3, False)
     dma("Y", T.yh[:], ap("YH", 0, 4096, ps=16), 131e3, False)
+    for c in range(0, 8, 2):
+        mms([(P(1, 16 * e, 16 * e + 16), ap("XW", 512 * e + rank, 512 * e + 512, 4), S2, True, True) for e in (c, c + 1)])
+    ts(ap("r1"), P(1, 0, 128), MAGIC, A.add, MAGIC, A.subtract)
+    ts(ap("r2"), P(1, 0, 128), 256 * MAGIC, A.add, 256 * MAGIC, A.subtract)
+    tt(ap("rd"), ap("r1"), ap("r2"), A.subtract)
+    for u in range(2):
+        mms([(P(2 + u, 128 * c, 128 * c + 128, p1=8), ap("rd", 64 * u + 16 * c + j, 64 * u + 16 * c + 16, 2), (I5, I11)[j], j == 0, j == 1)
+             for c in range(4) for j in range(2)])
+        affine("SV"[u], ap("yv8", 512 * u, 512 * u + 512, p1=8), P(2 + u, 0, 512, p1=8), 1.0 / 32, 2080.0)
+    dma("S", T.yv[:], ap("yv8", p1=8), 32e3, False)
     for j in range(4):
         lo, hi = 256 * j, 256 * j + 256
-        src = ap("XW", H * rank + lo, H * rank + hi)
-        ts(ap("xs", lo, hi), src, MAGIC, A.add, MAGIC, A.subtract)
-        mm(P(j % 2, 0, 256, p1=8), S0f, src, True, False)
-        mm(P(j % 2, 0, 256, p1=8), nS0, ap("xs", lo, hi), False, True)
-        act(ap("yv8", lo, hi, p1=8), P(j % 2, 0, 256, p1=8), scale=FR, bias=2047.5)
+        src = ap("XW", 4 * lo + rank, 4 * hi, 4)
+        if OPT["ys8"][j] == "V":
+            ts(ap("xs", lo, hi), src, MAGIC, A.add, MAGIC + UP, A.subtract)
+        else:
+            act(ap("PAY", lo, hi), src, bias=MAGIC)
+            act(ap("xs", lo, hi), ap("PAY", lo, hi), bias=-MAGIC - UP)
         if j % 2 == 1:
             dma("Y", T.ys[:, lo - 256:hi], ap("xs", lo - 256, hi), 131e3, False)
-    dma("Y", T.yv[:], ap("yv8", p1=8), 32e3, False)
     return ops
-
-
-def schedule(ops):
-    n = len(ops)
-    succ = [[] for _ in range(n)]
-    for i, o in enumerate(ops):
-        for j in o["deps"]:
-            succ[j].append(i)
-    bl = [0.0] * n
-    for i in range(n - 1, -1, -1):
-        o = ops[i]
-        bl[i] = o["dur"] + max([0.0] + [bl[k] + ((HOP + o["lat"]) if ops[k]["deps"][i] else 0.0) for k in succ[i]] + [o["lat"]])
-    left = [len(o["deps"]) for o in ops]
-    rdy = [0.0] * n
-    ready = {}
-    for i in range(n):
-        if left[i] == 0:
-            ready.setdefault(ops[i]["eng"], []).append(i)
-    free = {}
-    order = []
-    fin = [0.0] * n
-    while len(order) < n:
-        best = None
-        for e, lst in ready.items():
-            if lst:
-                t0 = max(free.get(e, 0.0), min(rdy[i] for i in lst))
-                if best is None or t0 < best[0]:
-                    best = (t0, e)
-        t0, e = best
-        lst = ready[e]
-        i = max([k for k in lst if rdy[k] <= t0], key=lambda k: (bl[k], -k))
-        late = [k for k in lst if t0 < rdy[k] < t0 + LOOK * ops[i]["dur"] and bl[k] > bl[i] + ops[i]["dur"]]
-        if late:
-            i = min(late, key=lambda k: (rdy[k], -bl[k]))
-        lst.remove(i)
-        st = max(t0, rdy[i])
-        end = st + ops[i]["dur"]
-        if e != "X":
-            free[e] = end
-        fin[i] = end + ops[i]["lat"]
-        ops[i]["st"] = st
-        order.append(i)
-        for k in succ[i]:
-            rdy[k] = max(rdy[k], (fin[i] + HOP) if ops[k]["deps"][i] else end)
-            left[k] -= 1
-            if left[k] == 0:
-                ready.setdefault(ops[k]["eng"], []).append(k)
-    return order, max(fin)
 
 
 def place(ops, pred, succ, prio):
@@ -767,7 +856,15 @@ def place(ops, pred, succ, prio):
 
 def schedule(ops):
     n = len(ops)
+    if n in DONE:
+        return DONE[n]
     pred = [[(j, (HOP + ops[j]["lat"]) if w else 0.0) for j, w in o["deps"].items()] for o in ops]
+    for i in range(n):
+        far = {}
+        for k, l2 in pred[i]:
+            for j, l1 in pred[k]:
+                far[j] = max(far.get(j, -1.0), l1 + ops[k]["dur"] + l2)
+        pred[i] = [(j, lag) for j, lag in pred[i] if far.get(j, -1.0) < lag]
     succ = [[] for _ in range(n)]
     for i in range(n):
         for j, lag in pred[i]:
@@ -775,50 +872,161 @@ def schedule(ops):
     bl = [0.0] * n
     for i in range(n - 1, -1, -1):
         bl[i] = ops[i]["dur"] + max([ops[i]["lat"]] + [bl[k] + lag for k, lag in succ[i]])
-    prio = [-bl[i] + 100.0 * (OFF.get(ops[i]["ty"], 0) + OFF.get(ops[i]["low"], 0)) for i in range(n)]
-    best = None
-    for it in range(PASSES):
-        st = place(ops, pred, succ, prio)
-        end = max(st[i] + ops[i]["dur"] + ops[i]["lat"] for i in range(n))
-        if best is None or end < best[0]:
-            best = (end, st)
-        if it == PASSES - 1:
-            break
-        back = place(ops, succ, pred, [-(st[i] + ops[i]["dur"] + ops[i]["lat"]) for i in range(n)])
-        prio = [-(back[i] + ops[i]["dur"]) for i in range(n)]
-    end, st = best
-    if n in DONE:
-        st = place(ops, pred, succ, DONE[n])
-    else:
-        rng = np.random.RandomState(SEED)
-        for it in range(POLISH):
-            a, w, sg = rng.rand() * end, (2000, 4000, 8000)[rng.randint(3)], (150, 400, 1000)[rng.randint(3)]
-            z = rng.randn(n).tolist()
-            s2 = place(ops, pred, succ, [s + sg * z[i] if a < s < a + w and ops[i]["eng"] != "P" else s for i, s in enumerate(st)])
-            e2 = max(s2[i] + ops[i]["dur"] + ops[i]["lat"] for i in range(n))
-            if e2 <= end:
-                end, st = e2, s2
-        if POLISH:
-            DONE[n] = st
-    for i in range(n):
-        ops[i]["st"] = st[i]
-    return sorted(range(n), key=lambda i: (st[i], i)), end
+
+    def length(st):
+        return max(st[i] + ops[i]["dur"] + ops[i]["lat"] for i in range(n))
+
+    kinds = [(o["low"], o["low"] + o["eng"] + o["nm"][0][:2]) for o in ops]
+    names = sorted({a for a, b in kinds}) * 4 + sorted({b for a, b in kinds})
+    nth = [0] * n
+    for i in range(1, n):
+        nth[i] = nth[i - 1] + 1 if ops[i]["low"] == ops[i - 1]["low"] else 0
+    twin = [ops[i]["low"] + str(nth[i]) for i in range(n)]
+    rng = np.random.RandomState(SEED)
+    off, end, st = {}, None, None
+    for it in range(CLIMB + FINE + 1):
+        o2 = dict(off)
+        for _ in range(rng.randint(1, 4) if it else 0):
+            k = names[rng.randint(len(names))] if it <= CLIMB or rng.rand() < 0.2 else twin[rng.randint(n)]
+            o2[k] = o2.get(k, 0) + rng.randn() * (300, 1000, 4000)[rng.randint(3)]
+        s2 = place(ops, pred, succ, [o2.get(kinds[i][0], 0) + o2.get(kinds[i][1], 0) + o2.get(twin[i], 0) - bl[i] for i in range(n)])
+        e2 = length(s2)
+        if end is None or e2 <= end + (WARM * (1.0 - it / (CLIMB + FINE)) * rng.rand() if CLIMB else 0.0):
+            end, st, off = e2, s2, o2
+    end, st = refine(ops, pred, succ, st, rng)
+    DONE[n] = (sorted(range(n), key=lambda i: (st[i], i)), end, st)
+    return DONE[n]
 
 
-PIECES = 4
-AHEAD = 512
-PASSES = 3
-OFF = {'B0':17,'B1':15,'B2':15,'ASgA':-53,'BSgB':12,'ASq0':10,'AVbj':8,'wSYH':26,'BVus':-233,'D':-26,'rVvt':2,'BPps2':12,'AVmA':4,'AVus':-128,'rVfk':-141,'C':-141,'BPps0':-9,'FSmB':37,'rVzc':22,'EShf':48,'rVow':-83,'JSx0':-80,'JVsu':23,'APps1':-157,'EPps0':-114,'FShf':-128,'rSyv':193,'rPps4':6,'BPps1':-1,'ESmA':33,'rVSW':-385,'ASq1':65,'rPps0':5,'rVkR':68,'APps2':-159,'rVwe':-124,'rVoS':48,'DVdd':49,'w0':-6,'FVbj':105,'iVNK':32,'wVpA':-50,'FPps0':11,'AVhu':20,'BSq1':-9,'EVbj':56,'BSx2':-185,'rVYH':121,'BVdd':-57,'A0':-110,'iVIf':48,'iVwe':-194,'AShf':-12,'rVe1':15,'ESxT':45,'rVfu':-65,'AVdd':-3,'BShf':-16,'iVkw':122,'iSYH':65,'rVza':42,'rVne':1,'BSq0':-29,'rVtb':1,'rVe2':-27,'r':1}
-OFF = {'B0':32,'B1':13,'B2':15,'ASgA':-53,'BSgB':14,'ASq0':11,'AVbj':26,'D':-28,'rVvt':2,'BPps2':-52,'AVmA':4,'rVfk':-90,'C':-150,'BPps0':-9,'rVzc':29,'rVow':-9,'APps1':-145,'FShf':-96,'rSyv':178,'rPps4':9,'BPps1':-1,'ESmA':73,'rVSW':-416,'rVkR':77,'DVdd':51,'w0':-23,'FVbj':146,'FPps0':-85,'BSq1':-11,'BSx2':-130,'BVdd':-162,'A0':-293,'iVIf':45,'ESxT':149,'BShf':-38,'rVza':33,'rVne':1,'BSq0':-51,'rVtb':1,'r':-9,'wSsB':18,'wVW':38,'iVR':-16,'BVem':-25,'rVta':2,'rPps2':44,'yPps0':21,'rSkO':85,'w2':-38,'BVhu':-54,'AVes':5,'BVes':-14,'rVzm':86,'w1':-48,'BVsu':-9,'y':16,'J':25,'rVt2':3,'BVmB':8,'JVjm':122,'CPps0':-18,'BVnf':-88}
-OFF = {'B0':32,'B1':16,'B2':15,'ASgA':-161,'BSgB':16,'ASq0':6,'AVbj':25,'D':-24,'rVvt':1,'BPps2':-76,'AVmA':3,'rVfk':-16,'C':-103,'BPps0':-12,'rVzc':15,'rVow':-20,'rSyv':197,'rPps4':8,'BPps1':-69,'ESmA':157,'rVSW':-75,'rVkR':85,'DVdd':51,'w0':-13,'FVbj':253,'FPps0':-41,'BSq1':-173,'BSx2':-240,'BVdd':-129,'ESxT':86,'BSq0':-121,'r':18,'BVem':-7,'rVta':1,'rPps2':64,'yPps0':93,'rSkO':99,'BVhu':-20,'BVes':-91,'w1':-162,'BVsu':-340,'y':-13,'J':25,'rVt2':2,'BVmB':6,'JVjm':125,'CPps0':-226,'BVnf':-37,'rVwe':120,'iVwe':-77,'CVes':77,'iVDL':-98,'rVmu':-95,'iGsT':-130,'rXME':49,'iVGb':36,'iVRC':-69,'i':3,'FSmB':-44,'wVpC':59,'FSgB':-17,'A1':3,'iVnI':-216,'AVdd':7,'wVpB':50,'rVe1':33,'rVdl':-16,'APps0':1,'rVe3':10,'FPps18':27,'rVe2':-89,'BSx1':-124}
-OFF = {'B0':32,'B1':16,'B2':12,'BSgB':11,'ASq0':5,'AVbj':33,'D':-27,'rVvt':63,'BPps2':-121,'AVmA':4,'C':-104,'BPps0':-17,'rVzc':42,'rVow':-156,'rSyv':382,'BPps1':-75,'ESmA':210,'rVSW':-136,'rVkR':119,'DVdd':56,'w0':-9,'FVbj':268,'FPps0':-245,'BSq1':-172,'BSx2':-409,'BVdd':-196,'ESxT':138,'BSq0':-160,'r':16,'BVem':-79,'rVta':75,'yPps0':95,'BVhu':-58,'BVes':-119,'w1':-64,'BVsu':-249,'J':11,'BVmB':4,'JVjm':25,'CPps0':-398,'BVnf':-230,'rVwe':57,'CVes':83,'rXME':38,'iVGb':39,'FSmB':-227,'FSgB':-14,'A1':3,'AVdd':5,'wVpB':21,'rVe1':73,'rVdl':-37,'APps0':-1,'rVe3':71,'rVe2':-88,'BSx1':-42,'rVzm':88,'rVfy':4,'AShf':-52,'A0':-354,'FPps2':32,'BSx3':86,'BSxT':11,'AVnf':-286,'FShf':-116,'BVbI':-75,'CVch':-161,'rVbD':14,'rVzb':47,'E':-46,'iVIb':44,'iVpi':96,'rVfj':85,'JVdd':48,'wSsB':21,'iGvv':-65,'rVth':33,'rPps0':20,'APps1':-238,'BVus':-52,'wVpD':44,'iGR':-167,'iVCR':167,'EVbI':145,'EShf':-218,'BVbu':-12,'rVne':48,'A2':-5,'APps2':-17}
+def refine(ops, pred, succ, st, rng):
+    n = len(ops)
+    dur = [o["dur"] for o in ops]
+    lat = [o["lat"] for o in ops]
+    pm, sm, last = [-1] * n, [-1] * n, {}
+    for i in sorted(range(n), key=lambda i: (st[i], i)):
+        e = ops[i]["eng"]
+        if e != "X":
+            if e in last:
+                pm[i], sm[last[e]] = last[e], i
+            last[e] = i
+    r, q = [0.0] * n, [0.0] * n
+
+    def sweep():
+        left = [len(pred[i]) + (pm[i] >= 0) for i in range(n)]
+        topo = [i for i in range(n) if left[i] == 0]
+        r[:] = [0.0] * n
+        for i in topo:
+            e = r[i] + dur[i]
+            for k, lag in succ[i] + ([(sm[i], 0.0)] if sm[i] >= 0 else []):
+                if r[k] < e + lag:
+                    r[k] = e + lag
+                left[k] -= 1
+                if left[k] == 0:
+                    topo.append(k)
+        if len(topo) < n:
+            return None
+        for i in reversed(topo):
+            t = max(lat[i], q[sm[i]] if sm[i] >= 0 else 0.0)
+            for k, lag in succ[i]:
+                if lag + q[k] > t:
+                    t = lag + q[k]
+            q[i] = t + dur[i]
+        return max(q)
+
+    def guess(seq, a, b):
+        t = r[a] + dur[a] if a >= 0 else 0.0
+        rr, qq, top = {}, {}, 0.0
+        for i in seq:
+            for j, lag in pred[i]:
+                v = rr.get(j, r[j]) + dur[j] + lag
+                if v > t:
+                    t = v
+            rr[i] = t
+            t += dur[i]
+        t = q[b] if b >= 0 else 0.0
+        for i in reversed(seq):
+            t = max(t, lat[i])
+            for k, lag in succ[i]:
+                v = lag + qq.get(k, q[k])
+                if v > t:
+                    t = v
+            t += dur[i]
+            qq[i] = t
+            top = max(top, rr[i] + t)
+        return top
+
+    def link(seq, a, b):
+        for i in seq:
+            pm[i] = a
+            if a >= 0:
+                sm[a] = i
+            a = i
+        sm[a] = b
+        if b >= 0:
+            pm[b] = a
+
+    end = sweep()
+    best, keep = end, (pm[:], sm[:], r[:])
+    barred, stale = {}, 0
+    for it in range(MOVES):
+        i = [k for k in range(n) if q[k] > end - 1e-6][0]
+        runs, cur = [], [i]
+        while i is not None:
+            e = r[i] + dur[i]
+            nx = [k for k, lag in succ[i] if abs(r[k] - e - lag) < 1e-6 and r[k] + q[k] > end - 1e-6]
+            k = sm[i]
+            if k >= 0 and abs(r[k] - e) < 1e-6 and r[k] + q[k] > end - 1e-6 and (not nx or rng.rand() < 0.5):
+                cur.append(k)
+                i = k
+            else:
+                if len(cur) > 1:
+                    runs.append(cur)
+                i = nx[rng.randint(len(nx))] if nx else None
+                cur = [i]
+        moves = []
+        for b in runs:
+            for x in range(len(b) - 1):
+                if rng.rand() > SHARE:
+                    continue
+                for y in range(x + 1, min(x + 4, len(b))):
+                    u, v = b[x], b[y]
+                    if all(q[k] < q[v] for k, lag in succ[u]):
+                        moves.append((b[x + 1:y + 1] + [u], b[x:y + 1], [(w, u) for w in b[x + 1:y + 1]]))
+                    if y - x > 1 and all(r[j] + dur[j] < r[u] + dur[u] for j, lag in pred[v]):
+                        moves.append(([v] + b[x:y], b[x:y + 1], [(v, w) for w in b[x:y]]))
+        moves = [(guess(m[0], pm[m[1][0]], sm[m[1][-1]]),) + m for m in moves if not any(barred.get(p, -1) > it for p in m[2])]
+        if not moves:
+            continue
+        lo = max(min(m[0] for m in moves), end - 1.0 + (SLACK if rng.rand() < 0.1 else 0.0))
+        moves = [m for m in moves if m[0] <= lo + 1e-6]
+        _, seq, old, pairs = moves[rng.randint(len(moves))]
+        a, z = pm[old[0]], sm[old[-1]]
+        link(seq, a, z)
+        end = sweep()
+        if end is None:
+            link(old, a, z)
+            end = sweep()
+            pairs = [(y, x) for x, y in pairs]
+        for x, y in pairs:
+            barred[(y, x)] = it + 20 + rng.randint(20)
+        stale += 1
+        if end < best - 1e-6:
+            best, keep, stale = end, (pm[:], sm[:], r[:]), 0
+        elif stale > 400:
+            pm[:], sm[:] = keep[0], keep[1]
+            end, stale = sweep(), 0
+    return best, keep[2]
+
+
 DONE = {}
 SEED = 1
-POLISH = 3000
-AV = ()
-QV = 0
-BSCAN = 0
-CHUNKS = (512, 512, 512, 512)
+PRUNE = 1
+FINE = 1500
+WARM = 0.0
+CLIMB = 1000
+MOVES = 3500
+SHARE = 0.3
+SLACK = 150.0
 
 
 def rank_program(g, core, T, topo):
@@ -826,7 +1034,7 @@ def rank_program(g, core, T, topo):
     if rank is None:
         return
     ops = build(g, core, T, topo, rank)
-    order, _ = schedule(ops)
+    order = schedule(ops)[0]
     queue = {"V": g.vector, "S": g.scalar, "P": g.tensor, "G": g, "Y": g.sync}
     pos = {i: k for k, i in enumerate(order)}
     need = set()
@@ -840,7 +1048,7 @@ def rank_program(g, core, T, topo):
         o["last"] = list(last.values())
         need.update(o["last"])
     count = {}
-    seen = {}
+    seen, waited = {}, {}
     total = {}
     for i in order:
         o = ops[i]
@@ -848,13 +1056,19 @@ def rank_program(g, core, T, topo):
         if e == "X":
             total[o["tok"][0]] = o["tok"][1]
             continue
-        toks = [ops[j]["tok"] for j, w in o["deps"].items() if w and ops[j]["tok"] is not None and j not in o["last"]]
-        toks += [ops[j]["tok"] for j in o["last"]]
-        for s, v in toks:
-            if seen.get((e, s), 0) < v:
+        know = seen.setdefault(e, {})
+        for j in sorted([j for j, w in o["deps"].items() if w and ops[j]["tok"] is not None], key=lambda j: -pos[j]):
+            s, v = ops[j]["tok"]
+            if know.get(s, 0) < v:
                 queue[e].wait_ge(T.sem[s], v)
-                seen[(e, s)] = v
-        ins = o["fn"]()
+                waited[s] = max(waited.get(s, 0), v)
+                know[s] = v
+                for s2, v2 in ops[j].get("know", {}).items():
+                    know[s2] = max(know.get(s2, 0), v2)
+        if PRUNE:
+            o["know"] = dict(know)
+        for fn in o["fns"]:
+            ins = fn()
         if o["tok"] is not None:
             total[o["tok"][0]] = o["tok"][1]
         elif i in need:
@@ -864,5 +1078,5 @@ def rank_program(g, core, T, topo):
             o["tok"] = (s, count[s])
             total[s] = count[s]
     for s, v in total.items():
-        if seen.get(("G", s), 0) < v:
+        if waited.get(s, 0) < v:
             g.wait_ge(T.sem[s], v)

@@ -1,6 +1,6 @@
 import numpy as np
 from concourse.bass import DstId, RemoteDMATransfer
-from concourse.mybir import AluOpType as A, ActivationFunctionType as F
+from concourse.mybir import AluOpType as A, ActivationFunctionType as F, AxisListType as X
 
 N, Q, H, L, CAP, TR, ST = 4, 4096, 1024, 256, 64, 4, 3
 MAGIC = 12582912.0
@@ -31,7 +31,7 @@ SB = {
     "K": (256, f32), "oS": (16, f32), "oU": (64, u16), "ab": (16, f32), "zm": (256, f32), "yn": (256, f32),
     "k4": (64, b16), "PAY": (4096, f32), "MET": (1280, f32), "mu": (64, u16),
     "jm": (256, f32), "ja": (256, b16), "yv8": (1024, f32),
-    "pi": (4, i32), "pc": (8, f32), "JJ": (272, f32), "EK": (272, f32), "NEG": (256, b16),
+    "pi": (4, i32), "pc": (8, f32), "JJ": (272, f32), "EK": (272, f32), "NK": (272, f32), "hk": (256, f32), "NEG": (256, b16),
     "vv": (136, f32), "v2": (136, f32), "If": (128, f32), "Ib": (1024, b16), "cst": (512, b16),
     "GB": (24, f32), "Gb": (64, b16), "c4": (96, b16),
     "v3": (144, f32), "DN": (144, f32), "DLN": (144, f32), "RC": (144, b16), "CR": (288, b16), "BF": (128, f32), "nIf": (128, f32),
@@ -39,7 +39,7 @@ SB = {
     "BD": (256, b16), "kw": (128, f32), "R": (2048, b16), "DM": (136, f32), "DLT": (136, f32), "RST": (256, f32),
     "ls": (64, u16), "J": (32, f32), "dc": (64, f32), "Aw": (288, b16), "sT": (128, b16), "sU": (256, f32), "j8": (128, f32), "j4": (32, f32),
 }
-CUBE = {"iq": 32, "th": 32, "MET": 80, "E": 256}
+CUBE = {"iq": 32, "th": 32, "MET": 80, "E": 256, "dd": 1}
 SCRATCH, WHERE = {}, {}
 for _k, (_n, _d) in SB.items():
     if _k in CUBE:
@@ -63,7 +63,7 @@ OPT = dict(
     step=("VVVV",) * 4,
     ahead=("SSSS", "SSSS"),
     gch=((0,), (1,), (2,), (3,)), vch=((0,), (1,), (2,), (3,)), ach=((0,), (1,), (2,), (3,)),
-    ecut=(3, 6, 10, 14, 16), xw="SSSS", ys8="VVVS", raw=1, ys=(0, 0, 8), dd="VVVV", xa="V", drow=50, dbw=450.0, scan=1.6, wc=15, vf=30, sf=40, pe=0.4, pl=100.0, gt=1.15, gc=1.25, pp=10, first=4000, schain=1, paylate=0, ser=0, pieces=2, splitw=1, eb="SS", zb="S", d1="V", ebh=1, lay="GGSS", sg="S", hch=(2048, 2048),
+    av=1, qv="V", edone="E", late="VVSS", early=(0,), cnt="S", hk=0, jv="SSSSSSSS", hu="VV", agch=((0,), (1,), (2,), (3,)), ecut=(3, 6, 10, 14, 16), xw="SSSS", ys8="VVVS", raw=1, ys=(0, 0, 8), dd="VVVV", xa="V", drow=50, dbw=450.0, scan=1.6, wc=15, vf=30, sf=70, pe=0.4, pl=100.0, gt=1.15, gc=1.25, pp=10, first=4000, schain=1, paylate=0, ser=0, pieces=2, splitw=1, eb="SS", zb="S", d1="V", ebh=1, lay="GGSS", sg="S", hch=(2048, 2048),
 )
 
 
@@ -322,6 +322,8 @@ def build(g, core, T, topo, rank):
     act(G17, GBf, scale=2.0 ** 17)
     ts(ap("EK"), ap("JJ"), pm, A.is_equal)
     act(ap("NEG"), ap("EK", 0, 256), scale=BG, bias=-BG)
+    if OPT["hk"]:
+        act(ap("NK"), ap("EK"), scale=-1.0, bias=1.0)
     lc, l17, l18, l3 = ap("ls", 0, 16), ap("ls", 16, 24), ap("ls", 32, 40), ap("ls", 48, 64)
     cp(lc, ap("JJ", 0, 16))
     ts(l17, ap("JJ", 0, 8), 17.0, A.mult, 16.0, A.add)
@@ -496,9 +498,9 @@ def build(g, core, T, topo, rank):
                     chain("g", i)
         return gn, mn
 
-    def choose(h, kb, mb, at, n, dl, ll, xo, xn, qn):
+    def choose(h, kb, mb, at, n, dl, ll, xo, xn, qn, s0):
         lo, hi = 128 * h, 128 * h + 128
-        s0, s1 = n * h, n * h + n
+        s1 = s0 + n
         scan(ap("us", s0, s1), dl, P(kb, 0, n), A.add, A.min)
         tt(ap("nf", s0, s1), ap("us", s0, s1), P(kb, 0, n), A.not_equal)
         scan(ap("es", s0, s1), P(mb, at, at + n), ap("nf", s0, s1), A.add, A.mult)
@@ -507,38 +509,49 @@ def build(g, core, T, topo, rank):
         su = ap("su", 8 * h, 8 * h + 8)
         cp(su, P(mb, 416, 424))
         apart(OPT["dd"][0 if n == 136 else 1], ap(xn, lo, hi), ap("Gz"), su, xo, h, P(2 + h, 256, 384))
-        act(ap(qn, lo, hi), ap(xn, lo, hi), scale=0.25, bias=191.625)
+        affine(OPT["qv"], ap(qn, lo, hi), ap(xn, lo, hi), 0.25, 191.625)
 
     def apart(eng, out, win, su, xo, h, bank):
         lo, hi = 128 * h, 128 * h + 128
         if eng == "V":
-            tt(ap("dd", lo, hi), ind(win, su), ap(xo, lo, hi), A.subtract)
-            act(out, ap("dd", lo, hi), F.Abs)
+            d = ap("dd", lo, hi)
+            tt((T["dd"][0:128, lo:hi, 0],) + d[1:], ind(win, su), ap(xo, lo, hi), A.subtract)
+            if OPT["av"]:
+                add("V", [lambda: g.vector.tensor_reduce(out[0], d[0], X.X, A.max, apply_absolute_value=True)], [out], [d], vcost(out, [d], 1))
+            else:
+                act(out, ap("dd", lo, hi), F.Abs)
         else:
             mm(bank, nIb, ap(xo, lo, hi), True, False)
             act(ap("dd", lo, hi), ind(win, su))
             mm(bank, Ib, ap("dd", lo, hi), False, True)
             act(out, bank, F.Abs)
 
-    def step_half(h, last, raw, xo, xn, qo, qn):
+    def step_half(h, last, raw, xo, xn, qo, qn, s0):
         lo, hi = 128 * h, 128 * h + 128
         kb, mb = 2 + h, 4 + h
-        modes = OPT["step"][2 * last + h]
-        mm(P(kb, 256, 384), ap(xo, lo, hi), Ib)
-        act(ap("xT", lo, hi), P(kb, 256, 384))
+        modes = OPT["late"] if s0 == 144 else OPT["step"][2 * last + h]
         bu = ap("bu", 8 * h, 8 * h + 8)
-        modulo(OPT["mod"], mb, 8, 0, AF, 0, 8 * h, (qo, lo, hi), kb, bu)
-        cp(ap("hu", lo, hi), ind(ap("hi" if raw else "SW", 0, 4096), bu))
+        if s0 != 144:
+            mm(P(kb, 256, 384), ap(xo, lo, hi), Ib)
+            act(ap("xT", lo, hi), P(kb, 256, 384))
+            modulo(OPT["mod"], mb, 8, 0, AF, 0, 8 * h, (qo, lo, hi), kb, bu)
+        if raw or OPT["hu"][0] == "V":
+            cp(ap("hu", lo, hi), ind(ap("hi" if raw else "SW", 0, 4096), bu))
+        else:
+            act(ap("hl" if last else "hf", lo, hi), ind(ap("SW", 0, 4096), bu), bias=0.0 if last else 16.0)
+            ts(ap("hu", lo, hi), ap("hl" if last else "hf", lo, hi), 0.0 if last else -16.0, A.add)
         if raw:
             ts(ap("hf", lo, hi), ind(ap("hi"), bu), 16.0, A.add)
             mm(P(mb, 272, 408), ap("hf", lo, hi), ap("DM"))
         elif last:
             mms([(P(mb, 8, 16), n192, ablk, True, False), (P(mb, 8, 16), ap(qo, lo, hi), ablk, False, True)])
             act(ap("rr", 16 * h + 8, 16 * h + 16), P(mb, 8, 16), scale=2.0 ** -12, bias=FLO)
-            act(ap("hl", lo, hi), ind(ap("SW", 0, 4096), bu))
+            if OPT["hu"][0] == "V":
+                act(ap("hl", lo, hi), ind(ap("SW", 0, 4096), bu))
             mms([(P(mb, 272, 408), ones, ap("C16"), True, False), (P(mb, 272, 408), ap("hl", lo, hi), ap("DM"), False, True)])
         else:
-            act(ap("hf", lo, hi), ind(ap("SW", 0, 4096), bu), bias=16.0)
+            if OPT["hu"][0] == "V":
+                act(ap("hf", lo, hi), ind(ap("SW", 0, 4096), bu), bias=16.0)
             mm(P(mb, 272, 408), ap("hf", lo, hi), ap("DM"))
         gn, mn = compare(h, modes, 6 * h, OPT["gch"], OPT["vch"], OPT["byv"][2 * last + h])
         mms([(P(kb, 0, 136), zeros, ap("R", 0, 136), True, False)]
@@ -548,18 +561,18 @@ def build(g, core, T, topo, rank):
             mms([(P(kb, k, 136, 17, p0, p1), ap(gn, 16 * p0 + k, 16 * p1, 16), W1n, False, False) for k in range(16)])
         for p0, p1 in cuts:
             mms([(P(kb, k, 136, 17, p0, p1), ap(mn, 16 * p0 + k, 16 * p1, 16), W2, False, k == 15 and p1 == 128) for k in range(16)])
-        choose(h, kb, mb, 272, 136, ap("DLT"), l17, xo, xn, qn)
+        choose(h, kb, mb, 272, 136, ap("DLT"), l17, xo, xn, qn, s0)
 
     def ahead(h, xo, qo):
         lo, hi = 128 * h, 128 * h + 128
         mb = 4 + h
         modes = OPT["ahead"][h]
         mm(P(mb, 384, 512), ap(xo, lo, hi), Ib)
-        act(ap("xT", lo, hi), P(mb, 384, 512))
+        affine(OPT["jv"][4 + h], ap("xT", lo, hi), P(mb, 384, 512), 1.0, 0.0)
         bu = ap("bu", 8 * h, 8 * h + 8)
         modulo(OPT["moda"], mb, 8, 0, AF, 0, 8 * h, (qo, lo, hi), mb, bu)
-        cp(ap("hu", lo, hi), ind(ap("SW", 0, 4096), bu))
         act(ap("hf", lo, hi), ind(ap("SW", 0, 4096), bu))
+        cp(ap("hu", lo, hi), ind(ap("SW", 0, 4096), bu) if OPT["hu"][1] == "V" else ap("hf", lo, hi))
         run = [(P(mb, 0, 288), ones, ap("CR"), True, False)]
         if "V" not in modes:
             run += [(P(mb, 17, 144, 18), ap(xo, lo, hi), W1, False, False)]
@@ -569,7 +582,8 @@ def build(g, core, T, topo, rank):
             run += [(P(mb, 16, 144, 18, p0, p1), ap(xo, lo + p0, lo + p1), W1n, False, False) for p0, p1 in spans(modes, "S")]
         mms(run)
         mm(P(mb, 144, 288), ap("hf", lo, hi), ap("DN"), False, False)
-        gn, mn = compare(h, modes, 0, OPT["gch"], OPT["ach"])
+        gn, mn = compare(h, modes, 0, OPT["agch"], OPT["ach"])
+        chain(OPT["edone"], len(ops) - 1)
         if "V" in modes:
             mms([(P(mb, k, 144, 18), ap(gn, k, 2048, 16), W1n, False, False) for k in range(16)])
         mms([(P(mb, k, 144, 18), ap(mn, k, 2048, 16), W2 if "V" in modes else W1, False, False) for k in range(16)])
@@ -590,16 +604,22 @@ def build(g, core, T, topo, rank):
         mms([(P(mb, 0, 144), ch, ap("RC"), False, False), (P(mb, 16, 144, 18), ch, KC, False, False)])
         mms([(P(mb, 160, 288, 18), sn, nGBf, False, False), (P(mb, 161, 288, 18), sn, GBf, False, False)])
         mm(P(mb, 16, 144, 18), ap("ja", lo, hi), W1, False, True)
-        choose(h, mb, mb, 144, 144, ap("DLN"), l18, xo, xn, qn)
+        choose(h, mb, mb, 144, 144, ap("DLN"), l18, xo, xn, qn, 144 * h)
 
     def words(lo, hi, e):
         w = ap("W", lo, hi)
-        act(ap("sA", lo, hi), e, F.Relu, bias=-0.5, scale=1.0 / 32)
+        for j, a in enumerate(e):
+            act(ap("sA", lo + j * a[2], lo + (j + 1) * a[2]), a, F.Relu, bias=-0.5, scale=1.0 / 32)
         act(ap("sB", lo, hi), ap("sA", lo, hi), bias=-5.0 * 2 ** 20, scale=1184.0 * 32)
         tt(ap("pA", lo, hi), w, ap("sA", lo, hi), A.mult)
         tt(ap("pC", lo, hi), w, ap("sB", lo, hi), A.add)
         tt(ap("pD", lo, hi), ap("pA", lo, hi), ap("pC", lo, hi), A.add)
         ts(w, ap("pD", lo, hi), 4095 * 32, A.bitwise_and)
+
+    def limits(t):
+        mms([(P(6, 0, 64), If, ap("MET", 320 * t + 80 * a + 16, 320 * t + 80 * a + 80), a == 0, a == N - 1) for a in range(N)])
+        cp(ap("ci"), P(6, 0, 64))
+        ts(ap("thr"), ap("ci"), 7, A.bitwise_and)
 
     def nextx():
         xo, qo = "x%d" % (xv[0] % 4), "q%d" % (qv[0] % 3)
@@ -617,9 +637,13 @@ def build(g, core, T, topo, rank):
                 low[0] = "AB"[h] + str(s)
                 if early:
                     low[0] = "CD"[h]
+                if early and h in OPT["early"]:
                     amend(h, xo, xn, qn)
                 else:
-                    step_half(h, s == ST - 1, t == 0 and s < OPT["raw"], xo, xn, qo, qn)
+                    step_half(h, s == ST - 1, t == 0 and s < OPT["raw"], xo, xn, qo, qn, 144 * h if early else 136 * h)
+                if early and h == 1:
+                    low[0] = "m"
+                    limits(t - 1)
                 if fin and h == 1 and s < 2:
                     low[0] = "y"
                     for j in range(sum(OPT["ys"][:s]), sum(OPT["ys"][:s + 1])):
@@ -631,9 +655,12 @@ def build(g, core, T, topo, rank):
             n = 18 if early else 17
             if s == ST - 1 and OPT["splitw"] and not fin:
                 for h in range(2):
-                    words(8 * h, 8 * h + 8, ap("es", 8 * n * h + n - 1, 8 * n * (h + 1), n))
+                    words(8 * h, 8 * h + 8, [ap("es", 8 * n * h + n - 1, 8 * n * (h + 1), n)])
+            elif early and len(OPT["early"]) < 2:
+                ns = [18 if h in OPT["early"] else 17 for h in range(2)]
+                words(0, 16, [ap("es", 144 * h + ns[h] - 1, 144 * h + 8 * ns[h], ns[h]) for h in range(2)])
             else:
-                words(0, 16, ap("es", n - 1, 16 * n, n))
+                words(0, 16, [ap("es", n - 1, 16 * n, n)])
         ql = qo
         xo, xn, qo, qn = nextx()
         x = ap(xo)
@@ -644,11 +671,17 @@ def build(g, core, T, topo, rank):
             su = ap("su", 8 * h, 8 * h + 8)
             ts(su, P(4 + h, 416, 424), 1.0 / 32, A.mult)
             apart(OPT["dd"][3], ap("ja", lo, hi), ap("Gz", 16, 4112), su, xo, h, P(4 + h, 0, 128))
-            act(ap(xn, lo, hi), ap("ja", lo, hi), scale=-1.0, bias=63.0)
+            affine(OPT["jv"][h], ap(xn, lo, hi), ap("ja", lo, hi), -1.0, 63.0)
             if not fin:
-                act(ap(qn, lo, hi), ap("ja", lo, hi), scale=-0.25, bias=207.375)
+                affine(OPT["jv"][2 + h], ap(qn, lo, hi), ap("ja", lo, hi), -0.25, 207.375)
                 low[0] = "EF"[h]
-                ahead(h, xn, qn)
+                if h in OPT["early"]:
+                    ahead(h, xn, qn)
+                else:
+                    mm(P(4 + h, 384, 512), ap(xn, lo, hi), Ib)
+                    act(ap("xT", lo, hi), P(4 + h, 384, 512))
+                    modulo(OPT["moda"], 4 + h, 8, 0, AF, 0, 8 * h, (qn, lo, hi), 4 + h, ap("bu", 8 * h, 8 * h + 8))
+                    chain("pre", len(ops) - 1)
         if fin:
             low[0] = "y"
             for j in range(sum(OPT["ys"][:2]), 8):
@@ -665,7 +698,7 @@ def build(g, core, T, topo, rank):
             mm(P(2, 256, 512), nIb, x, True, False)
             act(ap("xa"), ind(ap("XW", 0, 4096), ap("fu")))
             mm(P(2, 256, 512), If, ap("xa"), False, True)
-            act(ap("ad"), P(2, 256, 512), F.Abs)
+            act(ap("ad"), P(2, 256, 512), F.Abs, bias=-UP)
         run = [(P(3, 0, 64), n200, c4, True, False)] + [(P(3, 32 * h, 32 * h + 32), ap(qo, lo, hi), ap("c4", 0, 32), False, False) for h, (lo, hi) in enumerate(half)]
         mms(run[:2] + [run[2][:4] + (True,)])
         affine(OPT["rnd"], ap("r4"), P(3, 0, 64), 1.0, 758.5)
@@ -684,13 +717,17 @@ def build(g, core, T, topo, rank):
 
         def payload():
             mms([(P(7, 0, 256), Ib, x, True, False)] + [(P(7, lo, hi), ap("we", lo, hi), Ib, False, h == 1) for h, (lo, hi) in enumerate(half)])
-            act(ap("PAY", 1024 * t + 256 * rank, 1024 * t + 256 * rank + 256), P(7, 0, 256), bias=UP)
+            affine(OPT["jv"][6], ap("PAY", 1024 * t + 256 * rank, 1024 * t + 256 * rank + 256), P(7, 0, 256), 1.0, UP)
             share("PAY", 1024 * t, 256, 256)
 
         if fin or not OPT["paylate"]:
             payload()
-        act(ap("wz", 0, 16), ap("wz", 16, 32), scale=1.0 / 1024)
-        act(ap("wz", 32, 48), ap("wz", 16, 32), scale=2.0, bias=-2.0 ** 19)
+        if OPT["jv"][7] == "V":
+            ts(ap("wz", 0, 16), W, 1.0 / 1024, A.mult)
+            ts(ap("wz", 32, 48), W, 2.0, A.mult, -2.0 ** 19, A.add)
+        else:
+            act(ap("wz", 0, 16), ap("wz", 16, 32), scale=1.0 / 1024)
+            act(ap("wz", 32, 48), ap("wz", 16, 32), scale=2.0, bias=-2.0 ** 19)
         mms([(P(6, 64, 112), If, ap("CAT"), True, False)]
             + [(P(6, 64 + 24 * h, 88 + 24 * h, 3), ap(ql, lo, hi), ablk, False, False) for h, (lo, hi) in enumerate(half)]
             + [(P(6, 64 + 24 * h, 88 + 24 * h, 3), n12, ap("rr", 16 * h + 8, 16 * h + 16), False, False) for h in range(2)]
@@ -722,6 +759,17 @@ def build(g, core, T, topo, rank):
         for h, (lo, hi) in enumerate(half):
             mm(P(2, lo, hi), ap("EB", lo, hi), If)
         cp(ap("kR"), P(2, 0, 256))
+
+        def counts(bk, eng):
+            mms([(P(bk, 128, 192), nIb, ap("th"), True, False), (P(bk, 128, 192), nIb, ap("iq"), False, False)]
+                + [(P(bk, 128 + 32 * h, 160 + 32 * h), ap("ad", lo, hi), G4, False, h == 1) for h, (lo, hi) in enumerate(half)])
+            ts(ap("k4"), P(bk, 128, 192), -0.5, A.is_lt)
+            mms([(P(bk, 0, 64), ones, ap("k4"), True, False), (P(bk, 0, 32), ones, ap("k4", 32, 64), False, False),
+                 (P(bk, 32, 64), ones, ap("k4", 0, 32), False, True)])
+            affine(eng, ap("MET", 320 * t + 80 * rank + 16, 320 * t + 80 * rank + 80), P(bk, 0, 64), 1.0, 0.0)
+
+        if not fin and OPT["cnt"]:
+            counts(2, OPT["cnt"])
         mm(P(3, 15, 256, 16), If, kO, False, False)
         mms([(P(7, 288, 320), If, ap("wz", 16, 48), True, False)]
             + [(P(7, 288 + 16 * u, 304 + 16 * u), (I5, I11)[j], ap("rd", j, 32, 2), False, u + j == 2) for u in range(2) for j in range(2)])
@@ -733,8 +781,15 @@ def build(g, core, T, topo, rank):
         else:
             cp(ap("zf"), ap("zb"))
             act(ap("ZB"), ind(ap("zf"), lc))
+        keep = "hl"
+        if OPT["hk"]:
+            keep = "hk"
+            tt(ap("hk"), ap("hl"), ap("NK", t, t + 256), A.mult)
         for h, (lo, hi) in enumerate(half):
-            mms([(P(7, lo, hi), nIf, ap("hl", lo, hi), True, False), (P(7, lo, hi), ap("ZB", lo, hi), If, False, True)])
+            if OPT["hk"]:
+                mm(P(7, lo, hi), ap("ZB", lo, hi), If)
+            else:
+                mms([(P(7, lo, hi), nIf, ap("hl", lo, hi), True, False), (P(7, lo, hi), ap("ZB", lo, hi), If, False, True)])
         for c in range(16):
             ts(ap("E", 256 * c, 256 * c + 256 - 16 * c), ap("kR", 16 * c, 256), ap("KO", 16 * c + 15, 16 * c + 16), A.is_equal)
             if c + 1 in OPT["ecut"]:
@@ -742,29 +797,24 @@ def build(g, core, T, topo, rank):
                 mms([(P(3, 16 * e + 16, 256), BDB, ap("E", 256 * e + 16, 256 * e + 256 - 16 * e), False, False) for e in range(c0, min(c + 1, 15))]
                     + [(P(3, 16 * c0, 16 * c + 16), LTB, cube("E", c0, c + 1, 0, 16), False, c == 15)])
         tt(ap("zm"), P(7, 0, 256), ap("EK", t, t + 256), A.mult)
-        scan(ap("K"), ap("KO"), P(3, 0, 256), A.add, A.max)
+        chain("pre", scan(ap("K"), ap("KO"), P(3, 0, 256), A.add, A.max))
         Kd = ap("K", 15, 256, 16)
-        tt(ap("oS"), Kd, dumO, A.min)
+        chain("oS", tt(ap("oS"), Kd, dumO, A.min))
         oU = ap("oU", 16 * t, 16 * t + 16)
         cp(oU, ap("oS"))
         if not fin:
-            tt(ind(ap("SW"), oU), ap("zm"), ap("hl"), A.add)
+            chain("SW", tt(ind(ap("SW"), oU), ap("zm"), ap(keep), A.add))
         low[0] = "m"
         if not fin and OPT["paylate"]:
             payload()
         mb = 320 * t + 80 * rank
         act(ap("ab"), Kd, F.Abs, bias=-CS)
         tt(ap("MET", mb, mb + 16), ap("ab"), dumO, A.min)
-        if not fin:
-            mms([(P(6, 128, 192), nIb, ap("th"), True, False), (P(6, 128, 192), nIb, ap("iq"), False, False)]
-                + [(P(6, 128 + 32 * h, 160 + 32 * h), ap("ad", lo, hi), G4, False, h == 1) for h, (lo, hi) in enumerate(half)])
-            ts(ap("k4"), P(6, 128, 192), -0.5, A.is_lt)
-            mms([(P(6, 0, 64), ones, ap("k4"), True, False), (P(6, 0, 32), ones, ap("k4", 32, 64), False, False),
-                 (P(6, 32, 64), ones, ap("k4", 0, 32), False, True)])
-            act(ap("MET", mb + 16, mb + 80), P(6, 0, 64))
+        if not fin and not OPT["cnt"]:
+            counts(6, "S")
         share("MET", 320 * t, 80, 16 if fin else 80)
         if fin:
-            mm(P(7, 0, 256), ap("kw"), ap("hl"), True, False)
+            mm(P(7, 0, 256), ap("kw"), ap(keep), True, False)
             mm(P(7, 0, 256), ap("kw"), ap("zm"), False, True)
             act(ap("yn"), P(7, 0, 256))
             cp(ind(ap("YH"), oU), ap("yn"))
@@ -778,10 +828,6 @@ def build(g, core, T, topo, rank):
                     cp(o, i)
                 else:
                     add("S", [lambda o=o, i=i: g.scalar.activation(o[0], i[0], F.Silu)], [o], [i], 65 + 3.2 * o[2])
-        if not fin:
-            mms([(P(6, 0, 64), If, ap("MET", 320 * t + 80 * a + 16, 320 * t + 80 * a + 80), a == 0, a == N - 1) for a in range(N)])
-            cp(ap("ci"), P(6, 0, 64))
-            ts(ap("thr"), ap("ci"), 7, A.bitwise_and)
 
     low[0] = "o"
     dma("Y", T.yx[:], ap(xn), 65e3, False)
@@ -790,15 +836,16 @@ def build(g, core, T, topo, rank):
     act(ap("wf", p1=8), P(0, 0, 256, p1=8))
     dma("Y", T.yw[:], ap("wf", p1=8), 8e3, False)
     dma("Y", T.yh[:], ap("YH", 0, 4096, ps=16), 131e3, False)
-    for c in range(0, 8, 2):
-        mms([(P(1, 16 * e, 16 * e + 16), ap("XW", 512 * e + rank, 512 * e + 512, 4), S2, True, True) for e in (c, c + 1)])
-    ts(ap("r1"), P(1, 0, 128), MAGIC, A.add, MAGIC, A.subtract)
-    ts(ap("r2"), P(1, 0, 128), 256 * MAGIC, A.add, 256 * MAGIC, A.subtract)
-    tt(ap("rd"), ap("r1"), ap("r2"), A.subtract)
     for u in range(2):
+        mms([(P(6 + u, 16 * e, 16 * e + 16), ap("XW", 2048 * u + 512 * e + rank, 2048 * u + 512 * e + 512, 4), S2, True, True) for e in range(4)])
+    for u in range(2):
+        lo, hi = 64 * u, 64 * u + 64
+        ts(ap("r1", lo, hi), P(6 + u, 0, 64), MAGIC, A.add, MAGIC, A.subtract)
+        ts(ap("r2", lo, hi), P(6 + u, 0, 64), 256 * MAGIC, A.add, 256 * MAGIC, A.subtract)
+        tt(ap("rd", lo, hi), ap("r1", lo, hi), ap("r2", lo, hi), A.subtract)
         mms([(P(2 + u, 128 * c, 128 * c + 128, p1=8), ap("rd", 64 * u + 16 * c + j, 64 * u + 16 * c + 16, 2), (I5, I11)[j], j == 0, j == 1)
              for c in range(4) for j in range(2)])
-        affine("SV"[u], ap("yv8", 512 * u, 512 * u + 512, p1=8), P(2 + u, 0, 512, p1=8), 1.0 / 32, 2080.0)
+        affine("S", ap("yv8", 512 * u, 512 * u + 512, p1=8), P(2 + u, 0, 512, p1=8), 1.0 / 32, 2080.0)
     dma("S", T.yv[:], ap("yv8", p1=8), 32e3, False)
     for j in range(4):
         lo, hi = 256 * j, 256 * j + 256
@@ -893,7 +940,22 @@ def schedule(ops):
         e2 = length(s2)
         if end is None or e2 <= end + (WARM * (1.0 - it / (CLIMB + FINE)) * rng.rand() if CLIMB else 0.0):
             end, st, off = e2, s2, o2
-    end, st = refine(ops, pred, succ, st, rng)
+    mark = [i for i in range(n) if ops[i]["nm"][0] == "xa"]
+    first = [min(i for i in range(n) if ops[i]["low"] == "J" and i > ([0] + mark)[t]) for t in range(TR)]
+    cyc = [sum(1 for f in first if f <= i) - 1 for i in range(n)]
+    for it in range(LAPS):
+        end, st = refine(ops, pred, succ, st, rng)
+        best = st
+        span = [st[mark[t + 1]] - st[mark[t]] for t in range(TR - 1)]
+        for c in range(TR - 1):
+            rel = {twin[i]: st[i] - st[mark[c]] for i in range(n) if cyc[i] == c}
+            prio = [st[i] if cyc[i] < 0 else st[mark[0]] + cyc[i] * span[c]
+                    + (rel.get(twin[i], st[i] - st[mark[cyc[i]]]) if cyc[i] < TR - 1 else st[i] - st[mark[-1]]) for i in range(n)]
+            s2 = place(ops, pred, succ, prio)
+            e2 = length(s2)
+            if e2 < end:
+                end, best = e2, s2
+        st = best
     DONE[n] = (sorted(range(n), key=lambda i: (st[i], i)), end, st)
     return DONE[n]
 
@@ -1021,10 +1083,11 @@ def refine(ops, pred, succ, st, rng):
 DONE = {}
 SEED = 1
 PRUNE = 1
-FINE = 1500
+FINE = 1200
 WARM = 0.0
-CLIMB = 1000
-MOVES = 3500
+LAPS = 10
+CLIMB = 800
+MOVES = 300
 SHARE = 0.3
 SLACK = 150.0
 

import numpy as np
from concourse.bass import DstId, RemoteDMATransfer
from concourse.mybir import AluOpType as A, ActivationFunctionType as F, AxisListType as X

N, Q, H, L, CAP, TR, ST = 4, 4096, 1024, 256, 64, 4, 3
MAGIC = 12582912.0
BIGK = 32768.0
UP = 32.0
BG = 33554432.0
FLO = 191.5 + 2.0 ** -13
TOP = 4096.0 * 192
CS = 16384.0
f32, b16, i32, u16 = "float32", "bfloat16", "int32", "uint16"

SB = {
    "Gz": (4112, b16), "hi": (4096, i32), "SW": (4352, f32), "YH": (4352, f32), "XW": (4352, f32), "SG": (4096, f32),
    "xs": (1024, b16), "vi": (128, i32), "vd": (128, i32), "vb": (128, b16), "vf": (1024, b16), "wd": (32, i32),
    "S2": (16, f32), "r1": (128, f32), "r2": (128, f32), "rd": (128, b16), "wi": (256, i32), "wf": (256, f32),
    "cb": (16, b16), "cf": (8, f32), "cj": (8, i32),
    "x0": (256, b16), "x1": (256, b16), "x2": (256, b16), "x3": (256, b16), "q0": (256, b16), "q1": (256, b16), "q2": (256, b16),
    "xT": (256, b16), "gA": (2048, b16), "gB": (2048, b16), "mA": (2048, b16), "mB": (2048, b16),
    "rr": (32, b16), "rf": (32, b16), "cm": (8, f32), "pf": (32, f32), "rw": (512, b16), "EM": (256, f32), "bj": (32, i32), "bI": (32, i32), "bu": (16, u16),
    "hu": (256, u16), "hf": (256, f32), "hl": (256, f32),
    "us": (288, f32), "nf": (288, f32), "es": (288, f32), "em": (256, f32), "su": (16, u16), "dd": (256, b16),
    "W": (16, i32), "sA": (16, f32), "sB": (16, f32), "pA": (16, f32), "pC": (16, f32), "pD": (16, i32),
    "fu": (16, u16), "r4": (64, b16), "oh": (64, b16), "iq": (64, b16), "th": (64, b16), "thr": (64, i32), "ci": (64, i32),
    "xa": (256, f32), "ad": (256, b16), "we": (256, b16),
    "ne": (32, b16), "D1": (48, f32), "key": (48, f32), "wz": (48, f32),
    "za": (16, f32), "zi": (16, i32), "zb": (16, i32), "zf": (16, f32),
    "EB": (256, f32), "ZB": (256, f32), "KO": (256, f32), "kR": (256, u16), "E": (4096, b16),
    "K": (256, f32), "oS": (16, f32), "oU": (64, u16), "ab": (16, f32), "zm": (256, f32), "yn": (256, f32),
    "k4": (64, b16), "PAY": (4096, f32), "MET": (1280, f32), "mu": (64, u16),
    "jm": (256, f32), "ja": (256, b16), "yv8": (1024, f32),
    "pi": (4, i32), "pc": (8, f32), "JJ": (272, f32), "EK": (272, f32), "NK": (272, f32), "hk": (256, f32), "NEG": (256, b16),
    "vv": (136, f32), "v2": (136, f32), "If": (128, f32), "Ib": (1024, b16), "cst": (512, b16),
    "GB": (24, f32), "Gb": (64, b16), "c4": (96, b16),
    "v3": (144, f32), "DN": (144, f32), "DLN": (144, f32), "RC": (144, b16), "CR": (288, b16), "BF": (128, f32), "nIf": (128, f32),
    "AF": (256, b16), "KA": (256, f32), "ch": (256, b16), "sn": (256, f32), "C16": (136, b16), "CD": (48, b16), "CAT": (48, f32),
    "BD": (256, b16), "kw": (128, f32), "R": (2048, b16), "DM": (136, f32), "DLT": (136, f32), "RST": (256, f32),
    "ls": (64, u16), "J": (32, f32), "dc": (64, f32), "Aw": (288, b16), "sT": (128, b16), "sU": (256, f32), "j8": (128, f32), "j4": (32, f32),
}
CUBE = {"iq": 32, "th": 32, "MET": 80, "E": 256, "dd": 1}
SCRATCH, WHERE = {}, {}
for _k, (_n, _d) in SB.items():
    if _k in CUBE:
        SCRATCH[_k] = ("sbuf", [128, _n // CUBE[_k], CUBE[_k]], _d)
    elif _n <= 64:
        _at = SCRATCH.get("pool_" + _d, ("sbuf", [128, 0], _d))[1][1]
        WHERE[_k] = ("pool_" + _d, _at)
        SCRATCH["pool_" + _d] = ("sbuf", [128, _at + (_n + 31) // 32 * 32], _d)
    else:
        WHERE[_k] = (_k, 0)
        SCRATCH[_k] = ("sbuf", [128, _n], _d)
for _b in range(4):
    SCRATCH["pp%d" % _b] = ("psum", [128, 1024], f32)
NDMA = 40
SEMAPHORES = ["cV", "cS", "cP", "cG"] + ["d%d" % _i for _i in range(NDMA)] + ["ar%d" % _i for _i in range(9)]

HOP = 55.0
OPT = dict(
    mod="I", moda="I", modr="I", rnd="V", ko="V",
    byv=((), (), (), ()), cut=((0, 128),),
    step=("VVVV",) * 4,
    ahead=("SSSS", "SSSS"),
    gch=((0,), (1,), (2,), (3,)), vch=((0,), (1,), (2,), (3,)), ach=((0,), (1,), (2,), (3,)),
    av=1, qv="V", edone="E", late="VVSS", early=(0,), cnt="S", hk=0, jv="SSSSSSSS", hu="VV", agch=((0,), (1,), (2,), (3,)), ecut=(3, 6, 10, 14, 16), xw="SSSS", ys8="VVVS", raw=1, ys=(0, 0, 8), dd="VVVV", xa="V", drow=50, dbw=450.0, scan=1.6, wc=15, vf=30, sf=70, pe=0.4, pl=100.0, gt=1.15, gc=1.25, pp=10, first=4000, schain=1, paylate=0, ser=0, pieces=2, splitw=1, eb="SS", zb="S", d1="V", ebh=1, lay="GGSS", sg="S", hch=(2048, 2048),
)


def build(g, core, T, topo, rank):
    ops = []
    hist = {}
    ndma = [0]
    narr = [0]
    low = ["i"]

    def ap(name, lo=0, hi=None, step=1, p0=0, p1=128, ps=1):
        if hi is None:
            hi = SB[name][0]
        rows = slice(p0, p1, ps) if ps != 1 else slice(p0, p1)
        if name in CUBE:
            w = CUBE[name]
            if lo // w == (hi - 1) // w:
                a = T[name][rows, lo // w, lo % w:lo % w + hi - lo]
            else:
                a = T[name][rows, lo // w:hi // w, 0:w]
            return (a, [(name, lo, hi)], hi - lo, "")
        tn, at = WHERE[name]
        t = T[tn]
        a = t[rows, at + lo:at + hi:step] if step != 1 else t[rows, at + lo:at + hi]
        return (a, [(name, lo, hi)], len(range(lo, hi, step)), "")

    def cube(name, r0, r1, lo, hi):
        w = CUBE[name]
        return (T[name][0:128, r0:r1, lo:hi], [(name, r * w + lo, r * w + hi) for r in range(r0, r1)], (r1 - r0) * (hi - lo), "")

    def P(b, lo, hi, step=1, p0=0, p1=128):
        at = 512 * (b % 2)
        t = T["pp%d" % (b // 2)]
        a = t[p0:p1, at + lo:at + hi:step] if step != 1 else t[p0:p1, at + lo:at + hi]
        return (a, [("ps%d" % (b + j), 0, 512) for j in range((hi + 511) // 512)], len(range(lo, hi, step)), "")

    def ind(w, o):
        return (w[0].indirect(o[0]), w[1], 16 * o[2], "ind", o[1])

    def two(a):
        return a[1][0][0] in SB and SB[a[1][0][0]][1] in (b16, u16)

    def psum(a):
        return a[1][0][0].startswith("ps")

    def add(eng, fns, outs, ins, dur, lat=0.0, tok=None, extra=()):
        i = len(ops)
        deps = {}
        for e in extra:
            deps[e] = True
        acc = []
        for a in outs:
            acc += [(r, True) for r in a[1]]
            if a[3]:
                acc += [(r, False) for r in a[4]]
        for a in ins:
            if isinstance(a, tuple):
                acc += [(r, False) for r in a[1]]
                if a[3]:
                    acc += [(r, False) for r in a[4]]
        for (name, lo, hi), w in acc:
            h = hist.setdefault(name, [])
            if name.startswith("ps"):
                if h and h[-1] != i:
                    j = h[-1]
                    deps[j] = deps.get(j, False) or ops[j]["eng"] != eng
                continue
            for j, l2, h2, w2 in h:
                if j != i and l2 < hi and lo < h2 and (w or w2):
                    deps[j] = True
        for (name, lo, hi), w in acc:
            h = hist[name]
            if name.startswith("ps"):
                h.append(i)
                continue
            if w:
                h[:] = [e for e in h if not (lo <= e[1] and e[2] <= hi)]
            h.append((i, lo, hi, w))
        if dur and any(deps.values()):
            dur += OPT["wc"]
        ops.append(dict(eng=eng, fns=fns, deps=deps, dur=dur, lat=lat, tok=tok, nm=acc[0][0], low=low[0]))
        return i

    prev = {}

    def chain(k, i):
        if k in prev and prev[k] not in ops[i]["deps"]:
            ops[i]["deps"][prev[k]] = False
        prev[k] = i

    def val(s):
        return s[0] if isinstance(s, tuple) else s

    def vcost(o, ins, k):
        if o[3]:
            return 50 + 3.2 * o[2]
        if ins[0][3]:
            return 50 + 1.3 * o[2] * OPT["gt" if k == 2 else "gc"]
        return OPT["vf"] + 0.83 * max(64, k * o[2]) + (OPT["pp"] if any(psum(a) for a in ins) else 0)

    def cp(o, i):
        return add("V", [lambda: g.vector.tensor_copy(o[0], i[0])], [o], [i], vcost(o, [i], 0.5 if two(o) and two(i) else 1))

    def ts(o, i, s1, o0, s2=None, o1=None):
        if o1 is None:
            fn = lambda: g.vector.tensor_scalar(o[0], i[0], val(s1), None, o0)
        else:
            fn = lambda: g.vector.tensor_scalar(o[0], i[0], val(s1), val(s2), o0, o1)
        return add("V", [fn], [o], [i, s1, s2], vcost(o, [i], 0.5 if two(o) and two(i) else 1))

    def tt(o, a, b, op):
        return add("V", [lambda: g.vector.tensor_tensor(o[0], a[0], b[0], op)], [o], [a, b], vcost(o, [a, b], 1 if psum(a) or psum(b) else 2))

    def scan(o, a, b, o0, o1):
        return add("V", [lambda: g.vector.tensor_tensor_scan(o[0], a[0], b[0], 0.0, o0, o1)], [o], [a, b], vcost(o, [a, b], OPT["scan"]))

    def ms(o, c):
        return add("V", [lambda: g.vector.memset(o[0], c)], [o], [], vcost(o, [o], 0.5 if two(o) else 1))

    def act(o, i, func=F.Identity, bias=0.0, scale=1.0):
        return add("S", [lambda: g.scalar.activation(o[0], i[0], func, bias=val(bias), scale=scale)], [o], [i, bias],
                   65 + 1.3 * o[2] if i[3] else OPT["sf"] + 0.83 * max(o[2], 64) + (OPT["pp"] if psum(i) else 0))

    def affine(eng, o, i, scale, bias):
        return act(o, i, bias=bias, scale=scale) if eng == "S" else ts(o, i, scale, A.mult, bias, A.add)

    def mms(lst):
        fns = [(lambda m=m: g.tensor.matmul(m[0][0], m[1][0], m[2][0], m[3], m[4])) for m in lst]
        dur = sum(5 + OPT["pe"] * max(min(64, m[1][2]), m[2][2]) * (1 if two(m[1]) else 4) for m in lst)
        return add("P", fns, [m[0] for m in lst], [a for m in lst for a in m[1:3]], dur, lat=OPT["pl"])

    def mm(o, l, r, st=True, sp=True):
        return mms([(o, l, r, st, sp)])

    def iota(o, pat, base, cm):
        if SB[o[1][0][0]][1] == i32:
            fn = lambda: g.iota(o[0], pat, base, cm)
        else:
            fn = lambda: g.iota(o[0], pat, base, cm, allow_small_or_imprecise_dtypes=True)
        return add("G", [fn], [o], [], 130 + 1.7 * o[2])

    def sel(o, i, pat, op, base, cm):
        return add("G", [lambda: g.affine_select(o[0], i[0], pat, op, 0.0, base, cm)], [o], [i], 170 + 1.7 * o[2])

    def fill(o, c):
        i = ap("R", 0, o[2]) if two(o) else ap("JJ", 0, o[2])
        return add("G", [lambda: g.affine_select(o[0], i[0], [[0, o[2]]], A.is_gt, c, 0, 0)], [o], [i], 170 + 1.7 * o[2])

    dclock = [0.0]

    def dma(eng, o, i, nbytes, load):
        s = "d%d" % ndma[0]
        ndma[0] += 1
        q = g.sync if eng == "Y" else g.scalar
        if load:
            dclock[0] += OPT["drow"] + nbytes / OPT["dbw"]
            return chain(eng, add(eng, [lambda: q.dma_start(o[0], i).then_inc(T.sem[s], 16)], [o], [], 60, lat=1500 + dclock[0], tok=(s, 16)))
        return add(eng, [lambda: q.dma_start(o, i[0]).then_inc(T.sem[s], 16)], [], [i], 60, lat=2300 + nbytes / 300.0, tok=(s, 16))

    others = [c for c in T.cores if c != core]
    common = [e for e in topo.engines(core, others[0]) if all(e in topo.engines(core, c) for c in others)]
    ne = 1
    while ne * 2 <= len(common):
        ne *= 2
    emask = sum(1 << e for e in common[:ne])
    dsts = [DstId(rid=topo.addr(c)[0], pnc=topo.addr(c)[1]) for c in others]

    def share(name, base, pitch, width, after=()):
        s = "d%d" % ndma[0]
        ndma[0] += 1
        r = "ar%d" % narr[0]
        narr[0] += 1
        a = ap(name, base + rank * pitch, base + rank * pitch + width)
        fn = lambda: g.remote_dma_fused([RemoteDMATransfer(dst_ids=dsts, dma_engine_mask=emask, remote_sem=T.sem[r],
                                                           src=a[0], dsts=[a[0]] * len(dsts))], local_sem=T.sem[s])
        i = add("G", [fn], [], [a], 1000, lat=2000 + (OPT["first"] if narr[0] == 1 else 0) + 3 * (256 if two(a) else 512) * width / 150.0,
                tok=(s, ne), extra=after)
        land = [ap(name, base + d * pitch, base + d * pitch + width) for d in range(N) if d != rank]
        add("X", [], land, [], 0, lat=300.0, tok=(r, ne * len(others)), extra=[i])

    dma("Y", ap("cb", 0, 3), T.co[:], 1e3, True)
    dma("Y", ap("x0"), T.xl[:], 65e3, True)
    c0 = 0
    for cw in OPT["hch"]:
        dma("Y", ap("hi", c0, c0 + cw), T.hlp[:, c0:c0 + cw], 512 * cw, True)
        c0 += cw
    dma("Y", ap("Gz", 16, 4112), T.gen[:], 1.05e6, True)
    dma("Y", ap("vi", 0, 64), T.vst[:], 32e3, True)
    dma("Y", ap("xs"), T.xst[:], 262e3, True)
    dma("Y", ap("wi", p1=8), T.wl[:], 8e3, True)

    iota(ap("pi", 0, 2), [[0, 2]], 0, 1)
    iota(ap("JJ"), [[0, 17], [1, 16]], 0, 0)
    ts(ap("pi", 2, 3), ap("pi", 0, 1), 15, A.bitwise_and)
    ts(ap("pi", 3, 4), ap("pi", 1, 2), 4, A.arith_shift_right)
    cp(ap("pc", 0, 2), ap("pi", 2, 4))
    pm, pd = ap("pc", 0, 1), ap("pc", 1, 2)
    ts(ap("pc", 2, 3), pm, 1.0, A.add)
    cp(ap("cf", 0, 3), ap("cb", 0, 3))
    cw_, ca_, cc_ = ap("cf", 0, 1), ap("cf", 1, 2), ap("cf", 2, 3)
    GBf, S0f, nGBf = ap("GB", 0, 8), ap("GB", 8, 16), ap("GB", 16, 24)
    ts(GBf, ap("JJ", 0, 8), pd, A.is_equal)
    W1, W1n, W2, ablk, cblk, G17, nS0, KC = [ap("Gb", 8 * i, 8 * i + 8) for i in range(8)]
    ts(ablk, GBf, ca_, A.mult)
    ts(cblk, GBf, cc_, A.mult)
    ms(ap("Aw"), 0.0)
    cp(ap("Aw", 15, 128, 16), ablk)
    cp(ap("Aw", 159, 272, 16), cblk)
    ones, zeros, n192, n200 = [ap("cst", 128 * i, 128 * i + 128) for i in range(4)]
    ms(ones, 1.0)
    ms(zeros, 0.0)
    ms(n192, -192.0)
    ms(n200, -200.0)
    iota(ap("j8"), [[1, 8], [0, 16]], 0, 0)
    AF, CF = ap("AF", 0, 128), ap("AF", 128, 256)
    ts(AF, ap("j8"), pd, A.is_equal, ca_, A.mult)
    ts(CF, ap("j8"), pd, A.is_equal, cc_, A.mult)
    If, nIf = ap("If"), ap("nIf")
    Ib, nIb, n12, n17, LT, n8, I5, I11 = [ap("Ib", 128 * i, 128 * i + 128) for i in range(8)]
    diag = [[1, 128]]
    sel(Ib, ones, diag, A.is_equal, 0, -1)
    ts(n12, Ib, -4096.0, A.mult)
    iota(ap("yv8", 0, 128), [[1, 128]], 0, 0)
    cp(ap("kR", 0, 128), ap("yv8", 0, 128))
    for j in range(2):
        act(ap("R", 1024 * j, 1024 * j + 1024), ind(Ib, ap("kR", 64 * j, 64 * j + 64)))
    act(If, Ib)
    act(nIf, Ib, scale=-1.0)
    act(I5, Ib, scale=32.0)
    act(I11, Ib, scale=2048.0)
    act(nIb, Ib, scale=-1.0)
    act(n17, Ib, scale=-2.0 ** 17)
    sel(LT, ones, diag, A.is_gt, 0, -1)
    BDB, LTB = ap("BD", 0, 128), ap("BD", 128, 256)
    ts(BDB, ap("j8"), pd, A.is_equal, BIGK, A.mult)
    sel(LTB, BDB, diag, A.is_gt, 0, -1)
    act(n8, Ib, scale=-256.0)
    tt(LT, LT, n8, A.add)
    ts(ap("kw"), ap("j8"), pd, A.is_equal, ap("pc", 2, 3), A.mult)
    act(ap("BF"), BDB, scale=1.0 / BIGK)
    iota(ap("vv"), [[-16, 8], [-1, 17]], 0, 1)
    ts(ap("DM"), ap("vv"), -1.0, A.is_equal)
    ts(ap("v2"), ap("vv"), 0.0, A.is_equal)
    S2 = ap("S2")
    for j in range(2):
        act(ap("S2", j, 16, 2), ap("v2", j, 136, 17), scale=256.0)
    ms(ap("v2", 16, 136, 17), 0.0)
    tt(ap("DM"), ap("DM"), ap("v2"), A.subtract)
    ms(ap("DLT"), -1.0)
    ms(ap("DLT", 0, 136, 17), BG)
    ms(ap("DLT", 16, 136, 17), 16.0)
    ms(ap("Gz", 0, 16), 0.0)
    ts(W1, GBf, cw_, A.mult, 32.0, A.mult)
    act(W1n, W1, scale=-1.0)
    act(W2, W1, scale=2.0)
    act(G17, GBf, scale=2.0 ** 17)
    ts(ap("EK"), ap("JJ"), pm, A.is_equal)
    act(ap("NEG"), ap("EK", 0, 256), scale=BG, bias=-BG)
    if OPT["hk"]:
        act(ap("NK"), ap("EK"), scale=-1.0, bias=1.0)
    lc, l17, l18, l3 = ap("ls", 0, 16), ap("ls", 16, 24), ap("ls", 32, 40), ap("ls", 48, 64)
    cp(lc, ap("JJ", 0, 16))
    ts(l17, ap("JJ", 0, 8), 17.0, A.mult, 16.0, A.add)
    ts(l18, ap("JJ", 0, 8), 18.0, A.mult, 17.0, A.add)
    ts(l3, ap("JJ", 0, 16), 3.0, A.mult, 2.0, A.add)
    ts(ap("J", 0, 16), ap("JJ", 0, 16), 16.0, A.mult, pm, A.add)
    dumO = ap("J", 16, 32)
    act(dumO, ap("J", 0, 16), bias=4096.0)
    iota(ap("dc"), [[0, 2], [1, 4], [0, 8]], -760, 0)
    iota(ap("sU", 0, 128), [[1, 128]], 0, -16)
    ts(ap("sU", 128, 256), ap("sU", 0, 128), -127.0, A.is_equal)
    ts(ap("sU", 0, 128), ap("sU", 0, 128), 0.0, A.is_equal)
    tt(ap("sT"), ap("sU", 0, 128), ap("sU", 128, 256), A.add)
    ts(ap("cj", 0, 1), cc_, 2.0, A.add)
    ts(ap("cj", 1, 2), ap("cj", 0, 1), 3, A.bitwise_and)
    ts(ap("cf", 3, 4), ap("cj", 1, 2), -2.0, A.add)
    iota(ap("j4"), [[0, 4], [1, 8]], 0, 0)
    c4, G4 = ap("c4", 0, 64), ap("c4", 64, 96)
    ts(G4, ap("j4"), pd, A.is_equal)
    for h in range(2):
        ts(ap("c4", 32 * h, 32 * h + 32), G4, ap("cf", 3, 4), A.mult)
    ms = fill
    ms(ap("CD", 0, 48, 3), 2.0 ** 20 / 128)
    ms(ap("CD", 1, 48, 3), 8192.0 / 128)
    ms(ap("CD", 2, 48, 3), 2.0 ** 16 / 128)
    mms([(P(7, 0, 8), n192, ablk, True, True), (P(7, 8, 16), n192, cblk, True, True)])
    for h in range(2):
        act(ap("CAT", 24 * h, 24 * h + 24, 3), P(7, 0, 8), bias=TOP)
        act(ap("CAT", 24 * h + 2, 24 * h + 24, 3), P(7, 8, 16), bias=TOP + CS + 2.0 ** 17)
    ms(ap("CAT", 1, 48, 3), 2.0 ** 20)
    mms([(P(6, 2 * j, 2 * j + 2), (AF, CF)[j], ap("cst", 256, 258), True, True) for j in range(2)])
    for j in range(2):
        act(ap("cm", 4 * j, 4 * j + 1), P(6, 2 * j, 2 * j + 1))
        act(ap("cm", 4 * j + 1, 4 * j + 2), P(6, 2 * j, 2 * j + 1), scale=2.0 ** -12, bias=FLO)
        act(ap("cm", 4 * j + 2, 4 * j + 3), P(6, 2 * j, 2 * j + 1), bias=TOP)
    ms(ap("C16"), 0.0)
    ms(ap("C16", 16, 136, 17), 0.125)
    ts(KC, GBf, pm, A.mult)
    act(nGBf, GBf, scale=-1.0)
    iota(ap("v3"), [[-16, 8], [-1, 18]], 0, 1)
    ts(ap("DN"), ap("v3"), -1.0, A.is_equal)
    ts(ap("v3"), ap("v3"), 0.0, A.is_equal)
    ms(ap("v3", 16, 144, 18), 0.0)
    ms(ap("v3", 17, 144, 18), 0.0)
    ms(ap("DN", 17, 144, 18), 0.0)
    tt(ap("DN"), ap("DN"), ap("v3"), A.subtract)
    act(ap("RC"), ap("v3"), scale=BG)
    act(ap("RC", 16, 144, 18), GBf, scale=-BG)
    ms(ap("CR"), 0.0)
    ms(ap("CR", 16, 144, 18), BG / 128)
    ms(ap("CR", 161, 288, 18), 0.125)
    ms(ap("DLN"), -1.0)
    ms(ap("DLN", 0, 144, 18), BG)
    ms(ap("DLN", 16, 144, 18), 15.0)
    ms(ap("DLN", 17, 144, 18), 1.0)
    ms(ap("RST"), 0.0)
    ms(ap("RST", 0, 256, 16), -2 * BG)
    act(ap("KO"), ap("RST"))
    ms(ap("we"), 0.0)
    iota(ap("thr"), [[0, 64]], 0, 0)
    for nm in ("SW", "YH", "XW"):
        ms(ap(nm, 4096, 4352), 0.0)

    W = ap("W")
    cp(ap("wf", p1=8), ap("wi", p1=8))
    mms([(P(6, 8 * h, 8 * h + 8), ap("wf", 128 * h, 128 * h + 128, p1=8), ap("If", 0, 8, p1=8), True, True) for h in range(2)])
    ts(W, P(6, 0, 16), 32.0, A.mult)
    for j in range(8):
        cp(ap("SW", j * 512, (j + 1) * 512), ap("hi", j * 512, (j + 1) * 512))
    ts(ap("vd", 0, 64), ap("vi", 0, 64), 63, A.bitwise_and)
    ts(ap("vd", 64, 128), ap("vi", 0, 64), 6, A.arith_shift_right)
    ts(ap("vb"), ap("vd"), 1.0 / 256, A.mult, -0.125, A.add)
    for j in range(2):
        s = "d%d" % ndma[0]
        ndma[0] += 1
        o, i = ap("vf", p0=8 * j, p1=8 * j + 8), ap("vb", 64 * j, 64 * j + 64)
        fn = lambda o=o, i=i, s=s: g.sync.dma_start(o[0], i[0]).then_inc(T.sem[s], 16)
        add("Y", [fn], [ap("vf", j, j + 1)], [i], 60, lat=2600, tok=(s, 16))

    def sums(j, bk):
        for u in range(2):
            mm(P(bk, 256 * u, 256 * u + 256), ap("kw"), ap("SW", 512 * j + 256 * u, 512 * j + 256 * u + 256))
        act(ap("YH", 512 * j, 512 * j + 512), P(bk, 0, 512))

    def store():
        for j in range(2):
            bk = 6 + j
            mm(P(bk, 0, 512), Ib, ap("xs", 512 * j, 512 * j + 512), True, False)
            v = ap("vf", 512 * j, 512 * j + 512, p1=16)
            mm(P(bk, 0, 512), ap("sT", p1=16), (v[0], ap("vf")[1]) + v[2:], False, True)
            affine(OPT["sg"], ap("SG", H * rank + 512 * j, H * rank + 512 * j + 512), P(bk, 0, 512), 1.0, UP)
        share("SG", 0, H, H)
        chain("lay", len(ops) - 2)
        for d in [(rank + e) % N for e in range(N)]:
            if OPT["lay"][(d - rank) % N] == "G":
                chain("lay", sel(ap("XW", d, 4096, 4), ap("SG", H * d, H * d + H), [[0, H]], A.is_ge, 0, 0))
            else:
                for u in range(2):
                    act(ap("XW", 2048 * u + d, 2048 * u + 2048, 4), ap("SG", H * d + 512 * u, H * d + 512 * u + 512))

    xv, qv = [0], [0]
    for h in range(2):
        act(ap("q0", 128 * h, 128 * h + 128), ap("x0", 128 * h, 128 * h + 128), scale=0.25, bias=191.625)

    def modulo(eng, bk, n, more, first, o, blk, q, r, out):
        qn, lo, hi = q
        w = hi - lo
        col = [ap("cm", 4 * more + j, 4 * more + j + 1) for j in range(3)]
        if eng in "IC":
            mms([(P(bk, 0, n), ap("Aw", o + 15 - m, o + 143 - m), ap(qn, lo + m, hi, 16), m == 0, m == 15) for m in range(16)])
            src = P(bk, 0, n)
            if eng == "C":
                act(ap("rw", blk, blk + n), src, bias=col[1], scale=2.0 ** -12)
                act(ap("pf", blk, blk + n), src, bias=col[2])
                mms([(src, n12, ap("rw", blk, blk + n), True, False), (src, If, ap("pf", blk, blk + n), False, True)])
                cp(out, src)
                return
        else:
            if eng == "F":
                mm(P(bk, 16, 16 + w), first, ap(qn, lo, hi))
                act(ap("rw", lo, hi), P(bk, 16, 16 + w), bias=col[1], scale=2.0 ** -12)
                mms([(P(r, 384, 384 + w), Ib, ap("NEG", 0, w), True, False), (P(r, 384, 384 + w), first, ap(qn, lo, hi), False, False)])
                mm(P(r, 384, 384 + w), n12, ap("rw", lo, hi), False, True)
                scan(ap("KA", lo, hi), ap("RST", 0, w), P(r, 384, 384 + w), A.add, A.max)
                ts(out, ap("KA", lo + 15, hi, 16), col[2], A.add)
                return
            mm(P(bk, 16, 16 + w), Ib, ap("NEG", 0, w), True, False)
            mm(P(bk, 16, 16 + w), first, ap(qn, lo, hi), False, True)
            kn = "K" if more else "KA"
            scan(ap(kn, lo, hi), ap("RST", 0, w), P(bk, 16, 16 + w), A.add, A.max)
            src = ap(kn, lo + 15, hi, 16)
        ts(ap("bj", blk, blk + n), src, col[0], A.add)
        ts(ap("bI", blk, blk + n), ap("bj", blk, blk + n), 4095, A.bitwise_and)
        cp(out, ap("bI", blk, blk + n))

    def spans(modes, m):
        out = []
        for j in range(4):
            if modes[j] == m:
                if out and out[-1][1] == 32 * j and out[-1][0] != 32 and not (out[-1][0] == 32 * (j - 1) == 96):
                    out[-1][1] += 32
                else:
                    out.append([32 * j, 32 * j + 32])
        return out

    def compare(h, modes, banks, gch, vch, byv=()):
        lo = 128 * h
        gn, mn = ("gA", "mA") if h == 0 else ("gB", "mB")
        fn = F.Abs if "V" not in modes else F.Relu
        done = -1
        for j in range(4):
            if j in byv:
                cp(ap(gn, 512 * j, 512 * j + 512), ind(ap("Gz", 16, 4112), ap("hu", lo + 32 * j, lo + 32 * j + 32)))
        for js in vch:
            j0, j1 = js[0], js[-1] + 1
            for gs in gch:
                if gs[0] < j1 + (modes[j0] == "S") + (4 if j0 in byv else 0) and gs[0] > done:
                    done = gs[0]
                    if done not in byv:
                        chain("g", act(ap(gn, 512 * gs[0], 512 * gs[-1] + 512), ind(ap("Gz", 16, 4112), ap("hu", lo + 32 * gs[0], lo + 32 * gs[-1] + 32))))
            for j in js:
                on_v = modes[j] == "V"
                mm(P(banks + j % 2, 0, 512), ap("xT", lo, lo + 128), ap("R", 512 * j, 512 * j + 512), True, on_v)
                if not on_v:
                    mm(P(banks + j % 2, 0, 512), nIb, ap(gn, 512 * j, 512 * j + 512), False, True)
            src = P(banks + j0 % 2, 0, 512 * (j1 - j0))
            if modes[j0] == "V":
                tt(ap(mn, 512 * j0, 512 * j1), ap(gn, 512 * j0, 512 * j1), src, A.max)
            else:
                i = act(ap(mn, 512 * j0, 512 * j1), src, fn, scale=-1.0)
                if OPT["schain"]:
                    chain("g", i)
        return gn, mn

    def choose(h, kb, mb, at, n, dl, ll, xo, xn, qn, s0):
        lo, hi = 128 * h, 128 * h + 128
        s1 = s0 + n
        scan(ap("us", s0, s1), dl, P(kb, 0, n), A.add, A.min)
        tt(ap("nf", s0, s1), ap("us", s0, s1), P(kb, 0, n), A.not_equal)
        scan(ap("es", s0, s1), P(mb, at, at + n), ap("nf", s0, s1), A.add, A.mult)
        tt(ap("em", lo, hi), ind(ap("es", s0, s1), ll), ap("EK", 0, 128), A.mult)
        mm(P(mb, 416, 424), ap("em", lo, hi), GBf)
        su = ap("su", 8 * h, 8 * h + 8)
        cp(su, P(mb, 416, 424))
        apart(OPT["dd"][0 if n == 136 else 1], ap(xn, lo, hi), ap("Gz"), su, xo, h, P(2 + h, 256, 384))
        affine(OPT["qv"], ap(qn, lo, hi), ap(xn, lo, hi), 0.25, 191.625)

    def apart(eng, out, win, su, xo, h, bank):
        lo, hi = 128 * h, 128 * h + 128
        if eng == "V":
            d = ap("dd", lo, hi)
            tt((T["dd"][0:128, lo:hi, 0],) + d[1:], ind(win, su), ap(xo, lo, hi), A.subtract)
            if OPT["av"]:
                add("V", [lambda: g.vector.tensor_reduce(out[0], d[0], X.X, A.max, apply_absolute_value=True)], [out], [d], vcost(out, [d], 1))
            else:
                act(out, ap("dd", lo, hi), F.Abs)
        else:
            mm(bank, nIb, ap(xo, lo, hi), True, False)
            act(ap("dd", lo, hi), ind(win, su))
            mm(bank, Ib, ap("dd", lo, hi), False, True)
            act(out, bank, F.Abs)

    def step_half(h, last, raw, xo, xn, qo, qn, s0):
        lo, hi = 128 * h, 128 * h + 128
        kb, mb = 2 + h, 4 + h
        modes = OPT["late"] if s0 == 144 else OPT["step"][2 * last + h]
        bu = ap("bu", 8 * h, 8 * h + 8)
        if s0 != 144:
            mm(P(kb, 256, 384), ap(xo, lo, hi), Ib)
            act(ap("xT", lo, hi), P(kb, 256, 384))
            modulo(OPT["mod"], mb, 8, 0, AF, 0, 8 * h, (qo, lo, hi), kb, bu)
        if raw or OPT["hu"][0] == "V":
            cp(ap("hu", lo, hi), ind(ap("hi" if raw else "SW", 0, 4096), bu))
        else:
            act(ap("hl" if last else "hf", lo, hi), ind(ap("SW", 0, 4096), bu), bias=0.0 if last else 16.0)
            ts(ap("hu", lo, hi), ap("hl" if last else "hf", lo, hi), 0.0 if last else -16.0, A.add)
        if raw:
            ts(ap("hf", lo, hi), ind(ap("hi"), bu), 16.0, A.add)
            mm(P(mb, 272, 408), ap("hf", lo, hi), ap("DM"))
        elif last:
            mms([(P(mb, 8, 16), n192, ablk, True, False), (P(mb, 8, 16), ap(qo, lo, hi), ablk, False, True)])
            act(ap("rr", 16 * h + 8, 16 * h + 16), P(mb, 8, 16), scale=2.0 ** -12, bias=FLO)
            if OPT["hu"][0] == "V":
                act(ap("hl", lo, hi), ind(ap("SW", 0, 4096), bu))
            mms([(P(mb, 272, 408), ones, ap("C16"), True, False), (P(mb, 272, 408), ap("hl", lo, hi), ap("DM"), False, True)])
        else:
            if OPT["hu"][0] == "V":
                act(ap("hf", lo, hi), ind(ap("SW", 0, 4096), bu), bias=16.0)
            mm(P(mb, 272, 408), ap("hf", lo, hi), ap("DM"))
        gn, mn = compare(h, modes, 6 * h, OPT["gch"], OPT["vch"], OPT["byv"][2 * last + h])
        mms([(P(kb, 0, 136), zeros, ap("R", 0, 136), True, False)]
            + [(P(kb, 16, 136, 17, p0, p1), ap(xo, lo + p0, lo + p1), W2, False, False) for p0, p1 in spans(modes, "V")])
        cuts = OPT["cut"]
        for p0, p1 in cuts:
            mms([(P(kb, k, 136, 17, p0, p1), ap(gn, 16 * p0 + k, 16 * p1, 16), W1n, False, False) for k in range(16)])
        for p0, p1 in cuts:
            mms([(P(kb, k, 136, 17, p0, p1), ap(mn, 16 * p0 + k, 16 * p1, 16), W2, False, k == 15 and p1 == 128) for k in range(16)])
        choose(h, kb, mb, 272, 136, ap("DLT"), l17, xo, xn, qn, s0)

    def ahead(h, xo, qo):
        lo, hi = 128 * h, 128 * h + 128
        mb = 4 + h
        modes = OPT["ahead"][h]
        mm(P(mb, 384, 512), ap(xo, lo, hi), Ib)
        affine(OPT["jv"][4 + h], ap("xT", lo, hi), P(mb, 384, 512), 1.0, 0.0)
        bu = ap("bu", 8 * h, 8 * h + 8)
        modulo(OPT["moda"], mb, 8, 0, AF, 0, 8 * h, (qo, lo, hi), mb, bu)
        act(ap("hf", lo, hi), ind(ap("SW", 0, 4096), bu))
        cp(ap("hu", lo, hi), ind(ap("SW", 0, 4096), bu) if OPT["hu"][1] == "V" else ap("hf", lo, hi))
        run = [(P(mb, 0, 288), ones, ap("CR"), True, False)]
        if "V" not in modes:
            run += [(P(mb, 17, 144, 18), ap(xo, lo, hi), W1, False, False)]
        else:
            run += [(P(mb, 17, 144, 18, p0, p1), ap(xo, lo + p0, lo + p1), W2, False, False) for p0, p1 in spans(modes, "V")]
            run += [(P(mb, 16, 144, 18, p0, p1), ap(xo, lo + p0, lo + p1), W1, False, False) for p0, p1 in spans(modes, "V")]
            run += [(P(mb, 16, 144, 18, p0, p1), ap(xo, lo + p0, lo + p1), W1n, False, False) for p0, p1 in spans(modes, "S")]
        mms(run)
        mm(P(mb, 144, 288), ap("hf", lo, hi), ap("DN"), False, False)
        gn, mn = compare(h, modes, 0, OPT["agch"], OPT["ach"])
        chain(OPT["edone"], len(ops) - 1)
        if "V" in modes:
            mms([(P(mb, k, 144, 18), ap(gn, k, 2048, 16), W1n, False, False) for k in range(16)])
        mms([(P(mb, k, 144, 18), ap(mn, k, 2048, 16), W2 if "V" in modes else W1, False, False) for k in range(16)])

    def amend(h, xo, xn, qn):
        lo, hi = 128 * h, 128 * h + 128
        mb = 4 + h
        bu = ap("bu", 8 * h, 8 * h + 8)
        ch, sn = ap("ch", lo, hi), ap("sn", lo, hi)
        mm(P(2 + h, 0, 128), Ib, ap("NEG", 0, 128), True, False)
        tt(ch, ind(ap("SW", 0, 4096), bu), ap("hf", lo, hi), A.not_equal)
        tt(sn, ind(ap("SW", 0, 4096), bu), ch, A.mult)
        mm(P(2 + h, 0, 128), ap("BF"), sn, False, True)
        scan(ap("KA", lo, hi), ap("RST", 0, 128), P(2 + h, 0, 128), A.add, A.max)
        su = ap("su", 8 * h, 8 * h + 8)
        cp(su, ap("KA", lo + 15, hi, 16))
        apart(OPT["dd"][2], ap("ja", lo, hi), ap("Gz", 16, 4112), su, xo, h, P(2 + h, 128, 256))
        mms([(P(mb, 0, 144), ch, ap("RC"), False, False), (P(mb, 16, 144, 18), ch, KC, False, False)])
        mms([(P(mb, 160, 288, 18), sn, nGBf, False, False), (P(mb, 161, 288, 18), sn, GBf, False, False)])
        mm(P(mb, 16, 144, 18), ap("ja", lo, hi), W1, False, True)
        choose(h, mb, mb, 144, 144, ap("DLN"), l18, xo, xn, qn, 144 * h)

    def words(lo, hi, e):
        w = ap("W", lo, hi)
        for j, a in enumerate(e):
            act(ap("sA", lo + j * a[2], lo + (j + 1) * a[2]), a, F.Relu, bias=-0.5, scale=1.0 / 32)
        act(ap("sB", lo, hi), ap("sA", lo, hi), bias=-5.0 * 2 ** 20, scale=1184.0 * 32)
        tt(ap("pA", lo, hi), w, ap("sA", lo, hi), A.mult)
        tt(ap("pC", lo, hi), w, ap("sB", lo, hi), A.add)
        tt(ap("pD", lo, hi), ap("pA", lo, hi), ap("pC", lo, hi), A.add)
        ts(w, ap("pD", lo, hi), 4095 * 32, A.bitwise_and)

    def limits(t):
        mms([(P(6, 0, 64), If, ap("MET", 320 * t + 80 * a + 16, 320 * t + 80 * a + 80), a == 0, a == N - 1) for a in range(N)])
        cp(ap("ci"), P(6, 0, 64))
        ts(ap("thr"), ap("ci"), 7, A.bitwise_and)

    def nextx():
        xo, qo = "x%d" % (xv[0] % 4), "q%d" % (qv[0] % 3)
        xv[0] += 1
        qv[0] += 1
        return xo, "x%d" % (xv[0] % 4), qo, "q%d" % (qv[0] % 3)

    half = [(128 * h, 128 * h + 128) for h in range(2)]
    for t in range(TR):
        fin = t == TR - 1
        for s in range(ST):
            xo, xn, qo, qn = nextx()
            early = t > 0 and s == 0
            for h in range(2):
                low[0] = "AB"[h] + str(s)
                if early:
                    low[0] = "CD"[h]
                if early and h in OPT["early"]:
                    amend(h, xo, xn, qn)
                else:
                    step_half(h, s == ST - 1, t == 0 and s < OPT["raw"], xo, xn, qo, qn, 144 * h if early else 136 * h)
                if early and h == 1:
                    low[0] = "m"
                    limits(t - 1)
                if fin and h == 1 and s < 2:
                    low[0] = "y"
                    for j in range(sum(OPT["ys"][:s]), sum(OPT["ys"][:s + 1])):
                        sums(j, (6, 7, 0, 1)[j % 4] if s == 0 else j % 2)
                if t == 0 and s == 0 and h == 0:
                    low[0] = "s"
                    store()
            low[0] = "w%d" % s
            n = 18 if early else 17
            if s == ST - 1 and OPT["splitw"] and not fin:
                for h in range(2):
                    words(8 * h, 8 * h + 8, [ap("es", 8 * n * h + n - 1, 8 * n * (h + 1), n)])
            elif early and len(OPT["early"]) < 2:
                ns = [18 if h in OPT["early"] else 17 for h in range(2)]
                words(0, 16, [ap("es", 144 * h + ns[h] - 1, 144 * h + 8 * ns[h], ns[h]) for h in range(2)])
            else:
                words(0, 16, [ap("es", n - 1, 16 * n, n)])
        ql = qo
        xo, xn, qo, qn = nextx()
        x = ap(xo)
        for h, (lo, hi) in enumerate(half):
            low[0] = "JK"[h]
            tt(ap("jm", lo, hi), ind(ap("W", 8 * h, 8 * h + 8), ap("ls", 0, 8)), ap("EK", 0, 128), A.mult)
            mm(P(4 + h, 416, 424), ap("jm", lo, hi), GBf)
            su = ap("su", 8 * h, 8 * h + 8)
            ts(su, P(4 + h, 416, 424), 1.0 / 32, A.mult)
            apart(OPT["dd"][3], ap("ja", lo, hi), ap("Gz", 16, 4112), su, xo, h, P(4 + h, 0, 128))
            affine(OPT["jv"][h], ap(xn, lo, hi), ap("ja", lo, hi), -1.0, 63.0)
            if not fin:
                affine(OPT["jv"][2 + h], ap(qn, lo, hi), ap("ja", lo, hi), -0.25, 207.375)
                low[0] = "EF"[h]
                if h in OPT["early"]:
                    ahead(h, xn, qn)
                else:
                    mm(P(4 + h, 384, 512), ap(xn, lo, hi), Ib)
                    act(ap("xT", lo, hi), P(4 + h, 384, 512))
                    modulo(OPT["moda"], 4 + h, 8, 0, AF, 0, 8 * h, (qn, lo, hi), 4 + h, ap("bu", 8 * h, 8 * h + 8))
                    chain("pre", len(ops) - 1)
        if fin:
            low[0] = "y"
            for j in range(sum(OPT["ys"][:2]), 8):
                sums(j, (0, 1, 0, 1, 4, 5, 0, 1)[j])
        low[0] = "r"
        modulo(OPT["modr"], 2, 16, 1, CF, 144, 16, (qo, 0, 256), 2, ap("fu"))
        for h, (lo, hi) in enumerate(half):
            mms([(P(6, 16 + 8 * h, 24 + 8 * h), n192, cblk, True, False), (P(6, 16 + 8 * h, 24 + 8 * h), ap(qo, lo, hi), cblk, False, True)])
        affine(OPT["rnd"], ap("rf", 16, 32), P(6, 16, 32), 2.0 ** -12, FLO)
        if OPT["xa"] == "V":
            tt(ap("xa"), ind(ap("XW", 0, 4096), ap("fu")), x, A.subtract)
            act(ap("ad"), ap("xa"), F.Abs, bias=-UP)
        else:
            mm(P(2, 256, 512), nIb, x, True, False)
            act(ap("xa"), ind(ap("XW", 0, 4096), ap("fu")))
            mm(P(2, 256, 512), If, ap("xa"), False, True)
            act(ap("ad"), P(2, 256, 512), F.Abs, bias=-UP)
        run = [(P(3, 0, 64), n200, c4, True, False)] + [(P(3, 32 * h, 32 * h + 32), ap(qo, lo, hi), ap("c4", 0, 32), False, False) for h, (lo, hi) in enumerate(half)]
        mms(run[:2] + [run[2][:4] + (True,)])
        affine(OPT["rnd"], ap("r4"), P(3, 0, 64), 1.0, 758.5)
        mms(run + [(P(3, 0, 64), nIb, ap("r4"), False, True)])
        tt(ap("oh"), P(3, 0, 64), ap("dc"), A.is_equal)
        mms([(P(6, 0, 32), LT, ap("oh", 0, 32), True, True), (P(6, 32, 64), LT, ap("oh", 32, 64), True, False),
             (P(6, 32, 64), ones, ap("oh", 0, 32), False, True)])
        ts(ap("iq"), P(6, 0, 64), 0.5 - 256 + CAP - 1, A.is_lt)
        tt(ap("th"), ap("iq"), ap("thr"), A.mult)
        ts(ap("wd", 0, 16), W, 5, A.arith_shift_right, 63, A.bitwise_and)
        ts(ap("wd", 16, 32), W, 11, A.arith_shift_right)
        we = [ap("we", j, 256, 16) for j in range(2)]
        for j in range(2):
            ts(we[j], ap("wd", 16 * j, 16 * j + 16), 1.0 / 256, A.mult, -0.125, A.add)
        cp(ap("wz", 16, 32), W)

        def payload():
            mms([(P(7, 0, 256), Ib, x, True, False)] + [(P(7, lo, hi), ap("we", lo, hi), Ib, False, h == 1) for h, (lo, hi) in enumerate(half)])
            affine(OPT["jv"][6], ap("PAY", 1024 * t + 256 * rank, 1024 * t + 256 * rank + 256), P(7, 0, 256), 1.0, UP)
            share("PAY", 1024 * t, 256, 256)

        if fin or not OPT["paylate"]:
            payload()
        if OPT["jv"][7] == "V":
            ts(ap("wz", 0, 16), W, 1.0 / 1024, A.mult)
            ts(ap("wz", 32, 48), W, 2.0, A.mult, -2.0 ** 19, A.add)
        else:
            act(ap("wz", 0, 16), ap("wz", 16, 32), scale=1.0 / 1024)
            act(ap("wz", 32, 48), ap("wz", 16, 32), scale=2.0, bias=-2.0 ** 19)
        mms([(P(6, 64, 112), If, ap("CAT"), True, False)]
            + [(P(6, 64 + 24 * h, 88 + 24 * h, 3), ap(ql, lo, hi), ablk, False, False) for h, (lo, hi) in enumerate(half)]
            + [(P(6, 64 + 24 * h, 88 + 24 * h, 3), n12, ap("rr", 16 * h + 8, 16 * h + 16), False, False) for h in range(2)]
            + [(P(6, 66 + 24 * h, 88 + 24 * h, 3), ap(qo, lo, hi), cblk, False, False) for h, (lo, hi) in enumerate(half)]
            + [(P(6, 66, 112, 3), n12, ap("rf", 16, 32), False, False)])
        mms([(P(6, 66, 112, 3), n17, cube("iq", 0, 2, 8 * d, 8 * d + 8), False, d == 3) for d in range(N)])
        affine("S" if fin else OPT["d1"], ap("D1"), P(6, 64, 112), 1.0, 0.0)
        mms([(P(7, 256, 288), zeros, ap("R", 0, 32), True, False)] + [(P(7, 256 + j, 288, 2), n8, we[j], False, False) for j in range(2)])
        mms([(P(7, 256 + 16 * h, 272 + 16 * h), ap("xa", lo, hi), S2, False, h == 1) for h, (lo, hi) in enumerate(half)])
        r1, r2 = ap("r1", 0, 32), ap("r2", 0, 32)
        ts(r1, P(7, 256, 288), MAGIC, A.add, MAGIC, A.subtract)
        ts(r2, P(7, 256, 288), 256 * MAGIC, A.add, 256 * MAGIC, A.subtract)
        tt(ap("ne"), r1, r2, A.not_equal)
        tt(ap("rd", 0, 32), r1, r2, A.subtract)
        mms([(P(3, 64, 112), ones, ap("CD"), True, False)]
            + [(P(3, 66, 112, 3), n17, cube(nm, 0, 2, 8 * d, 8 * d + 8), False, False) for nm in ("iq", "th") for d in range(N)])
        mms([(P(3, 66 + 24 * h, 88 + 24 * h, 3), ap("ad", lo, hi), G17, False, False) for h, (lo, hi) in enumerate(half)])
        mms([(P(3, 65, 112, 3), n17, ap("ne", j, 32, 2), False, j == 1) for j in range(2)])
        scan(ap("key"), P(3, 64, 112), ap("D1"), A.max, A.min)
        mm(P(3, 0, 256), Ib, ap("NEG"), True, False)
        tt(ap("EM"), ind(ap("key"), l3), ap("EK", 0, 256), A.mult)
        mms([(P(6, 8 * h, 8 * h + 8), ap("EM", lo, hi), GBf, True, True) for h, (lo, hi) in enumerate(half)])
        kO = ap("KO", 15, 256, 16)
        affine(OPT["ko"], kO, P(6, 0, 16), 1.0, 0.0)
        for u in range(OPT["ebh"]):
            w = 16 // OPT["ebh"]
            o, i = ap("EB", 16 * w * u, 16 * w * (u + 1)), ind(ap("key"), ap("ls", 48 + w * u, 48 + w * (u + 1)))
            act(o, i) if OPT["eb"][u] == "S" or fin else cp(o, i)
        for h, (lo, hi) in enumerate(half):
            mm(P(2, lo, hi), ap("EB", lo, hi), If)
        cp(ap("kR"), P(2, 0, 256))

        def counts(bk, eng):
            mms([(P(bk, 128, 192), nIb, ap("th"), True, False), (P(bk, 128, 192), nIb, ap("iq"), False, False)]
                + [(P(bk, 128 + 32 * h, 160 + 32 * h), ap("ad", lo, hi), G4, False, h == 1) for h, (lo, hi) in enumerate(half)])
            ts(ap("k4"), P(bk, 128, 192), -0.5, A.is_lt)
            mms([(P(bk, 0, 64), ones, ap("k4"), True, False), (P(bk, 0, 32), ones, ap("k4", 32, 64), False, False),
                 (P(bk, 32, 64), ones, ap("k4", 0, 32), False, True)])
            affine(eng, ap("MET", 320 * t + 80 * rank + 16, 320 * t + 80 * rank + 80), P(bk, 0, 64), 1.0, 0.0)

        if not fin and OPT["cnt"]:
            counts(2, OPT["cnt"])
        mm(P(3, 15, 256, 16), If, kO, False, False)
        mms([(P(7, 288, 320), If, ap("wz", 16, 48), True, False)]
            + [(P(7, 288 + 16 * u, 304 + 16 * u), (I5, I11)[j], ap("rd", j, 32, 2), False, u + j == 2) for u in range(2) for j in range(2)])
        tt(ap("za"), P(7, 288, 304), ap("wz", 0, 16), A.mult)
        tt(ap("zi"), P(7, 304, 320), ap("za"), A.add)
        ts(ap("zb"), ap("zi"), 5, A.arith_shift_right, 4095, A.bitwise_and)
        if OPT["zb"] == "V" and not fin:
            cp(ap("ZB"), ind(ap("zb"), lc))
        else:
            cp(ap("zf"), ap("zb"))
            act(ap("ZB"), ind(ap("zf"), lc))
        keep = "hl"
        if OPT["hk"]:
            keep = "hk"
            tt(ap("hk"), ap("hl"), ap("NK", t, t + 256), A.mult)
        for h, (lo, hi) in enumerate(half):
            if OPT["hk"]:
                mm(P(7, lo, hi), ap("ZB", lo, hi), If)
            else:
                mms([(P(7, lo, hi), nIf, ap("hl", lo, hi), True, False), (P(7, lo, hi), ap("ZB", lo, hi), If, False, True)])
        for c in range(16):
            ts(ap("E", 256 * c, 256 * c + 256 - 16 * c), ap("kR", 16 * c, 256), ap("KO", 16 * c + 15, 16 * c + 16), A.is_equal)
            if c + 1 in OPT["ecut"]:
                c0 = max([e for e in (0,) + OPT["ecut"] if e <= c])
                mms([(P(3, 16 * e + 16, 256), BDB, ap("E", 256 * e + 16, 256 * e + 256 - 16 * e), False, False) for e in range(c0, min(c + 1, 15))]
                    + [(P(3, 16 * c0, 16 * c + 16), LTB, cube("E", c0, c + 1, 0, 16), False, c == 15)])
        tt(ap("zm"), P(7, 0, 256), ap("EK", t, t + 256), A.mult)
        chain("pre", scan(ap("K"), ap("KO"), P(3, 0, 256), A.add, A.max))
        Kd = ap("K", 15, 256, 16)
        chain("oS", tt(ap("oS"), Kd, dumO, A.min))
        oU = ap("oU", 16 * t, 16 * t + 16)
        cp(oU, ap("oS"))
        if not fin:
            chain("SW", tt(ind(ap("SW"), oU), ap("zm"), ap(keep), A.add))
        low[0] = "m"
        if not fin and OPT["paylate"]:
            payload()
        mb = 320 * t + 80 * rank
        act(ap("ab"), Kd, F.Abs, bias=-CS)
        tt(ap("MET", mb, mb + 16), ap("ab"), dumO, A.min)
        if not fin and not OPT["cnt"]:
            counts(6, "S")
        share("MET", 320 * t, 80, 16 if fin else 80)
        if fin:
            mm(P(7, 0, 256), ap("kw"), ap(keep), True, False)
            mm(P(7, 0, 256), ap("kw"), ap("zm"), False, True)
            act(ap("yn"), P(7, 0, 256))
            cp(ind(ap("YH"), oU), ap("yn"))
        cp(ap("mu"), cube("MET", 4 * t, 4 * t + 4, 0, 16))
        for a in range(N - 1, -1, -1):
            w = 16 if fin else 16 // OPT["pieces"]
            for u in range(0, 16, w):
                p0 = 1024 * t + 256 * a + 16 * u
                o, i = ind(ap("XW"), ap("mu", 16 * a + u, 16 * a + u + w)), ap("PAY", p0, p0 + 16 * w)
                if fin or OPT["xw"][a] == "V":
                    cp(o, i)
                else:
                    add("S", [lambda o=o, i=i: g.scalar.activation(o[0], i[0], F.Silu)], [o], [i], 65 + 3.2 * o[2])

    low[0] = "o"
    dma("Y", T.yx[:], ap(xn), 65e3, False)
    ts(ap("sA"), W, 1.0 / 32, A.mult)
    mms([(P(0, lo, hi, p1=8), ap("sA", 8 * h, 8 * h + 8), If, True, True) for h, (lo, hi) in enumerate(half)])
    act(ap("wf", p1=8), P(0, 0, 256, p1=8))
    dma("Y", T.yw[:], ap("wf", p1=8), 8e3, False)
    dma("Y", T.yh[:], ap("YH", 0, 4096, ps=16), 131e3, False)
    for u in range(2):
        mms([(P(6 + u, 16 * e, 16 * e + 16), ap("XW", 2048 * u + 512 * e + rank, 2048 * u + 512 * e + 512, 4), S2, True, True) for e in range(4)])
    for u in range(2):
        lo, hi = 64 * u, 64 * u + 64
        ts(ap("r1", lo, hi), P(6 + u, 0, 64), MAGIC, A.add, MAGIC, A.subtract)
        ts(ap("r2", lo, hi), P(6 + u, 0, 64), 256 * MAGIC, A.add, 256 * MAGIC, A.subtract)
        tt(ap("rd", lo, hi), ap("r1", lo, hi), ap("r2", lo, hi), A.subtract)
        mms([(P(2 + u, 128 * c, 128 * c + 128, p1=8), ap("rd", 64 * u + 16 * c + j, 64 * u + 16 * c + 16, 2), (I5, I11)[j], j == 0, j == 1)
             for c in range(4) for j in range(2)])
        affine("S", ap("yv8", 512 * u, 512 * u + 512, p1=8), P(2 + u, 0, 512, p1=8), 1.0 / 32, 2080.0)
    dma("S", T.yv[:], ap("yv8", p1=8), 32e3, False)
    for j in range(4):
        lo, hi = 256 * j, 256 * j + 256
        src = ap("XW", 4 * lo + rank, 4 * hi, 4)
        if OPT["ys8"][j] == "V":
            ts(ap("xs", lo, hi), src, MAGIC, A.add, MAGIC + UP, A.subtract)
        else:
            act(ap("PAY", lo, hi), src, bias=MAGIC)
            act(ap("xs", lo, hi), ap("PAY", lo, hi), bias=-MAGIC - UP)
        if j % 2 == 1:
            dma("Y", T.ys[:, lo - 256:hi], ap("xs", lo - 256, hi), 131e3, False)
    return ops


def place(ops, pred, succ, prio):
    n = len(ops)
    left = [len(p) for p in pred]
    st = [0.0] * n
    busy = {}
    ready = sorted([(prio[i], i) for i in range(n) if left[i] == 0], reverse=True)
    while ready:
        i = ready.pop()[1]
        d = ops[i]["dur"]
        t = 0.0
        for j, lag in pred[i]:
            t = max(t, st[j] + ops[j]["dur"] + lag)
        if d > 0:
            iv = busy.setdefault(ops[i]["eng"], [])
            lo, hi = 0, len(iv)
            while lo < hi:
                mid = (lo + hi) // 2
                if iv[mid][1] <= t:
                    lo = mid + 1
                else:
                    hi = mid
            while lo < len(iv) and iv[lo][0] < t + d:
                t = max(t, iv[lo][1])
                lo += 1
            iv.insert(lo, (t, t + d))
        st[i] = t
        for k, lag in succ[i]:
            left[k] -= 1
            if left[k] == 0:
                e = (prio[k], k)
                lo, hi = 0, len(ready)
                while lo < hi:
                    mid = (lo + hi) // 2
                    if ready[mid] > e:
                        lo = mid + 1
                    else:
                        hi = mid
                ready.insert(lo, e)
    return st


def schedule(ops):
    n = len(ops)
    if n in DONE:
        return DONE[n]
    pred = [[(j, (HOP + ops[j]["lat"]) if w else 0.0) for j, w in o["deps"].items()] for o in ops]
    for i in range(n):
        far = {}
        for k, l2 in pred[i]:
            for j, l1 in pred[k]:
                far[j] = max(far.get(j, -1.0), l1 + ops[k]["dur"] + l2)
        pred[i] = [(j, lag) for j, lag in pred[i] if far.get(j, -1.0) < lag]
    succ = [[] for _ in range(n)]
    for i in range(n):
        for j, lag in pred[i]:
            succ[j].append((i, lag))
    bl = [0.0] * n
    for i in range(n - 1, -1, -1):
        bl[i] = ops[i]["dur"] + max([ops[i]["lat"]] + [bl[k] + lag for k, lag in succ[i]])

    def length(st):
        return max(st[i] + ops[i]["dur"] + ops[i]["lat"] for i in range(n))

    kinds = [(o["low"], o["low"] + o["eng"] + o["nm"][0][:2]) for o in ops]
    names = sorted({a for a, b in kinds}) * 4 + sorted({b for a, b in kinds})
    nth = [0] * n
    for i in range(1, n):
        nth[i] = nth[i - 1] + 1 if ops[i]["low"] == ops[i - 1]["low"] else 0
    twin = [ops[i]["low"] + str(nth[i]) for i in range(n)]
    rng = np.random.RandomState(SEED)
    off, end, st = {}, None, None
    for it in range(CLIMB + FINE + 1):
        o2 = dict(off)
        for _ in range(rng.randint(1, 4) if it else 0):
            k = names[rng.randint(len(names))] if it <= CLIMB or rng.rand() < 0.2 else twin[rng.randint(n)]
            o2[k] = o2.get(k, 0) + rng.randn() * (300, 1000, 4000)[rng.randint(3)]
        s2 = place(ops, pred, succ, [o2.get(kinds[i][0], 0) + o2.get(kinds[i][1], 0) + o2.get(twin[i], 0) - bl[i] for i in range(n)])
        e2 = length(s2)
        if end is None or e2 <= end + (WARM * (1.0 - it / (CLIMB + FINE)) * rng.rand() if CLIMB else 0.0):
            end, st, off = e2, s2, o2
    mark = [i for i in range(n) if ops[i]["nm"][0] == "xa"]
    first = [min(i for i in range(n) if ops[i]["low"] == "J" and i > ([0] + mark)[t]) for t in range(TR)]
    cyc = [sum(1 for f in first if f <= i) - 1 for i in range(n)]
    for it in range(LAPS):
        end, st = refine(ops, pred, succ, st, rng)
        best = st
        span = [st[mark[t + 1]] - st[mark[t]] for t in range(TR - 1)]
        for c in range(TR - 1):
            rel = {twin[i]: st[i] - st[mark[c]] for i in range(n) if cyc[i] == c}
            prio = [st[i] if cyc[i] < 0 else st[mark[0]] + cyc[i] * span[c]
                    + (rel.get(twin[i], st[i] - st[mark[cyc[i]]]) if cyc[i] < TR - 1 else st[i] - st[mark[-1]]) for i in range(n)]
            s2 = place(ops, pred, succ, prio)
            e2 = length(s2)
            if e2 < end:
                end, best = e2, s2
        st = best
    DONE[n] = (sorted(range(n), key=lambda i: (st[i], i)), end, st)
    return DONE[n]


def refine(ops, pred, succ, st, rng):
    n = len(ops)
    dur = [o["dur"] for o in ops]
    lat = [o["lat"] for o in ops]
    pm, sm, last = [-1] * n, [-1] * n, {}
    for i in sorted(range(n), key=lambda i: (st[i], i)):
        e = ops[i]["eng"]
        if e != "X":
            if e in last:
                pm[i], sm[last[e]] = last[e], i
            last[e] = i
    r, q = [0.0] * n, [0.0] * n

    def sweep():
        left = [len(pred[i]) + (pm[i] >= 0) for i in range(n)]
        topo = [i for i in range(n) if left[i] == 0]
        r[:] = [0.0] * n
        for i in topo:
            e = r[i] + dur[i]
            for k, lag in succ[i] + ([(sm[i], 0.0)] if sm[i] >= 0 else []):
                if r[k] < e + lag:
                    r[k] = e + lag
                left[k] -= 1
                if left[k] == 0:
                    topo.append(k)
        if len(topo) < n:
            return None
        for i in reversed(topo):
            t = max(lat[i], q[sm[i]] if sm[i] >= 0 else 0.0)
            for k, lag in succ[i]:
                if lag + q[k] > t:
                    t = lag + q[k]
            q[i] = t + dur[i]
        return max(q)

    def guess(seq, a, b):
        t = r[a] + dur[a] if a >= 0 else 0.0
        rr, qq, top = {}, {}, 0.0
        for i in seq:
            for j, lag in pred[i]:
                v = rr.get(j, r[j]) + dur[j] + lag
                if v > t:
                    t = v
            rr[i] = t
            t += dur[i]
        t = q[b] if b >= 0 else 0.0
        for i in reversed(seq):
            t = max(t, lat[i])
            for k, lag in succ[i]:
                v = lag + qq.get(k, q[k])
                if v > t:
                    t = v
            t += dur[i]
            qq[i] = t
            top = max(top, rr[i] + t)
        return top

    def link(seq, a, b):
        for i in seq:
            pm[i] = a
            if a >= 0:
                sm[a] = i
            a = i
        sm[a] = b
        if b >= 0:
            pm[b] = a

    end = sweep()
    best, keep = end, (pm[:], sm[:], r[:])
    barred, stale = {}, 0
    for it in range(MOVES):
        i = [k for k in range(n) if q[k] > end - 1e-6][0]
        runs, cur = [], [i]
        while i is not None:
            e = r[i] + dur[i]
            nx = [k for k, lag in succ[i] if abs(r[k] - e - lag) < 1e-6 and r[k] + q[k] > end - 1e-6]
            k = sm[i]
            if k >= 0 and abs(r[k] - e) < 1e-6 and r[k] + q[k] > end - 1e-6 and (not nx or rng.rand() < 0.5):
                cur.append(k)
                i = k
            else:
                if len(cur) > 1:
                    runs.append(cur)
                i = nx[rng.randint(len(nx))] if nx else None
                cur = [i]
        moves = []
        for b in runs:
            for x in range(len(b) - 1):
                if rng.rand() > SHARE:
                    continue
                for y in range(x + 1, min(x + 4, len(b))):
                    u, v = b[x], b[y]
                    if all(q[k] < q[v] for k, lag in succ[u]):
                        moves.append((b[x + 1:y + 1] + [u], b[x:y + 1], [(w, u) for w in b[x + 1:y + 1]]))
                    if y - x > 1 and all(r[j] + dur[j] < r[u] + dur[u] for j, lag in pred[v]):
                        moves.append(([v] + b[x:y], b[x:y + 1], [(v, w) for w in b[x:y]]))
        moves = [(guess(m[0], pm[m[1][0]], sm[m[1][-1]]),) + m for m in moves if not any(barred.get(p, -1) > it for p in m[2])]
        if not moves:
            continue
        lo = max(min(m[0] for m in moves), end - 1.0 + (SLACK if rng.rand() < 0.1 else 0.0))
        moves = [m for m in moves if m[0] <= lo + 1e-6]
        _, seq, old, pairs = moves[rng.randint(len(moves))]
        a, z = pm[old[0]], sm[old[-1]]
        link(seq, a, z)
        end = sweep()
        if end is None:
            link(old, a, z)
            end = sweep()
            pairs = [(y, x) for x, y in pairs]
        for x, y in pairs:
            barred[(y, x)] = it + 20 + rng.randint(20)
        stale += 1
        if end < best - 1e-6:
            best, keep, stale = end, (pm[:], sm[:], r[:]), 0
        elif stale > 400:
            pm[:], sm[:] = keep[0], keep[1]
            end, stale = sweep(), 0
    return best, keep[2]


DONE = {}
SEED = 1
PRUNE = 1
FINE = 1200
WARM = 0.0
LAPS = 10
CLIMB = 800
MOVES = 300
SHARE = 0.3
SLACK = 150.0


def rank_program(g, core, T, topo):
    rank = T.rank_of(core)
    if rank is None:
        return
    ops = build(g, core, T, topo, rank)
    order = schedule(ops)[0]
    queue = {"V": g.vector, "S": g.scalar, "P": g.tensor, "G": g, "Y": g.sync}
    pos = {i: k for k, i in enumerate(order)}
    need = set()
    for o in ops:
        last = {}
        for j, w in o["deps"].items():
            if w and ops[j]["tok"] is None:
                e = ops[j]["eng"]
                if e not in last or pos[j] > pos[last[e]]:
                    last[e] = j
        o["last"] = list(last.values())
        need.update(o["last"])
    count = {}
    seen, waited = {}, {}
    total = {}
    for i in order:
        o = ops[i]
        e = o["eng"]
        if e == "X":
            total[o["tok"][0]] = o["tok"][1]
            continue
        know = seen.setdefault(e, {})
        for j in sorted([j for j, w in o["deps"].items() if w and ops[j]["tok"] is not None], key=lambda j: -pos[j]):
            s, v = ops[j]["tok"]
            if know.get(s, 0) < v:
                queue[e].wait_ge(T.sem[s], v)
                waited[s] = max(waited.get(s, 0), v)
                know[s] = v
                for s2, v2 in ops[j].get("know", {}).items():
                    know[s2] = max(know.get(s2, 0), v2)
        if PRUNE:
            o["know"] = dict(know)
        for fn in o["fns"]:
            ins = fn()
        if o["tok"] is not None:
            total[o["tok"][0]] = o["tok"][1]
        elif i in need:
            s = "c" + e
            count[s] = count.get(s, 0) + 1
            ins.then_inc(T.sem[s], 1)
            o["tok"] = (s, count[s])
            total[s] = count[s]
    for s, v in total.items():
        if waited.get(s, 0) < v:
            g.wait_ge(T.sem[s], v)
